import numpy as np, ml_dtypes
CORES = [3,11,19,27,35,43,51,59]
N = 8
BF = ml_dtypes.bfloat16
W, S, RO, LIM = 4096, 192, 3, 5
HEARER = [[1, 0, 3, 2, 5, 4, 7, 6], [2, 3, 0, 1, 6, 7, 4, 5], [4, 5, 6, 7, 0, 1, 2, 3]]
def world(rng, skew):
    m = rng.integers(2, 5, (8, 1, 1)); pn = rng.integers(2, 9, (1, 8, 1)); noise = 0.05 + 0.45 * rng.random((N, 8, 1, 1))
    alph = np.argsort(rng.random((8, 16, 513)), axis=-1)[..., :4] - 256
    proto = (rng.random((8, 8, 16)) * m).astype(np.int64); z = (rng.random((N, 8, W)) * pn).astype(np.int64)
    e = proto[np.arange(8)[None, :, None], z]
    u = (rng.random(e.shape, dtype=np.float32) ** skew * m).astype(np.int64)
    e = np.where(rng.random(e.shape, dtype=np.float32) < noise, np.minimum(u, 3), e)
    return np.ascontiguousarray(alph[np.arange(8)[None, :, None, None], np.arange(16), e].transpose(0, 1, 3, 2))
def parts(rng, skew=1):
    X = world(rng, skew)
    As = np.minimum((W * rng.random((N, 8, 16, W)) ** skew).astype(np.int64), W - 1)
    C = np.minimum((W * rng.random((N, 8, 16, S)) ** skew).astype(np.int64), W - 1); H = np.minimum((W * rng.random((N, 8, 16, S)) ** skew).astype(np.int64), W - 1)
    R = np.argsort(rng.random((N, 8, 16, S)), axis=2); A = np.minimum((256 * rng.random((N, 8, S)) ** skew).astype(np.int64), 255)
    return X, As, C, H, R, A
def pack(X, As, C, H, R, A):
    return {"x": np.ascontiguousarray(X.reshape(N, 128, W)).astype(np.float32).astype(BF), "assoc": np.ascontiguousarray(As.reshape(N, 128, W)).astype(np.int32),
            "ctx": np.ascontiguousarray(C.reshape(N, 128, S)).astype(np.int32), "cand": np.ascontiguousarray(H.reshape(N, 128, S)).astype(np.int32),
            "pref": np.ascontiguousarray(R.reshape(N, 128, S)).astype(np.int32), "fail0": np.ascontiguousarray(A).astype(np.int32)}
def setup_inputs(rng):
    return pack(*parts(rng))
def setup_inputs_spread(rng):
    X, As, C, H, R, A = parts(rng, 3)
    X = np.where((X == X[0, :, :, :1]) & (rng.random((8, 16, 1)) < 0.5), 0, X)
    share = 0.05 + 0.4 * rng.random((N, 8, 1, 1))
    X = np.where(rng.random((N, 8, 1, W)) < share, rng.integers(-256, 257, X.shape), X)
    X = np.where((X == 0) & (rng.random(X.shape, dtype=np.float32) < 0.5), -0.0, X)
    return pack(X, As, C, H, R, A)
def endlist(rng, shape):
    return np.where(rng.random(shape) < 0.68, rng.choice(np.array([0, W - 1]), shape), rng.integers(0, W, shape))
def setup_inputs_ends(rng):
    proto = rng.choice(np.array([-1, 1]), (8, 6, 16)); e = proto[np.arange(8)[None, :, None], rng.integers(0, 6, (N, 8, W))]
    e = np.where(rng.random(e.shape, dtype=np.float32) < 0.05 + 0.3 * rng.random((N, 8, 1, 1)), -e, e)
    u = rng.random((N, 8, W, 1)); e = np.where(u < 0.15, 1, np.where(u < 0.3, -1, e))
    X = np.ascontiguousarray(256 * e.transpose(0, 1, 3, 2)); sg = 256 * rng.choice(np.array([-1, 1]), (8, 1)); a = np.arange(16)[:, None]
    X[..., 0] = -sg; X[..., W - 1] = sg
    X[..., W - 16:W - 1] = sg[:, :, None] * np.where(np.arange(16)[:, None] == np.arange(1, 16), -1, 1)
    X[..., 1:16] = -X[..., W - 16:W - 1]
    X[..., 16:32] = sg[:, :, None] * np.where((a >= 1) & (a <= np.arange(16)), 1, -1)
    As = endlist(rng, (N, 8, 16, W)); C = endlist(rng, (N, 8, 16, S)); H = endlist(rng, (N, 8, 16, S))
    C[..., S - 8:] = np.concatenate([np.array([W - 1]), np.arange(W - 16, W - 1)])[:, None]
    H[..., S - 3:] = 0; H[:, :, 15, S - 1] = W - 1; H[:, :, 14:, S - 3] = W - 1
    C[..., S - 4] = a[:, 0]; H[..., S - 4] = W - 1
    H[..., S - 8:S - 4] = 31 - np.arange(11, 15) - (a < rng.integers(1, 16, (N, 8, 1, 4)))
    C[..., 0] = W - 1; C[:, :, 0, 0] = 0; H[..., 0] = W - 1
    C[..., 1] = W - 1; H[..., 1] = 0
    R = np.where(rng.random((N, 8, 1, S)) < 0.5, a, 15 - a); R = np.where(rng.random((N, 8, 1, S)) < 0.25, np.argsort(rng.random((N, 8, 16, S)), axis=2), R)
    return pack(X, As, C, H, R, rng.choice(np.array([0, 255]), (N, 8, S)))
def setup_inputs_corners(rng):
    X, As, C, H, R, A = parts(rng); k = np.arange(16); kk = k[:, None]; o = np.arange(1, S, 2); M = len(o); sp = np.argsort(np.array(HEARER[0]))
    A = rng.choice(np.array([0, 1, 2, 3, 252, 253, 254, 255]), (N, 8, S))
    R = np.where(rng.random((N, 8, 1, S)) < 0.3, np.where(rng.random((N, 8, 1, S)) < 0.5, kk, 15 - kk), R)
    rk = R[..., o].transpose(0, 1, 3, 2)[:, :, :, None, :]
    kind = rng.integers(0, 4, (N, 8, M, 1, 1)); b = rng.integers(-256, 256, (N, 8, M, 1, 16))
    one = (rk == kk) | ((rk > kk) & (rng.random((N, 8, M, 16, 16)) < 0.5))
    dx = (((kind == 1) & one) | (kind == 2) | ((kind == 3) & (rk == 15) & (kk >= 8))) & (kk > 0)
    room = (LIM + (A[..., o] & 3))[..., None, None]; how = rng.integers(0, 4, (N, 8, M, 1, 1))
    m = np.where(how == 0, 0, np.where(how == 1, room, np.where(how == 2, room + 1, 16)))
    w = np.where(kind == 0, 0, rng.choice(np.array([0, 1, 14, 15]), (N, 8, M, 1, 1)))
    dy = np.where(kind == 3, rk < m, rk >= 16 - m) | (kk < w)
    cols = (16 * o[:, None] + k).reshape(-1)
    X[..., cols] = (b + dx).transpose(0, 1, 4, 2, 3).reshape(N, 8, 16, 16 * M)
    X[..., cols - 16] = (b + dy).transpose(0, 1, 4, 2, 3).reshape(N, 8, 16, 16 * M)[sp]
    C[..., o] = 16 * o + kk; H[..., o] = 16 * (o - 1) + kk
    C[:, 6, :, 0::2] = C[:, 6, :1, 0::2]; H[:, 2, :, 0::2] = H[:, 2, :1, 0::2]
    As[:, 3] = np.where(rng.random((N, 16, W)) < 0.5, np.arange(W), As[:, 3]); As[:, 5] = rng.choice(np.array([0, W - 1]), (N, 16, W))
    return pack(X, As, C, H, R, A)
def setup_inputs_bulk(rng):
    X, As, C, H, R, A = parts(rng); h = W // 2; v = h // 2; m = min(LIM, 8)
    ga, gb, gc, gd, ge = [int(i) for i in rng.permutation(8)[:5]]
    X[:, ga, :, :h] = 2 * rng.integers(-128, 129, (N, 16, h)); X[:, gb, :, :h] = 2 * rng.integers(-128, 129, (16, 1))
    for g in (ga, gb):
        X[:, g, :, h:] = 2 * rng.integers(-128, 128, (N, 16, W - h)) + 1
        C[:, g] = rng.integers(h, W, (N, 16, S)); C[:, g, 0] = rng.integers(0, h, (N, S))
    H[:, ga] = rng.integers(h, W, (N, 16, S)); H[:, gb] = rng.integers(0, h, (N, 16, S))
    X[:, gc] = (np.argsort(rng.random((16, 513)), axis=-1)[:, :N] - 256).T[:, :, None]; A[:, gc, ::2] = 255
    X[:, gd] = 2 * rng.integers(-128, 128, (16, 1))
    X[:, gd, 8:8 + m, v:h] += rng.integers(0, 2, (N, m, h - v)); X[:, gd, :8, h:] += rng.integers(0, 2, (N, 8, W - h))
    C[:, gd] = rng.integers(h, W, (N, 16, S)); C[:, gd, 0] = rng.integers(0, v, (N, S)); H[:, gd] = rng.integers(v, h, (N, 16, S))
    near = LIM + ((254 + RO) & 3); b = 2 * rng.integers(-128, 128, (16, 1))
    X[:, ge, :, :h] = b; X[:, ge, :, h:] = b + 1; X[:, ge, :, h + v:] = b + (np.argsort(rng.random(16)) < near)[:, None]; X[:, ge, :, ::16] = b
    C[:, ge] = h + 2 * rng.integers(0, v // 2, (N, 16, S)) + 1
    H[:, ge] = N * rng.integers(0, h // N, (N, 16, S)) + np.arange(N)[:, None, None]
    As[:, ge, 0, :h] = h + v * (np.arange(h) % N == np.array(HEARER[RO - 2])[:, None]) + 2 * rng.integers(0, v // 2, (N, h)) + 1
    A[:, ge, ::2] = 255
    return pack(X, As, C, H, R, A)
def check_inputs(d):
    bad = []
    for name, lo, hi in (("x", -256, 256), ("assoc", 0, W - 1), ("ctx", 0, W - 1), ("cand", 0, W - 1), ("pref", 0, 15), ("fail0", 0, 255)):
        v = np.asarray(d[name]).astype(np.float64)
        if not (np.min(v) >= lo and np.max(v) <= hi): bad.append("range of " + name)
        if np.any(v != np.rint(v)): bad.append("whole numbers in " + name)
    if np.any(np.sort(np.asarray(d["pref"]).astype(np.int64).reshape(-1, 8, 16, S), axis=2) != np.arange(16)[:, None]): bad.append("permutations in pref")
    return bad
def pick(a, ix):
    return np.take_along_axis(a, ix.reshape(N, 8, 1, 16 * S), 3).reshape(N, 8, 16, 16, S)
def front(R, row, fail):
    old = np.take_along_axis(R, row[:, :, None, :], 2)
    moved = np.where(np.arange(16)[:, None] == row[:, :, None, :], 0, R + (R < old))
    return np.where(fail[:, :, None, :], moved, R)
def reference(x, assoc, ctx, cand, pref, fail0):
    X = x.astype(np.float32).astype(np.int16).reshape(N, 8, 16, W); As = assoc.astype(np.int64).reshape(N, 8, 16, W)
    C = ctx.astype(np.int64).reshape(N, 8, 16, S); H = cand.astype(np.int64).reshape(N, 8, 16, S); R = pref.astype(np.int64).reshape(N, 8, 16, S); A = fail0.astype(np.int64).reshape(N, 8, S)
    for t in range(RO):
        q = np.array(HEARER[t]); sp = np.argsort(q)
        xk = pick(X, C); x0 = xk[:, :, :, 0]
        first = np.min(np.where(xk != x0[:, :, :, None], R[:, :, :, None], 16), axis=2)
        desc = np.any(R[:, :, :, None] == first[:, :, None], axis=3)
        top = np.min(first, axis=2)
        yk = pick(X, H)[q]
        miss = np.sum((yk != x0[:, :, :, None]) & desc[:, :, :, None], axis=2)
        ks = np.argmin(miss, axis=2)
        n = np.take_along_axis(H[q], ks[:, :, None, :], 2)[:, :, 0]
        y = np.take_along_axis(yk, ks[:, :, None, None, :], 3)[:, :, :, 0]
        un = y != x0; fail = np.sum(un, axis=2) > LIM + (A & 3); row = np.argmin(np.where(un, R, 16), axis=2)
        A = A + fail
        R = front(R, row, fail); R = front(R, row[sp], fail[sp])
        cn = np.take_along_axis(As, n[:, :, None, :], 3); hn = np.take_along_axis(As, n[sp][:, :, None, :], 3)
        C = np.where((first == top[:, :, None]) & (first < 16), cn, C); C[:, :, 0] = cn[:, :, 0]
        H = np.where(miss[sp] > 0, hn, H)
        if t < RO - 1:
            put = np.broadcast_to((16 * np.arange(S) + ks[sp])[:, :, None, :], (N, 8, 16, S))
            np.put_along_axis(X, put, np.where(desc, x0, y)[sp], 3)
    return {"yctx": C.reshape(N, 128, S).astype(np.float32), "ycand": H.reshape(N, 128, S).astype(np.float32), "ypref": R.reshape(N, 128, S).astype(np.float32), "yfail": A.astype(np.float32)}

@@ -1,0 +1,668 @@
+import math
+import numpy as np
+from concourse.mybir import AluOpType as A, ActivationFunctionType as F
+
+RO = 3
+S = 192
+WID = [128, 64]
+LO = [0, 128]
+NC = 2
+H0 = 64
+
+SCRATCH = {
+    "ps": ("psum", [128, 4096], "float32"),
+    "xs": ("sbuf", [128, 4096], "bfloat16"),
+    "az": ("sbuf", [128, 4096], "int32"),
+    "ci": ("sbuf", [128, S], "int32"), "hi": ("sbuf", [128, S], "int32"), "ri": ("sbuf", [128, S], "int32"),
+    "fi": ("sbuf", [8, S], "int32"), "fb": ("sbuf", [8, S], "bfloat16"),
+    "cf": ("sbuf", [128, S], "float32"), "cu": ("sbuf", [128, S], "uint16"),
+    "hf": ("sbuf", [128, S], "float32"), "hu": ("sbuf", [128, S], "uint16"), "hm16": ("sbuf", [128, S], "float16"),
+    "rb": ("sbuf", [128, S], "bfloat16"), "rb2": ("sbuf", [128, S], "bfloat16"), "rout": ("sbuf", [128, 2 * S], "float32"),
+    "a32": ("sbuf", [128, S], "int32"), "a3": ("sbuf", [128, S], "int32"),
+    "p1": ("sbuf", [128, S], "bfloat16"), "t1": ("sbuf", [128, S], "bfloat16"),
+    "ones": ("sbuf", [128, 128], "bfloat16"), "idn": ("sbuf", [128, 128], "bfloat16"), "bo0": ("sbuf", [128, 128], "bfloat16"),
+    "bo": ("sbuf", [128, 128], "bfloat16"), "k8a": ("sbuf", [8, 128], "bfloat16"), "k8": ("sbuf", [8, 128], "bfloat16"),
+    "mtmp": ("sbuf", [128, 896], "bfloat16"), "lw": ("sbuf", [128, 1], "float32"), "m1": ("sbuf", [128, 128], "bfloat16"), "m2": ("sbuf", [128, 128], "bfloat16"),
+    "m3": ("sbuf", [128, 128], "bfloat16"), "nb": ("sbuf", [128, 128], "bfloat16"), "ni": ("sbuf", [128, 128], "bfloat16"),
+    "ibig": ("sbuf", [128, 128], "bfloat16"), "i16": ("sbuf", [128, 128], "float16"),
+    "ek": ("sbuf", [128, 2048], "bfloat16"), "ek16": ("sbuf", [128, 2048], "float16"),
+    "pi": ("sbuf", [128, 1], "int32"), "ki": ("sbuf", [128, 1], "int32"), "kc": ("sbuf", [128, 1], "float32"),
+    "k16": ("sbuf", [128, 1], "float32"), "bk": ("sbuf", [128, 1], "float32"), "tc": ("sbuf", [128, 1], "float32"),
+    "rowq": ("sbuf", [128, 12], "float32"),
+}
+SEMAPHORES = ["sv", "ss", "sp", "sg", "lctx", "lcand", "lpref", "lfail", "lx", "las", "loc", "o0", "o1", "o2", "o3"]
+for _c in range(NC):
+    _w = WID[_c]
+    for _n, _k, _d in (("xg", 16, "bfloat16"), ("yg", 16, "bfloat16"), ("z", 16, "bfloat16"), ("yr", 16, "bfloat16"), ("nv", 1, "float32"), ("nd", 1, "bfloat16"),
+                       ("fk", 1, "bfloat16"), ("mk", 1, "float32"), ("km", 1, "float32"), ("ck", 1, "float32"), ("ct", 1, "float32"),
+                       ("wk", 1, "bfloat16"), ("ow", 1, "float16"), ("pr", 2, "float16"), ("hm", 1, "float32"), ("hd", 1, "float32"),
+                       ("ys", 1, "bfloat16"), ("un", 1, "bfloat16"), ("zf", 1, "bfloat16"), ("tt", 1, "float32"), ("de", 1, "bfloat16"),
+                       ("na", 1, "bfloat16"), ("nx", 1, "bfloat16")):
+        SCRATCH["%s%d" % (_n, _c)] = ("sbuf", [128, _k * _w], _d)
+    SCRATCH["cs%d" % _c] = ("sbuf", [128, _w // 8], "float16")
+    for _t in range(RO):
+        SCRATCH["sM%d%d" % (_t, _c)] = ("sbuf", [128, _w], "float16")
+        SCRATCH["rM%d%d" % (_t, _c)] = ("sbuf", [128, _w], "float16")
+        SCRATCH["L%d%d" % (_t, _c)] = ("sbuf", [128, _w // 8], "uint16")
+        SCRATCH["rL%d%d" % (_t, _c)] = ("sbuf", [128, _w // 16], "uint16")
+        SEMAPHORES += ["msg%d%d" % (_t, _c), "lst%d%d" % (_t, _c)]
+for _t in range(RO):
+    SCRATCH["sP%d" % _t] = ("sbuf", [128, S], "bfloat16")
+    SCRATCH["rP%d" % _t] = ("sbuf", [128, S], "bfloat16")
+    SCRATCH["sW%d" % _t] = ("sbuf", [128, 2 * S], "bfloat16")
+    SCRATCH["rW%d" % _t] = ("sbuf", [128, 2 * S], "bfloat16")
+    SEMAPHORES += ["wth%d" % _t, "phi%d" % _t]
+
+OPT = {"sq": 0, "nda": 3, "vr": 2, "cb": 0}
+QS = {"V": "sv", "S": "ss", "P": "sp", "G": "sg"}
+LNB = 0.96 * math.log(2.0)
+LNW = 5.0 * math.log(2.0)
+
+
+def tracker(g, T):
+    qq = {"V": g.vector, "S": g.scalar, "P": g.tensor, "G": g, "Y": g.sync}
+    seen = {q: {} for q in qq}
+    know = {}
+    cnt = {q: 0 for q in QS}
+    lastw, readers, bank = {}, {}, {}
+
+    def need(q, tok):
+        s, n = tok
+        if seen[q].get(s, 0) >= n:
+            return
+        qq[q].wait_ge(T.sem[s], n)
+        for k, v in list(know.get(tok, {}).items()) + [(s, n)]:
+            if seen[q].get(k, 0) < v:
+                seen[q][k] = v
+
+    def before(q, r, w, b):
+        toks = {}
+        for k in r:
+            if k in lastw:
+                s, n = lastw[k]
+                toks[s] = max(toks.get(s, 0), n)
+        for k in w:
+            for s, n in ([lastw[k]] if k in lastw else []) + readers.get(k, []):
+                toks[s] = max(toks.get(s, 0), n)
+        for k in b:
+            for q2, (s, n) in bank.get(k, {}).items():
+                if q2 != q:
+                    toks[s] = max(toks.get(s, 0), n)
+        own = QS.get(q)
+        for s in sorted(toks, key=lambda s: s == own):
+            need(q, (s, toks[s]))
+
+    def after(q, tok, r, w, b):
+        know[tok] = dict(seen[q])
+        for k in r:
+            readers.setdefault(k, []).append(tok)
+        for k in w:
+            lastw[k] = tok
+            readers[k] = []
+        for k in b:
+            bank.setdefault(k, {})[q] = tok
+
+    def op(q, call, r=(), w=(), b=()):
+        before(q, r, w, b)
+        ins = call(qq[q])
+        cnt[q] += 1
+        ins.then_inc(T.sem[QS[q]], 1)
+        after(q, (QS[q], cnt[q]), r, w, b)
+
+    def mm(seq, r, w, b):
+        before("P", r, w, b)
+        ins = None
+        for out, lhsT, rhs, start, stop in seq:
+            ins = g.tensor.matmul(out, lhsT, rhs, start, stop)
+        cnt["P"] += 1
+        ins.then_inc(T.sem["sp"], 1)
+        after("P", ("sp", cnt["P"]), r, w, b)
+
+    def dma(q, out, in_, sem, r=(), w=()):
+        before(q, r, w, ())
+        qq[q].dma_start(out, in_).then_inc(T.sem[sem], 16)
+        after(q, (sem, 16), r, w, ())
+
+    def mark(key, tok):
+        lastw[key] = tok
+
+    return {"op": op, "mm": mm, "dma": dma, "before": before, "need": need, "mark": mark, "cnt": cnt}
+
+
+def rank_program(g, core, T, topo):
+    rank = T.rank_of(core)
+    if rank is None:
+        return
+    K = tracker(g, T)
+    op, mm, dma = K["op"], K["mm"], K["dma"]
+    nloc = [0]
+
+    def V(call, r=(), w=(), b=()):
+        op("V", call, r, w, b)
+
+    def SC(call, r=(), w=(), b=()):
+        op("S", call, r, w, b)
+
+    def bank(i, lo, n, step=1):
+        return T.ps[:, 512 * i + lo:512 * i + lo + n:step]
+
+    def B(name, c):
+        return T["%s%d" % (name, c)]
+
+    def send(t, out, in_, sem, rk, wk):
+        peer = T.cores[rank ^ (1 << t)]
+        rid, pid = topo.addr(peer)[:2]
+        ne = len(topo.engines(core, peer))
+        K["before"]("G", rk, (), ())
+        g.remote_dma(out_ap=out, in_ap=in_, remote_sem=T.sem[sem], local_sem=T.sem["loc"], pid=pid, routing_id=rid,
+                     dma_engine_mask=topo.mask(core, peer))
+        nloc[0] += ne
+        for k in wk:
+            K["mark"](k, (sem, ne))
+
+    def sl(c):
+        return slice(LO[c], LO[c] + WID[c])
+
+    def qr(c, a):
+        return slice(4 * WID[c] * a, 4 * WID[c] * (a + 1))
+
+    def qj(c, a, j):
+        return slice(4 * WID[c] * a + j, 4 * WID[c] * (a + 1), 4)
+
+    dma("S", T.ci[:], T.ctx[:], "lctx", (), ["ci"])
+    dma("Y", T.xs[:], T.x[:], "lx", (), ["xs"])
+    dma("S", T.ri[:], T.pref[:], "lpref", (), ["ri"])
+    dma("S", T.hi[:], T.cand[:], "lcand", (), ["hi"])
+    dma("S", T.fi[:], T.fail0[:], "lfail", (), ["fi"])
+    dma("Y", T.az[:], T.assoc[:], "las", ["xs"], ["az"])
+    V(lambda v: v.memset(T.ones[:], 1.0), (), ["ones"])
+    op("G", lambda e: e.affine_select(T.bo0[:], T.ones[:], [[-16, 8], [0, 16]], A.is_ge, 0.0, 0, 1), ["ones"], ["bo0"])
+    op("G", lambda e: e.affine_select(T.bo[:], T.bo0[:], [[16, 8], [0, 16]], A.is_ge, 0.0, 15, -1), ["bo0"], ["bo"])
+    op("G", lambda e: e.affine_select(T.idn[:], T.ones[:], [[-1, 128]], A.is_equal, 0.0, 0, 1), ["ones"], ["idn"])
+    op("G", lambda e: e.affine_select(T.k8a[:], T.ones[0:8, :], [[1, 128]], A.is_ge, 0.0, 0, -16), ["ones"], ["k8a"])
+    op("G", lambda e: e.affine_select(T.k8[:], T.k8a[:], [[-1, 128]], A.is_ge, 0.0, 15, 16), ["k8a"], ["k8"])
+    op("G", lambda e: e.iota(T.pi[:], [[1, 1]], 0, 1), (), ["pi"])
+    op("G", lambda e: e.iota(T.rowq[:], [[256, 12]], 0, 0, allow_small_or_imprecise_dtypes=True), (), ["rowq"])
+    SC(lambda s: s.activation(T.mtmp[:, 0:128], T.idn[:], F.Copy, scale=2.0), ["idn"], ["mt0"])
+    SC(lambda s: s.activation(T.mtmp[:, 128:256], T.idn[:], F.Copy, scale=16.0), ["idn"], ["mt1"])
+    SC(lambda s: s.activation(T.mtmp[:, 256:384], T.bo[:], F.Copy, scale=0.41), ["bo"], ["mt2"])
+    SC(lambda s: s.activation(T.nb[:], T.bo[:], F.Copy, scale=-1.0), ["bo"], ["nb"])
+    SC(lambda s: s.activation(T.ni[:], T.idn[:], F.Copy, scale=-1.0), ["idn"], ["ni"])
+    SC(lambda s: s.activation(T.ibig[:], T.idn[:], F.Copy, scale=-1024.0), ["idn"], ["ibig"])
+    for i in range(4):
+        SC(lambda s: s.activation(T.mtmp[:, 384 + 128 * i:512 + 128 * i], T.idn[:], F.Copy, scale=float(2.0 ** (5 * i - 20))), ["idn"], ["iw"] if i == 3 else ["iw%d" % i])
+    V(lambda v: v.memset(T.lw[:], -5.0 * LNW), (), ["lw"])
+    V(lambda v: v.memset(T.ek[:], 0.0), (), ["ek"])
+    for k in range(16):
+        V(lambda v: v.tensor_copy(T.ek[:, 129 * k:129 * k + 113:16], T.bo[:, 0:128:16]), ["bo", "ek"], ["ek_%d" % k])
+    ekk = ["ek_%d" % k for k in range(16)]
+    V(lambda v: v.tensor_tensor(T.m1[:], T.mtmp[:, 0:128], T.bo[:], A.subtract), ["mt0", "bo"], ["m1"])
+    V(lambda v: v.tensor_scalar(T.ki[:], T.pi[:], 15, None, A.bitwise_and), ["pi"], ["ki"])
+    V(lambda v: v.tensor_copy(T.kc[:], T.ki[:]), ["ki"], ["kc"])
+    V(lambda v: v.tensor_copy(T.cu[:], T.ci[:]), ["ci"], ["cu0", "cu1"])
+
+    def orders():
+        V(lambda v: v.tensor_copy(T.rb[:], T.ri[:]), ["ri"], ["rb"])
+        SC(lambda s: s.activation(T.sW0[:, 0:S], T.rb[:], F.Exp, bias=T.lw[:], scale=-LNW), ["rb", "lw"], ["w00", "w01"])
+
+    def counts():
+        V(lambda v: v.tensor_copy(T.fb[:], T.fi[:]), ["fi"], ["fb"])
+        mm([(bank(5, 320, S), T.k8[:], T.fb[:], True, True)], ["k8", "fb"], ["A0"], [5])
+        V(lambda v: v.tensor_copy(T.hu[:], T.hi[:]), ["hi"], ["hu0", "hu1"])
+        V(lambda v: v.tensor_copy(T.a32[:], bank(5, 320, S)), ["A0"], ["a32"], [5])
+
+    def late_constants():
+        V(lambda v: v.tensor_tensor(T.m2[:], T.mtmp[:, 128:256], T.bo[:], A.subtract), ["mt1", "bo"], ["m2"])
+        V(lambda v: v.tensor_tensor(T.m3[:], T.idn[:], T.mtmp[:, 256:384], A.subtract), ["mt2", "idn"], ["m3"])
+        V(lambda v: v.tensor_copy(T.i16[:], T.idn[:]), ["idn"], ["i16"])
+        V(lambda v: v.tensor_copy(T.ek16[:], T.ek[:]), ekk, ["ek16"])
+        V(lambda v: v.tensor_scalar(T.k16[:], T.kc[:], 16.0, None, A.mult), ["kc"], ["k16"])
+        V(lambda v: v.tensor_scalar(T.bk[:], T.kc[:], -LNB, 84.5, A.mult, A.add), ["kc"], ["bk"])
+        V(lambda v: v.tensor_scalar(T.tc[:], T.kc[:], 0.0, -1e29, A.is_equal, A.mult), ["kc"], ["tc"])
+        for c in range(NC):
+            n, o = WID[c] // 16, LO[c] // 16
+            V(lambda v: v.tensor_scalar(B("cs", c)[:, 0:n], T.rowq[:, 0:n], 0.0, 2048.0, A.mult, A.add), ["rowq"], ["csa%d" % c])
+            V(lambda v: v.tensor_scalar(B("cs", c)[:, n:2 * n], T.rowq[:, o:o + n], T.k16[:], None, A.add), ["rowq", "k16"], ["csb%d" % c])
+        V(lambda v: v.tensor_copy(T.cf[:], T.ci[:]), ["ci"], ["cf0", "cf1"])
+        V(lambda v: v.tensor_copy(T.hf[:], T.hi[:]), ["hi"], ["hf0", "hf1"])
+        V(lambda v: v.tensor_scalar(T.hm16[:], T.hi[:], -2048.0, None, A.add), ["hi"], ["hm160", "hm161"])
+
+    def iw(i):
+        return T.mtmp[:, 384 + 128 * i:512 + 128 * i]
+
+    def ek(k):
+        return T.ek[:, 128 * k:128 * k + 128]
+
+    def ek16(k):
+        return T.ek16[:, 128 * k:128 * k + 128]
+
+    def pieces(c):
+        return list(range(WID[c] // H0))
+
+    def gather(q, which, c, p):
+        name, lst = (("xg", T.cu), ("yg", T.hu))[which]
+        lkey = ("cu%d", "hu%d")[which] % c
+        dst = B(name, c)[:, 16 * H0 * p:16 * H0 * (p + 1)]
+        src = T.xs[:, :].indirect(lst[:, LO[c] + H0 * p:LO[c] + H0 * (p + 1)])
+        key = "%s%d_%d" % (name, c, p)
+        if q == "V":
+            V(lambda v: v.tensor_copy(dst, src), [lkey, "xs"], [key])
+        else:
+            SC(lambda s: s.activation(dst, src, F.Copy), [lkey, "xs"], [key])
+
+    def gx(q, c, p):
+        gather(q, 0, c, p)
+
+    def gy(q, c, p):
+        gather(q, 1, c, p)
+
+    def gk(name, c):
+        return ["%s%d_%d" % (name, c, p) for p in pieces(c)]
+
+    def thr(t):
+        sw = B("sW", t)
+        V(lambda v: v.tensor_scalar(T.a3[:], T.a32[:], 3, None, A.bitwise_and), ["a32"], ["a3"])
+        V(lambda v: v.tensor_scalar(sw[:, S:2 * S], T.a3[:], 5.5, None, A.add), ["a3"], ["thr%d" % t])
+        send(t, B("rW", t)[:], sw[:], "wth%d" % t, ["w%d0" % t, "w%d1" % t, "thr%d" % t], ["rw%d" % t])
+
+    def x0dup(c):
+        mm([(bank(c, j, 4 * WID[c], 4), T.idn[:], B("xg", c)[:, 0:16 * WID[c]:16], True, True) for j in range(4)],
+           ["idn"] + gk("xg", c), ["x0d%d" % c], [c])
+
+    def wdb(c):
+        return ((2, 0), (1, 256))[c]
+
+    def wdup(t, c):
+        b, o = wdb(c)
+        if t == 0:
+            mm([(bank(b, o + j, 4 * WID[c] - j, 4), T.idn[:], T.sW0[:, sl(c)], True, True) for j in range(4)], ["idn", "w00", "w01"], ["wd%d" % c], [b])
+            return
+        seq = []
+        for j in range(4):
+            out = bank(b, o + j, 4 * WID[c] - j, 4)
+            seq += [(out, T.idn[:], B("sW", t - 1)[:, sl(c)], True, False),
+                    (out, iw(2 * t - 1), B("sP", t - 1)[:, sl(c)], False, False),
+                    (out, iw(2 * t - 2), B("rP", t - 1)[:, sl(c)], False, True)]
+        mm(seq, ["idn", "iw", "w%d%d" % (t - 1, c), "sp%d%d" % (t - 1, c), "rp%d" % (t - 1)], ["wd%d" % c], [b])
+
+    def wcopy(t, c):
+        b, o = wdb(c)
+        SC(lambda s: s.activation(B("sW", t)[:, sl(c)], bank(b, o, 4 * WID[c], 4), F.Copy), ["wd%d" % c], ["w%d%d" % (t, c)], [b])
+
+    def spk_cmp(c, a):
+        V(lambda v: v.tensor_tensor(B("z", c)[:, qr(c, a)], B("xg", c)[:, a:16 * WID[c]:4], bank(c, 0, 4 * WID[c]), A.not_equal),
+          gk("xg", c) + ["x0d%d" % c], ["z%d%d" % (c, a)], [c])
+
+    def dif_b(a):
+        w, c = WID[1], 1
+        o = 4 * w * a
+        seq = [(bank(6, o, 4 * w), T.idn[:], B("xg", c)[:, a:16 * w:4], True, False)]
+        seq += [(bank(6, o + j, 4 * w - j, 4), T.ni[:], B("xg", c)[:, 0:16 * w:16], False, j == 3) for j in range(4)]
+        mm(seq, ["idn", "ni"] + gk("xg", c), ["dif%d" % a], [6 + a // 2])
+
+    def sqr_b():
+        w = WID[1]
+        SC(lambda s: s.activation(T.z1[:, 0:16 * w], bank(6, 0, 16 * w), F.Square), ["dif%d" % a for a in range(4)], ["z1%d" % a for a in range(4)], [6, 7])
+
+    def x0one():
+        w = WID[1]
+        mm([(bank(1, 0, w), T.idn[:], T.xg1[:, 0:16 * w:16], True, True)], ["idn"] + gk("xg", 1), ["x0d1"], [1])
+
+    def spk_wt(c, a):
+        z = B("z", c)[:, qr(c, a)]
+        b, o = wdb(c)
+        V(lambda v: v.tensor_tensor(z, z, bank(b, o, 4 * WID[c]), A.min), ["wd%d" % c], ["z%d%d" % (c, a)], [b])
+
+    def spk_y(c, a):
+        bb = 3 + a % 2
+        mm([(bank(bb, 0, 4 * WID[c]), T.m1[:], B("z", c)[:, qr(c, a)], True, True)], ["m1", "z%d%d" % (c, a)], ["Y%d" % bb], [bb])
+
+    def spk_relu(c, a):
+        bb = 3 + a % 2
+        if c == 1 and a >= OPT["vr"]:
+            V(lambda v: v.tensor_scalar(B("yr", c)[:, qr(c, a)], bank(bb, 0, 4 * WID[c]), 0.0, None, A.max), ["Y%d" % bb], ["yr%d%d" % (c, a)], [bb])
+            return
+        SC(lambda s: s.activation(B("yr", c)[:, qr(c, a)], bank(bb, 0, 4 * WID[c]), F.Relu), ["Y%d" % bb], ["yr%d%d" % (c, a)], [bb])
+
+    def spk_sum(c, a):
+        seq = [(bank(5 + c, 384 * c, WID[c]), T.idn[:], B("yr", c)[:, qj(c, a, j)], a + j == 0, a + j == 6) for j in range(4)]
+        mm(seq, ["idn", "yr%d%d" % (c, a)], ["dsum%d" % c], [5 + c])
+
+    def spk_nd(t, c):
+        sm, w = T["sM%d%d" % (t, c)], WID[c]
+        V(lambda v: v.tensor_scalar(B("nv", c)[:], bank(5 + c, 384 * c, w), 0.0, 1024.0, A.is_le, A.mult), ["dsum%d" % c], ["nv%d" % c], [5 + c])
+        V(lambda v: v.tensor_tensor(sm[:], B("nv", c)[:], (bank(0, 0, 4 * w, 4), bank(1, 0, w) if OPT["sq"] else bank(1, 0, 4 * w, 4))[c], A.add), ["nv%d" % c, "x0d%d" % c], ["sm%d%d" % (t, c)], [c])
+        send(t, T["rM%d%d" % (t, c)][:], sm[:], "msg%d%d" % (t, c), ["sm%d%d" % (t, c)], ["rm%d%d" % (t, c)])
+
+    def mask_f(c, a):
+        w = WID[c]
+        seq = [(bank(5, 128 - 128 * c, w), ek(a + 4 * j), B("z", c)[:, qj(c, a, j)], a + j == 0, a + j == 6) for j in range(4)]
+        mm(seq, ekk + ["z%d%d" % (c, a)], ["F%d" % c] + ["dsum0"][:c], [5])
+
+    def mask_k(c):
+        w = WID[c]
+        SC(lambda s: s.activation(B("fk", c)[:], bank(5, 128 - 128 * c, w), F.Copy), ["F%d" % c], ["fk%d" % c], [5])
+        mm([(bank(5, 256 + 192 * c, w), T.m2[:], B("fk", c)[:], True, True)], ["m2", "fk%d" % c], ["mp%d" % c], [5])
+
+    def mask_m(c):
+        w = WID[c]
+        V(lambda v: v.tensor_scalar(B("mk", c)[:], bank(5, 256 + 192 * c, w), T.tc[:], None, A.is_gt), ["mp%d" % c, "tc"], ["mk%d" % c], [5])
+
+    def mask3(c):
+        SC(lambda s: s.activation(B("km", c)[:], B("mk", c)[:], F.Copy, bias=1.0, scale=-1.0), ["mk%d" % c], ["km%d" % c])
+        V(lambda v: v.tensor_tensor(B("ck", c)[:], T.cf[:, sl(c)], B("km", c)[:], A.mult), ["cf%d" % c, "km%d" % c], ["ck%d" % c])
+
+    def xb(c):
+        return 2 + c
+
+    def hb(c):
+        return 7 - c
+
+    def hear_in(t, c):
+        rm, w = T["rM%d%d" % (t, c)], WID[c]
+        mm([(bank(xb(c), j, 4 * w - j, 4), T.i16[:], rm[:], True, True) for j in range(4)], ["i16", "rm%d%d" % (t, c)], ["xm%d" % c], [xb(c)])
+
+    def hear_nd(t, c):
+        V(lambda v: v.tensor_scalar(B("nd", c)[:], T["rM%d%d" % (t, c)][:], 512.0, None, A.is_ge), ["rm%d%d" % (t, c)], ["nd%d" % c])
+
+    def hear_px(t, c):
+        rm, w = T["rM%d%d" % (t, c)], WID[c]
+        mm([(bank(c, 0, w), T.i16[:], rm[:], True, False), (bank(c, 0, w), T.ibig[:], B("nd", c)[:], False, True)],
+           ["i16", "ibig", "nd%d" % c, "rm%d%d" % (t, c)], ["pre%d" % c], [c])
+        if t < RO - 1:
+            SC(lambda s: s.activation(B("de", c)[:], B("nd", c)[:], F.Copy, bias=1.0, scale=-1.0), ["nd%d" % c], ["de%d" % c])
+
+    def hear_pw(t, c):
+        w = WID[c]
+        mm([(bank(c, w, w), T.idn[:], B("rW", t)[:, sl(c)], True, True)], ["idn", "rw%d" % t], ["pw%d" % c], [c])
+
+    def hear_nx(t, c):
+        w = WID[c]
+        if t < RO - 1:
+            V(lambda v: v.tensor_tensor(B("nx", c)[:], B("de", c)[:], bank(c, 0, w), A.mult), ["de%d" % c, "pre%d" % c], ["nx%d" % c], [c])
+
+    def hear_cmp(c, a):
+        V(lambda v: v.tensor_tensor(B("yr", c)[:, qr(c, a)], B("yg", c)[:, a:16 * WID[c]:4], bank(xb(c), 0, 4 * WID[c]), A.not_equal),
+          gk("yg", c) + ["xm%d" % c], ["yr%d%d" % (c, a)], [xb(c)])
+
+    def hear_cnt(t, c, a):
+        seq, w = [], WID[c]
+        if a == 1:
+            seq.append((bank(hb(c), 0, w), T.nb[:], B("nd", c)[:], False, False))
+        for j in range(4):
+            seq.append((bank(hb(c), 0, w), ek(a + 4 * j), B("yr", c)[:, qj(c, a, j)], a + j == 0, a + j == 6))
+        mm(seq, ekk + ["yr%d%d" % (c, a)] + (["nb", "nd%d" % c] if a else []), ["miss%d" % c], [hb(c)])
+
+    def hear_b(t, a):
+        hear_cmp(1, a)
+        if a == 0:
+            hear_nd(t, 1)
+        hear_cnt(t, 1, a)
+
+    def pick1(t, c):
+        h, w = hb(c), WID[c]
+        SC(lambda s: s.activation(B("wk", c)[:], bank(h, 0, w), F.Exp, bias=T.bk[:], scale=-16.0 * LNB), ["miss%d" % c, "bk"], ["wk%d" % c], [h])
+        SC(lambda s: s.activation(B("hm", c)[:], bank(h, 0, w), F.Sign), ["miss%d" % c], ["hm%d" % c], [h])
+        mm([(bank(h, 128, w), T.m3[:], B("wk", c)[:], True, True)], ["m3", "wk%d" % c], ["G%d" % c], [h])
+
+    def pick2(t, c):
+        h, w = hb(c), WID[c]
+        pr, n = B("pr", c), WID[c] // 8
+        V(lambda v: v.tensor_scalar(B("ow", c)[:], bank(h, 128, w), 0.0, None, A.is_gt), ["G%d" % c], ["ow%d" % c], [h])
+        V(lambda v: v.tensor_scalar(pr[:, w:2 * w], bank(h, 128, w), 0.0, T.kc[:], A.is_gt, A.mult), ["G%d" % c, "kc"], ["prq%d" % c], [h])
+        V(lambda v: v.tensor_tensor(pr[:, 0:w], B("ow", c)[:], T.hm16[:, sl(c)], A.mult), ["ow%d" % c, "hm16%d" % c], ["prn%d" % c])
+        seq = [(bank(h, 256, n), T.i16[:], B("cs", c)[:], True, False)]
+        for k in range(16):
+            seq.append((bank(h, 256, n), ek16(k), pr[:, k:2 * w:16], False, k == 15))
+        mm(seq, ["i16", "csa%d" % c, "csb%d" % c, "ek16", "prq%d" % c, "prn%d" % c], ["lp%d" % c], [h])
+
+    def pick3(t, c):
+        h, n = hb(c), WID[c] // 16
+        lt = T["L%d%d" % (t, c)]
+        V(lambda v: v.tensor_copy(lt[:], bank(h, 256, 2 * n)), ["lp%d" % c], ["L%d" % c], [h])
+        send(t, T["rL%d%d" % (t, c)][:], lt[:, 0:n], "lst%d%d" % (t, c), ["L%d" % c], ["rl%d%d" % (t, c)])
+
+    def post_h(t, c):
+        hf, n = T.hf[:, sl(c)], WID[c] // 16
+        lt = T["L%d%d" % (t, c)]
+        hd = B("hd", c)
+        V(lambda v: v.tensor_tensor(hd[:], T.az[:, :].indirect(lt[:, 0:n]), hf, A.subtract), ["az", "L%d" % c, "hf%d" % c], ["hd%d" % c])
+        V(lambda v: v.tensor_tensor(hd[:], hd[:], B("hm", c)[:], A.mult), ["hm%d" % c], ["hd%d" % c])
+        V(lambda v: v.tensor_tensor(hf, hf, hd[:], A.add), ["hd%d" % c], ["hf%d" % c])
+        if t < RO - 1:
+            V(lambda v: v.tensor_copy(T.hu[:, sl(c)], hf), ["hf%d" % c], ["hu%d" % c])
+            V(lambda v: v.tensor_scalar(T.hm16[:, sl(c)], hf, -2048.0, None, A.add), ["hf%d" % c], ["hm16%d" % c])
+
+    def post_y(t, c):
+        lt, n = T["L%d%d" % (t, c)], WID[c] // 16
+        SC(lambda s: s.activation(B("ys", c)[:], T.xs[:, :].indirect(lt[:, 0:n]), F.Copy), ["xs", "L%d" % c], ["ys%d" % c])
+
+    def post_na(t, c):
+        lt, n, w = T["L%d%d" % (t, c)], WID[c] // 16, WID[c]
+        V(lambda v: v.tensor_tensor(B("na", c)[:], T.xs[:, :].indirect(lt[:, 0:n]), B("nd", c)[:], A.mult),
+          ["xs", "L%d" % c, "nd%d" % c], ["na%d" % c])
+
+    def post_un(t, c):
+        w = WID[c]
+        V(lambda v: v.tensor_tensor(B("un", c)[:], B("ys", c)[:], bank(c, 0, w), A.not_equal), ["ys%d" % c, "pre%d" % c], ["un%d" % c], [c])
+        V(lambda v: v.tensor_tensor(B("zf", c)[:], B("un", c)[:], bank(c, w, w), A.mult), ["un%d" % c, "pw%d" % c], ["zf%d" % c], [c])
+        u = 4 - c
+        mm([(bank(u, 0, w), T.bo[:], B("un", c)[:], True, True), (bank(u, 128, w), T.m1[:], B("zf", c)[:], True, True)],
+           ["bo", "m1", "un%d" % c, "zf%d" % c], ["UY%d" % c], [u])
+
+    def post_phi(t, c):
+        w, u = WID[c], 4 - c
+        V(lambda v: v.tensor_tensor(B("tt", c)[:], bank(u, 0, w), B("rW", t)[:, S + LO[c]:S + LO[c] + w], A.is_le), ["UY%d" % c, "rw%d" % t], ["tt%d" % c], [u])
+        V(lambda v: v.tensor_tensor(B("sP", t)[:, sl(c)], bank(u, 128, w), B("tt", c)[:], A.is_gt), ["UY%d" % c, "tt%d" % c], ["sp%d%d" % (t, c)], [u])
+
+    def send_phi(t):
+        send(t, B("rP", t)[:], B("sP", t)[:], "phi%d" % t, ["sp%d%d" % (t, c) for c in range(NC)], ["rp%d" % t])
+
+    def scatter(t, c):
+        lt, n = T["L%d%d" % (t, c)], WID[c] // 16
+        V(lambda v: v.tensor_tensor(T.xs[:, :].indirect(lt[:, n:2 * n]), B("na", c)[:], B("nx", c)[:], A.add),
+          ["L%d" % c, "na%d" % c, "nx%d" % c], ["xs"])
+
+    def cupd(t, c):
+        V(lambda v: v.tensor_tensor(B("ct", c)[:], T.az[:, :].indirect(T["rL%d%d" % (t, c)][:]), B("mk", c)[:], A.mult),
+          ["az", "rl%d%d" % (t, c), "mk%d" % c], ["ct%d" % c])
+        V(lambda v: v.tensor_tensor(T.cf[:, sl(c)], B("ct", c)[:], B("ck", c)[:], A.add), ["ct%d" % c, "ck%d" % c], ["cf%d" % c])
+        if t < RO - 1:
+            V(lambda v: v.tensor_copy(T.cu[:, sl(c)], T.cf[:, sl(c)]), ["cf%d" % c], ["cu%d" % c])
+
+    def move1(phi, pk, rb, rk, pb, m):
+        V(lambda v: v.tensor_tensor(pb[:], phi[:], rb[:], A.mult), [rk] + pk, [pb.name])
+        mm([(bank(m, 0, S), T.bo[:], pb[:], True, True)], ["bo", pb.name], ["rf"], [m])
+        mm([(bank(m + 1, 0, S), T.idn[:], rb[:], True, False), (bank(m + 1, 0, S), T.ni[:], pb[:], False, False)],
+           ["idn", "ni", rk, pb.name], ["RR"], [m + 1])
+
+    def move2(rb, rk, tb, m):
+        V(lambda v: v.tensor_tensor(tb[:], bank(m, 0, S), rb[:], A.is_gt), ["rf", rk], [tb.name], [m])
+        mm([(bank(m + 1, 0, S), T.idn[:], tb[:], False, True)], ["idn", tb.name], ["RR"], [m + 1])
+
+    def rup1(t):
+        move1(B("rP", t), ["rp%d" % t], T.rb, "rb", T.p1, 0)
+        mm([(bank(0, 192, S), T.bo[:], B("rP", t)[:], True, True)], ["bo", "rp%d" % t], ["Fo"], [0])
+
+    def rup2(t):
+        move2(T.rb, "rb", T.t1, 0)
+
+    def rup3(t):
+        V(lambda v: v.tensor_copy(T.rb2[:], bank(1, 0, S)), ["RR"], ["rb2"], [1])
+        move1(B("sP", t), ["sp%d%d" % (t, c) for c in range(NC)], T.rb2, "rb2", T.p1, 2)
+
+    def rup4(t):
+        move2(T.rb2, "rb2", T.t1, 2)
+
+    def last_orders1():
+        sp = B("sP", RO - 1)
+        sk = ["sp%d%d" % (RO - 1, c) for c in range(NC)]
+        V(lambda v: v.tensor_tensor(T.p1[:], sp[:], T.rb[:], A.mult), ["rb"] + sk, ["p1"])
+        mm([(bank(2, 0, S), T.bo[:], T.p1[:], True, True)], ["bo", "p1"], ["rf"], [2])
+        V(lambda v: v.tensor_tensor(T.t1[:], bank(2, 0, S), T.rb[:], A.is_gt), ["rf", "rb"], ["t1"], [2])
+        m = [(T.idn[:], T.rb[:]), (T.ni[:], T.p1[:]), (T.idn[:], T.t1[:])]
+        seq = []
+        for out, terms in ((bank(7, 0, S), m + [(T.mtmp[:, 128:256], sp[:])]), (bank(6, 0, S), m),
+                           (bank(6, 192, S), m + [(T.nb[:], sp[:]), (T.idn[:], sp[:])])):
+            seq += [(out, l, r, i == 0, i == len(terms) - 1) for i, (l, r) in enumerate(terms)]
+        mm(seq, ["idn", "ni", "nb", "mt1", "rb", "p1", "t1"] + sk, ["MK"], [6, 7])
+        SC(lambda s: s.activation(T.rb2[:], bank(7, 0, S), F.Copy), ["MK"], ["rb2"], [7])
+
+    def last_orders2():
+        rp = B("rP", RO - 1)
+        rk = ["rp%d" % (RO - 1)]
+        V(lambda v: v.tensor_tensor(T.p1[:], rp[:], bank(6, 0, S), A.mult), ["MK"] + rk, ["p1"], [6])
+        mm([(bank(5, 0, S), T.bo[:], T.p1[:], True, True)], ["bo", "p1"], ["m1f"], [5])
+        V(lambda v: v.tensor_tensor(T.t1[:], rp[:], bank(6, 192, S), A.mult), ["MK"] + rk, ["t1"], [6])
+        V(lambda v: v.tensor_tensor(bank(0, 0, S), bank(6, 0, S), T.t1[:], A.subtract), ["MK", "t1"], ["dd"], [6, 0])
+        V(lambda v: v.tensor_tensor(T.p1[:], bank(5, 0, S), T.rb2[:], A.is_gt), ["m1f", "rb2"], ["p1"], [5])
+        V(lambda v: v.tensor_tensor(T.rout[:, 0:S], T.p1[:], bank(0, 0, S), A.add), ["p1", "dd"], ["rout"], [0])
+        dma("Y", T.ypref[:], T.rout[:, 0:S], "o2", ["rout"], [])
+        mm([(bank(4, 192, S), T.bo[:], rp[:], True, True)], ["bo"] + rk, ["Fo"], [4])
+        V(lambda v: v.tensor_tensor(T.rout[:, S:2 * S], bank(4, 192, S), T.a32[:], A.add), ["Fo", "a32"], ["aout"], [4])
+        dma("S", T.yfail[:], T.rout[0:128:16, S:2 * S], "o3", ["aout"], [])
+
+    def rup5(t):
+        SC(lambda s: s.activation(T.rb[:], bank(3, 0, S), F.Copy), ["RR"], ["rb"], [3])
+
+    def aup(t):
+        V(lambda v: v.tensor_tensor(T.a32[:], bank(0, 192, S), T.a32[:], A.add), ["Fo"], ["a32"], [0])
+
+    cb = OPT["cb"]
+    if OPT["sq"]:
+        cb = 0
+    for t in range(RO):
+        if t == 0:
+            gx("S", 0, 0)
+            gx("V", 0, 1)
+            x0dup(0)
+            orders()
+            gx("S", 1, 0)
+            wdup(t, 0)
+            for a in range(4):
+                spk_cmp(0, a)
+            x0dup(1)
+            wdup(t, 1)
+            counts()
+            thr(t)
+        else:
+            x0dup(0)
+            cupd(t - 1, 1)
+            gx("S", 1, 0)
+            for a in range(4):
+                spk_cmp(0, a)
+            wdup(t, 0)
+            wcopy(t, 0)
+            x0dup(1)
+            wdup(t, 1)
+            for a in range(cb):
+                spk_cmp(1, a)
+        for a in range(4):
+            spk_wt(0, a)
+            spk_y(0, a)
+            spk_relu(0, a)
+            if a > 0:
+                spk_sum(0, a - 1)
+        for a in range(4):
+            if t == 0 or a >= cb:
+                spk_cmp(1, a)
+            spk_wt(1, a)
+            spk_y(1, a)
+            if a < OPT["vr"]:
+                spk_relu(1, a)
+            if a == 0:
+                spk_sum(0, 3)
+            elif a <= OPT["vr"]:
+                spk_sum(1, a - 1)
+            if a == OPT["nda"]:
+                spk_nd(t, 0)
+        for a in range(OPT["vr"], 4):
+            spk_relu(1, a)
+            spk_sum(1, a)
+        if OPT["vr"] == 4:
+            spk_sum(1, 3)
+        spk_nd(t, 1)
+        if t == 0:
+            late_constants()
+        else:
+            wcopy(t, 1)
+            rup1(t - 1)
+        for a in range(4):
+            mask_f(0, a)
+        gy("V", 0, 0)
+        gy("S", 0, 1)
+        if t > 0:
+            rup2(t - 1)
+            aup(t - 1)
+            thr(t)
+            post_h(t - 1, 1)
+        for a in range(4):
+            mask_f(1, a)
+        gy("S", 1, 0)
+        hear_in(t, 0)
+        for a in range(4):
+            hear_cmp(0, a)
+            if a == 0:
+                hear_nd(t, 0)
+            hear_cnt(t, 0, a)
+            if a == 1:
+                hear_in(t, 1)
+        mask_k(0)
+        pick1(t, 0)
+        hear_b(t, 0)
+        hear_b(t, 1)
+        pick2(t, 0)
+        mask_m(0)
+        hear_b(t, 2)
+        hear_b(t, 3)
+        pick1(t, 1)
+        if t > 0:
+            rup3(t - 1)
+        mask_k(1)
+        hear_px(t, 0)
+        pick3(t, 0)
+        post_y(t, 0)
+        hear_nx(t, 0)
+        if t < RO - 1:
+            post_na(t, 0)
+        mask3(0)
+        pick2(t, 1)
+        if t > 0:
+            rup4(t - 1)
+        post_h(t, 0)
+        hear_px(t, 1)
+        hear_pw(t, 0)
+        hear_pw(t, 1)
+        pick3(t, 1)
+        post_y(t, 1)
+        if t > 0:
+            rup5(t - 1)
+        if t < RO - 1:
+            post_na(t, 1)
+        post_un(t, 0)
+        post_un(t, 1)
+        post_phi(t, 0)
+        post_phi(t, 1)
+        send_phi(t)
+        hear_nx(t, 1)
+        if t < RO - 1:
+            scatter(t, 0)
+            scatter(t, 1)
+        mask_m(1)
+        cupd(t, 0)
+        mask3(1)
+        if t < RO - 1:
+            gx("V", 0, 0)
+            gx("S", 0, 1)
+        else:
+            post_h(t, 1)
+            dma("Y", T.ycand[:], T.hf[:], "o1", ["hf0", "hf1"], [])
+            last_orders1()
+    cupd(RO - 1, 1)
+    dma("Y", T.yctx[:], T.cf[:], "o0", ["cf0", "cf1"], [])
+    last_orders2()
+    for s in ("o0", "o1", "o2", "o3"):
+        g.sync.wait_ge(T.sem[s], 16)
+    for q in ("V", "S", "P", "G"):
+        K["need"]("G", (QS[q], K["cnt"][q]))
+    g.wait_ge(T.sem["loc"], nloc[0])

@@ -6,57 +6,116 @@ RO = 3
 S = 192
 WID = [128, 64]
 LO = [0, 128]
-NC = 2
-H0 = 64
+NC = len(WID)
+BIGW = 16 * S
+OPT = {"passes": 4, "xg": [[0, 1], [0], [0]], "yg": [[0], [0], [0]], "piece": 32, "cyc": 0.95, "pe": 0.55, "hop": 110, "flight": 1900, "look": 200, "spare": 400, "fix": 40, "gat": 1.56}
 
-SCRATCH = {
-    "ps": ("psum", [128, 4096], "float32"),
-    "xs": ("sbuf", [128, 4096], "bfloat16"),
-    "az": ("sbuf", [128, 4096], "int32"),
-    "ci": ("sbuf", [128, S], "int32"), "hi": ("sbuf", [128, S], "int32"), "ri": ("sbuf", [128, S], "int32"),
-    "fi": ("sbuf", [8, S], "int32"), "fb": ("sbuf", [8, S], "bfloat16"),
-    "cf": ("sbuf", [128, S], "float32"), "cu": ("sbuf", [128, S], "uint16"),
-    "hf": ("sbuf", [128, S], "float32"), "hu": ("sbuf", [128, S], "uint16"), "hm16": ("sbuf", [128, S], "float16"),
-    "rb": ("sbuf", [128, S], "bfloat16"), "rb2": ("sbuf", [128, S], "bfloat16"), "rout": ("sbuf", [128, 2 * S], "float32"),
-    "a32": ("sbuf", [128, S], "int32"), "a3": ("sbuf", [128, S], "int32"),
-    "p1": ("sbuf", [128, S], "bfloat16"), "t1": ("sbuf", [128, S], "bfloat16"),
-    "ones": ("sbuf", [128, 128], "bfloat16"), "idn": ("sbuf", [128, 128], "bfloat16"), "bo0": ("sbuf", [128, 128], "bfloat16"),
-    "bo": ("sbuf", [128, 128], "bfloat16"), "k8a": ("sbuf", [8, 128], "bfloat16"), "k8": ("sbuf", [8, 128], "bfloat16"),
-    "mtmp": ("sbuf", [128, 896], "bfloat16"), "lw": ("sbuf", [128, 1], "float32"), "m1": ("sbuf", [128, 128], "bfloat16"), "m2": ("sbuf", [128, 128], "bfloat16"),
-    "m3": ("sbuf", [128, 128], "bfloat16"), "nb": ("sbuf", [128, 128], "bfloat16"), "ni": ("sbuf", [128, 128], "bfloat16"),
-    "ibig": ("sbuf", [128, 128], "bfloat16"), "i16": ("sbuf", [128, 128], "float16"),
-    "ek": ("sbuf", [128, 2048], "bfloat16"), "ek16": ("sbuf", [128, 2048], "float16"),
-    "pi": ("sbuf", [128, 1], "int32"), "ki": ("sbuf", [128, 1], "int32"), "kc": ("sbuf", [128, 1], "float32"),
-    "k16": ("sbuf", [128, 1], "float32"), "bk": ("sbuf", [128, 1], "float32"), "tc": ("sbuf", [128, 1], "float32"),
-    "rowq": ("sbuf", [128, 12], "float32"),
-}
-SEMAPHORES = ["sv", "ss", "sp", "sg", "lctx", "lcand", "lpref", "lfail", "lx", "las", "loc", "o0", "o1", "o2", "o3"]
-for _c in range(NC):
-    _w = WID[_c]
-    for _n, _k, _d in (("xg", 16, "bfloat16"), ("yg", 16, "bfloat16"), ("z", 16, "bfloat16"), ("yr", 16, "bfloat16"), ("nv", 1, "float32"), ("nd", 1, "bfloat16"),
-                       ("fk", 1, "bfloat16"), ("mk", 1, "float32"), ("km", 1, "float32"), ("ck", 1, "float32"), ("ct", 1, "float32"),
-                       ("wk", 1, "bfloat16"), ("ow", 1, "float16"), ("pr", 2, "float16"), ("hm", 1, "float32"), ("hd", 1, "float32"),
-                       ("ys", 1, "bfloat16"), ("un", 1, "bfloat16"), ("zf", 1, "bfloat16"), ("tt", 1, "float32"), ("de", 1, "bfloat16"),
-                       ("na", 1, "bfloat16"), ("nx", 1, "bfloat16")):
-        SCRATCH["%s%d" % (_n, _c)] = ("sbuf", [128, _k * _w], _d)
-    SCRATCH["cs%d" % _c] = ("sbuf", [128, _w // 8], "float16")
-    for _t in range(RO):
-        SCRATCH["sM%d%d" % (_t, _c)] = ("sbuf", [128, _w], "float16")
-        SCRATCH["rM%d%d" % (_t, _c)] = ("sbuf", [128, _w], "float16")
-        SCRATCH["L%d%d" % (_t, _c)] = ("sbuf", [128, _w // 8], "uint16")
-        SCRATCH["rL%d%d" % (_t, _c)] = ("sbuf", [128, _w // 16], "uint16")
-        SEMAPHORES += ["msg%d%d" % (_t, _c), "lst%d%d" % (_t, _c)]
+SCRATCH = {"ps": ("psum", [128, 4096], "float32"), "xs": ("sbuf", [128, 4096], "bfloat16"), "az": ("sbuf", [128, 4096], "int32"),
+           "fi": ("sbuf", [8, S], "int32"), "f3": ("sbuf", [8, S], "int32"), "fb": ("sbuf", [8, S], "bfloat16"), "fo": ("sbuf", [8, S], "float32"),
+           "k8a": ("sbuf", [8, 128], "bfloat16"), "k8": ("sbuf", [8, 128], "bfloat16")}
+for _d, _l in (("int32", (("ci", S), ("hi", S), ("ri", S), ("pi", 1), ("ki", 1))),
+               ("uint16", (("cu", S), ("hu", S), ("ls", 16 * RO * NC), ("rl", 8 * RO * NC))),
+               ("float16", (("c16", S), ("h16", S), ("tc", S), ("th", S), ("pr", 2 * S), ("i16", 128), ("e16", 144), ("cs", 16))),
+               ("float32", (("cf", S), ("hf", S), ("rf", S), ("kc", 1), ("k16", 1), ("bk", 1), ("cm", 1), ("lw", 1), ("rq", 8))),
+               ("bfloat16", (("xg", BIGW), ("yg", 2 * BIGW), ("z", BIGW), ("yr", BIGW), ("nq", BIGW), ("ekm", 2048), ("e1", 144), ("es", 144),
+                             ("sa", 2 * S * RO), ("ra", 2 * S * RO), ("sn", 2 * S * RO), ("rn", 2 * S * RO), ("sp", S * RO), ("rp", S * RO),
+                             ("ones", S), ("bo0", 128), ("bo", 128), ("idn", 128), ("m1", 128), ("m1s", 128), ("m3", 128), ("nb", 128), ("nb0", 128),
+                             ("cmd", 128), ("sc", 128 * 14),
+                             ("wk", S), ("bh", S), ("bc", S), ("na", S), ("nx", S), ("un", S), ("zf", S), ("nf", S), ("q", S),
+                             ("rb", S), ("rb1", S), ("p1", S), ("t1", S)))):
+    for _n, _w in _l:
+        SCRATCH[_n] = ("sbuf", [128, _w], _d)
+SEMAPHORES = ["sv", "ss", "st", "sg", "lctx", "lcand", "lpref", "lfail", "lx", "las", "loc", "o0", "o1", "o2", "o3"]
 for _t in range(RO):
-    SCRATCH["sP%d" % _t] = ("sbuf", [128, S], "bfloat16")
-    SCRATCH["rP%d" % _t] = ("sbuf", [128, S], "bfloat16")
-    SCRATCH["sW%d" % _t] = ("sbuf", [128, 2 * S], "bfloat16")
-    SCRATCH["rW%d" % _t] = ("sbuf", [128, 2 * S], "bfloat16")
-    SEMAPHORES += ["wth%d" % _t, "phi%d" % _t]
+    SEMAPHORES += ["wax%d" % _t] + ["%s%d%d" % (_n, _t, _c) for _n in ("nd", "lst", "phi") for _c in range(NC)]
 
-OPT = {"sq": 0, "nda": 3, "vr": 2, "cb": 0}
-QS = {"V": "sv", "S": "ss", "P": "sp", "G": "sg"}
+QS = {"V": "sv", "S": "ss", "P": "st", "G": "sg"}
 LNB = 0.96 * math.log(2.0)
-LNW = 5.0 * math.log(2.0)
+LN2 = math.log(2.0)
+SCALED = [("i2", "idn", 2.0), ("neg", "idn", -1.0), ("i1024", "idn", 1024.0), ("i2048", "idn", 2048.0), ("nhalf", "idn", -0.5), ("n32", "idn", -32.0),
+          ("n16", "idn", -16.0), ("i32", "idn", 32.0), ("i60", "idn", 2.0 ** 60)] + [("lv%d" % _i, "i60", 2.0 ** (35 + 5 * _i)) for _i in range(4)] + [("b41", "bo", 0.41)]
+
+
+def banks(pieces):
+    return sorted({b for n, lo, hi in pieces if n == "ps" for b in range(lo // 512, (hi - 1) // 512 + 1)})
+
+
+def meet(table, pieces):
+    return [x for n, lo, hi in pieces for l, h, x in table.get(n, []) if l < hi and lo < h]
+
+
+def note(wrote, read, r, w, x):
+    for n, lo, hi in w:
+        wrote[n] = [y for y in wrote.get(n, []) if not (lo <= y[0] and y[1] <= hi)] + [(lo, hi, x)]
+        read[n] = [y for y in read.get(n, []) if not (lo <= y[0] and y[1] <= hi)]
+    for n, lo, hi in r:
+        read.setdefault(n, []).append((lo, hi, x))
+
+
+def plan(calls):
+    hop, n = OPT["hop"], len(calls)
+    wrote, read, group, loose = {}, {}, {}, {}
+    pre, post = [], [[] for _ in calls]
+    for i, c in enumerate(calls):
+        p = set(meet(wrote, c["r"]) + meet(wrote, c["w"]) + meet(read, c["w"]))
+        note(wrote, read, c["r"], c["w"], i)
+        for b in c["starts"]:
+            p.update(group.get(b, []))
+            if c["open"][b]:
+                p.update(loose.pop(b, []))
+            loose.setdefault(b, []).append(i)
+        for b in c["open"]:
+            if c["open"][b] or b not in c["starts"]:
+                group[b] = [i]
+        p.discard(i)
+        pre.append(sorted(p))
+        for j in pre[i]:
+            post[j].append(i)
+        c["banks"] = banks(c["r"] + c["w"])
+
+    def lay(rank, before, after, back, fixed):
+        busy, held, at, left = {}, {}, {}, [len(p) for p in before]
+        ready = [i for i in range(n) if not left[i]]
+        while ready:
+            i = min(ready, key=lambda j: (rank[j], j))
+            ready.remove(i)
+            c, best = calls[i], None
+            s0 = max([at[j][1] + (hop if calls[j]["first"] != "P" or c["first"] != "P" else 0.0) + calls[i if back else j]["lat"] for j in before[i]],
+                     default=c["lat"] if back else 0.0)
+            for q in ([fixed[i]] if fixed else c["on"]):
+                d, s = c["on"][q][0], s0
+                taken = sorted(busy.get(q, []) + [(a - hop, b + hop) for k in c["banks"] for a, b, q2 in held.get(k, []) if q2 != q])
+                for a, b in taken:
+                    if b > s and a < s + d:
+                        s = b
+                key = s + d + (OPT["spare"] if q != c["first"] else 0.0)
+                if best is None or key < best[0]:
+                    best = (key, s, s + d, q)
+            at[i] = best[1:]
+            busy.setdefault(best[3], []).append(best[1:3])
+            for k in c["banks"]:
+                held.setdefault(k, []).append(best[1:])
+            for j in after[i]:
+                left[j] -= 1
+                if not left[j]:
+                    ready.append(j)
+        return at
+
+    way = [0.0] * n
+    for i in range(n - 1, -1, -1):
+        way[i] = min(x[0] for x in calls[i]["on"].values()) + calls[i]["lat"] + max([hop + way[j] for j in post[i]], default=0.0)
+    pin = {i: i - 1e9 for i, c in enumerate(calls) if c["sem"] and c["w"]}
+    rank, best = [pin.get(i, -x) for i, x in enumerate(way)], None
+    for _ in range(OPT["passes"]):
+        at = lay(rank, pre, post, False, None)
+        end = max(at[i][1] + calls[i]["lat"] for i in range(n))
+        if best is None or end < best[0]:
+            best = (end, at)
+        bk = lay([-(at[i][1] + calls[i]["lat"]) for i in range(n)], post, pre, True, [at[i][2] for i in range(n)])
+        rank = [pin.get(i, -bk[i][1]) for i in range(n)]
+    at = best[1]
+    OPT["end"] = best[0]
+    return [(i, at[i][2]) for i in sorted(range(n), key=lambda i: (at[i][0], i))]
 
 
 def tracker(g, T):
@@ -64,7 +123,7 @@ def tracker(g, T):
     seen = {q: {} for q in qq}
     know = {}
     cnt = {q: 0 for q in QS}
-    lastw, readers, bank = {}, {}, {}
+    wrote, read, bank = {}, {}, {}
 
     def need(q, tok):
         s, n = tok
@@ -75,594 +134,376 @@ def tracker(g, T):
             if seen[q].get(k, 0) < v:
                 seen[q][k] = v
 
-    def before(q, r, w, b):
-        toks = {}
-        for k in r:
-            if k in lastw:
-                s, n = lastw[k]
-                toks[s] = max(toks.get(s, 0), n)
-        for k in w:
-            for s, n in ([lastw[k]] if k in lastw else []) + readers.get(k, []):
-                toks[s] = max(toks.get(s, 0), n)
-        for k in b:
-            for q2, (s, n) in bank.get(k, {}).items():
-                if q2 != q:
-                    toks[s] = max(toks.get(s, 0), n)
-        own = QS.get(q)
-        for s in sorted(toks, key=lambda s: s == own):
-            need(q, (s, toks[s]))
-
-    def after(q, tok, r, w, b):
+    def issue(q, c):
+        r, w = c["r"], ([] if c["lands"] else c["w"])
+        toks = meet(wrote, r) + meet(read, w) + meet(wrote, [x for x in w if x not in c["goes_on"]])
+        toks += [tok for b in c["banks"] for q2, tok in bank.get(b, {}).items() if q2 != q]
+        top = {}
+        for s, n in toks:
+            top[s] = max(top.get(s, 0), n)
+        for s in sorted(top, key=lambda s: s == QS.get(q)):
+            need(q, (s, top[s]))
+        ins = c["on"][q][1](qq[q])
+        if c["lands"]:
+            return
+        if c["sem"]:
+            tok = (c["sem"], 16)
+            ins.then_inc(T.sem[c["sem"]], 16)
+        else:
+            cnt[q] += 1
+            tok = (QS[q], cnt[q])
+            ins.then_inc(T.sem[QS[q]], 1)
         know[tok] = dict(seen[q])
-        for k in r:
-            readers.setdefault(k, []).append(tok)
-        for k in w:
-            lastw[k] = tok
-            readers[k] = []
-        for k in b:
-            bank.setdefault(k, {})[q] = tok
+        note(wrote, read, r, w, tok)
+        for b in c["banks"]:
+            bank.setdefault(b, {})[q] = tok
 
-    def op(q, call, r=(), w=(), b=()):
-        before(q, r, w, b)
-        ins = call(qq[q])
-        cnt[q] += 1
-        ins.then_inc(T.sem[QS[q]], 1)
-        after(q, (QS[q], cnt[q]), r, w, b)
+    def lands(pieces, tok):
+        note(wrote, read, [], pieces, tok)
 
-    def mm(seq, r, w, b):
-        before("P", r, w, b)
-        ins = None
-        for out, lhsT, rhs, start, stop in seq:
-            ins = g.tensor.matmul(out, lhsT, rhs, start, stop)
-        cnt["P"] += 1
-        ins.then_inc(T.sem["sp"], 1)
-        after("P", ("sp", cnt["P"]), r, w, b)
-
-    def dma(q, out, in_, sem, r=(), w=()):
-        before(q, r, w, ())
-        qq[q].dma_start(out, in_).then_inc(T.sem[sem], 16)
-        after(q, (sem, 16), r, w, ())
-
-    def mark(key, tok):
-        lastw[key] = tok
-
-    return {"op": op, "mm": mm, "dma": dma, "before": before, "need": need, "mark": mark, "cnt": cnt}
+    return issue, lands, need, cnt
 
 
 def rank_program(g, core, T, topo):
     rank = T.rank_of(core)
     if rank is None:
         return
-    K = tracker(g, T)
-    op, mm, dma = K["op"], K["mm"], K["dma"]
+    issue, lands, need, cnt = tracker(g, T)
+    calls = []
     nloc = [0]
 
-    def V(call, r=(), w=(), b=()):
-        op("V", call, r, w, b)
+    def v(name, lo=0, n=None, step=1, rows=128):
+        n = T[name].shape[1] - lo if n is None else n
+        return {"ap": T[name][0:min(rows, T[name].shape[0]), lo:lo + n:step], "at": [(name, lo, lo + n)], "n": (n + step - 1) // step, "by": [],
+                "two": SCRATCH[name][2] in ("bfloat16", "float16", "uint16"), "ps": name == "ps"}
 
-    def SC(call, r=(), w=(), b=()):
-        op("S", call, r, w, b)
+    def ps(b, lo, n, step=1, rows=128):
+        return v("ps", 512 * b + lo, n, step, rows)
 
-    def bank(i, lo, n, step=1):
-        return T.ps[:, 512 * i + lo:512 * i + lo + n:step]
+    def ch(name, c, base=0):
+        return v(name, base + LO[c], WID[c])
 
-    def B(name, c):
-        return T["%s%d" % (name, c)]
+    def by(win, lst):
+        return dict(win, ap=win["ap"].indirect(lst["ap"]), n=16 * lst["n"], by=lst["at"])
 
-    def send(t, out, in_, sem, rk, wk):
+    def ap(x):
+        return x["ap"] if isinstance(x, dict) else x
+
+    def call(on, out, ins, lat=0.0, sem=None, landing=False, starts=(), open_=(), goes_on=()):
+        ins = [i for i in ins if isinstance(i, dict)]
+        calls.append({"on": on, "first": list(on)[0], "w": [x for o in out for x in o["at"]], "lat": lat, "sem": sem, "lands": landing,
+                      "r": [x for i in ins for x in i["at"] + i["by"]] + [x for o in out for x in o["by"]],
+                      "starts": starts, "open": dict(open_), "goes_on": goes_on})
+
+    def ns(out, a, per):
+        if out["by"]:
+            per = 3.8
+        elif a["by"]:
+            per = OPT["gat"]
+        return OPT["fix"] + max(64, per * a["n"]) * OPT["cyc"]
+
+    def half(out, a):
+        return 0.5 if out["two"] and a["two"] else 1.0
+
+    def tt(out, a, b, o):
+        call({"V": (ns(out, a, 1 if a["ps"] or b["ps"] else 2), lambda e: e.tensor_tensor(out["ap"], a["ap"], b["ap"], o))}, [out], [a, b])
+
+    def ts(out, a, s1, s2, *o):
+        call({"V": (ns(out, a, half(out, a)), lambda e: e.tensor_scalar(out["ap"], a["ap"], ap(s1), ap(s2), *o))}, [out], [a, s1, s2])
+
+    def cp(out, a):
+        call({"V": (ns(out, a, half(out, a)), lambda e: e.tensor_copy(out["ap"], a["ap"]))}, [out], [a])
+
+    def fill(out, x):
+        call({"V": (ns(out, out, half(out, out)), lambda e: e.memset(out["ap"], x))}, [out], [])
+
+    def act(out, a, f, bias=0.0, scale=1.0, more=0.0):
+        call({"S": (more + ns(out, a, 1), lambda e: e.activation(out["ap"], a["ap"], f, bias=ap(bias), scale=ap(scale)))}, [out], [a, bias, scale])
+
+    def either(out, a, relu=False, on="S"):
+        how = {"S": (ns(out, a, 1), lambda e: e.activation(out["ap"], a["ap"], F.Relu if relu else F.Copy)),
+               "V": (ns(out, a, 1), lambda e: e.tensor_scalar(out["ap"], a["ap"], 0.0, None, A.max) if relu else e.tensor_copy(out["ap"], a["ap"]))}
+        call({q: how[q] for q in on}, [out], [a])
+
+    def sel(out, a, *rest):
+        call({"G": (170 + 2 * OPT["cyc"] * out["n"], lambda e: e.affine_select(out["ap"], a["ap"], *rest))}, [out], [a])
+
+    def iota(out, pattern, mult, **kw):
+        call({"G": (150.0, lambda e: e.iota(out["ap"], pattern, 0, mult, **kw))}, [out], [])
+
+    def mm(seq):
+        def run(e):
+            return [e.matmul(o["ap"], l["ap"], r["ap"], start, stop) for o, l, r, start, stop in seq][-1]
+        started = [x for s in seq if s[3] for x in s[0]["at"]]
+        call({"P": (sum(max(64, s[2]["n"]) for s in seq) * OPT["pe"], run)}, [s[0] for s in seq], [x for s in seq for x in s[1:3]], starts=banks(started),
+             open_=[(b, not s[4]) for s in seq for b in banks(s[0]["at"])], goes_on=[x for s in seq for x in s[0]["at"] if x not in started])
+
+    def acc(out, terms, start=True, stop=True):
+        return [(out, l, r, start and i == 0, stop and i == len(terms) - 1) for i, (l, r) in enumerate(terms)]
+
+    def load(q, name, src, sem, lat, after=()):
+        call({q: (60.0, lambda e: e.dma_start(T[name][:], src[:]))}, [v(name)], list(after), lat, sem)
+
+    def store(q, dst, name, sem):
+        call({q: (60.0, lambda e: e.dma_start(dst[:], T[name][:]))}, [], [v(name)], 2000.0, sem)
+
+    def send(t, out, in_, sem):
         peer = T.cores[rank ^ (1 << t)]
         rid, pid = topo.addr(peer)[:2]
         ne = len(topo.engines(core, peer))
-        K["before"]("G", rk, (), ())
-        g.remote_dma(out_ap=out, in_ap=in_, remote_sem=T.sem[sem], local_sem=T.sem["loc"], pid=pid, routing_id=rid,
-                     dma_engine_mask=topo.mask(core, peer))
+        lands(out["at"], (sem, ne))
         nloc[0] += ne
-        for k in wk:
-            K["mark"](k, (sem, ne))
+        call({"G": (300.0, lambda e: e.remote_dma(out_ap=out["ap"], in_ap=in_["ap"], remote_sem=T.sem[sem], local_sem=T.sem["loc"], pid=pid, routing_id=rid,
+                                                   dma_engine_mask=topo.mask(core, peer)))}, [out], [in_], OPT["flight"] - 300.0, landing=True)
 
-    def sl(c):
-        return slice(LO[c], LO[c] + WID[c])
+    M = {n: v("sc", 128 * i, 128) for i, (n, _, _) in enumerate(SCALED)}
+    for n in ("idn", "bo", "m1", "m1s", "m3", "nb", "nb0", "cmd", "i16"):
+        M[n] = v(n)
 
-    def qr(c, a):
-        return slice(4 * WID[c] * a, 4 * WID[c] * (a + 1))
+    def ek(name, k):
+        return v(name, 15 - k, 128)
 
-    def qj(c, a, j):
-        return slice(4 * WID[c] * a + j, 4 * WID[c] * (a + 1), 4)
+    def ones(c):
+        return v("ones", 0, WID[c])
 
-    dma("S", T.ci[:], T.ctx[:], "lctx", (), ["ci"])
-    dma("Y", T.xs[:], T.x[:], "lx", (), ["xs"])
-    dma("S", T.ri[:], T.pref[:], "lpref", (), ["ri"])
-    dma("S", T.hi[:], T.cand[:], "lcand", (), ["hi"])
-    dma("S", T.fi[:], T.fail0[:], "lfail", (), ["fi"])
-    dma("Y", T.az[:], T.assoc[:], "las", ["xs"], ["az"])
-    V(lambda v: v.memset(T.ones[:], 1.0), (), ["ones"])
-    op("G", lambda e: e.affine_select(T.bo0[:], T.ones[:], [[-16, 8], [0, 16]], A.is_ge, 0.0, 0, 1), ["ones"], ["bo0"])
-    op("G", lambda e: e.affine_select(T.bo[:], T.bo0[:], [[16, 8], [0, 16]], A.is_ge, 0.0, 15, -1), ["bo0"], ["bo"])
-    op("G", lambda e: e.affine_select(T.idn[:], T.ones[:], [[-1, 128]], A.is_equal, 0.0, 0, 1), ["ones"], ["idn"])
-    op("G", lambda e: e.affine_select(T.k8a[:], T.ones[0:8, :], [[1, 128]], A.is_ge, 0.0, 0, -16), ["ones"], ["k8a"])
-    op("G", lambda e: e.affine_select(T.k8[:], T.k8a[:], [[-1, 128]], A.is_ge, 0.0, 15, 16), ["k8a"], ["k8"])
-    op("G", lambda e: e.iota(T.pi[:], [[1, 1]], 0, 1), (), ["pi"])
-    op("G", lambda e: e.iota(T.rowq[:], [[256, 12]], 0, 0, allow_small_or_imprecise_dtypes=True), (), ["rowq"])
-    SC(lambda s: s.activation(T.mtmp[:, 0:128], T.idn[:], F.Copy, scale=2.0), ["idn"], ["mt0"])
-    SC(lambda s: s.activation(T.mtmp[:, 128:256], T.idn[:], F.Copy, scale=16.0), ["idn"], ["mt1"])
-    SC(lambda s: s.activation(T.mtmp[:, 256:384], T.bo[:], F.Copy, scale=0.41), ["bo"], ["mt2"])
-    SC(lambda s: s.activation(T.nb[:], T.bo[:], F.Copy, scale=-1.0), ["bo"], ["nb"])
-    SC(lambda s: s.activation(T.ni[:], T.idn[:], F.Copy, scale=-1.0), ["idn"], ["ni"])
-    SC(lambda s: s.activation(T.ibig[:], T.idn[:], F.Copy, scale=-1024.0), ["idn"], ["ibig"])
-    for i in range(4):
-        SC(lambda s: s.activation(T.mtmp[:, 384 + 128 * i:512 + 128 * i], T.idn[:], F.Copy, scale=float(2.0 ** (5 * i - 20))), ["idn"], ["iw"] if i == 3 else ["iw%d" % i])
-    V(lambda v: v.memset(T.lw[:], -5.0 * LNW), (), ["lw"])
-    V(lambda v: v.memset(T.ek[:], 0.0), (), ["ek"])
-    for k in range(16):
-        V(lambda v: v.tensor_copy(T.ek[:, 129 * k:129 * k + 113:16], T.bo[:, 0:128:16]), ["bo", "ek"], ["ek_%d" % k])
-    ekk = ["ek_%d" % k for k in range(16)]
-    V(lambda v: v.tensor_tensor(T.m1[:], T.mtmp[:, 0:128], T.bo[:], A.subtract), ["mt0", "bo"], ["m1"])
-    V(lambda v: v.tensor_scalar(T.ki[:], T.pi[:], 15, None, A.bitwise_and), ["pi"], ["ki"])
-    V(lambda v: v.tensor_copy(T.kc[:], T.ki[:]), ["ki"], ["kc"])
-    V(lambda v: v.tensor_copy(T.cu[:], T.ci[:]), ["ci"], ["cu0", "cu1"])
+    load("Y", "ci", T.ctx, "lctx", 2000.0)
+    load("S", "ri", T.pref, "lpref", 2500.0)
+    load("Y", "xs", T.x, "lx", 5900.0)
+    load("Y", "hi", T.cand, "lcand", 6400.0)
+    load("Y", "fi", T.fail0, "lfail", 6500.0)
+    load("Y", "az", T.assoc, "las", 8000.0, [v("xs")])
 
-    def orders():
-        V(lambda v: v.tensor_copy(T.rb[:], T.ri[:]), ["ri"], ["rb"])
-        SC(lambda s: s.activation(T.sW0[:, 0:S], T.rb[:], F.Exp, bias=T.lw[:], scale=-LNW), ["rb", "lw"], ["w00", "w01"])
+    fill(v("ones"), 1.0)
+    fill(v("e1"), 0.0)
+    fill(v("lw"), 90.0 * LN2)
+    o128 = v("ones", 0, 128)
+    sel(v("idn"), o128, [[-1, 128]], A.is_equal, 0.0, 0, 1)
+    sel(v("bo0"), o128, [[-16, 8], [0, 16]], A.is_ge, 0.0, 0, 1)
+    sel(v("bo"), v("bo0"), [[16, 8], [0, 16]], A.is_ge, 0.0, 15, -1)
+    iota(v("pi"), [[1, 1]], 1)
+    iota(v("rq"), [[256, 8]], 0, allow_small_or_imprecise_dtypes=True)
+    sel(v("k8a"), v("ones", 0, 128, rows=8), [[1, 128]], A.is_ge, 0.0, 0, -16)
+    sel(v("k8"), v("k8a"), [[-1, 128]], A.is_ge, 0.0, 15, 16)
+    for n, src, f in SCALED:
+        ts(M[n], M[src], float(f), None, A.mult)
+    cp(v("i16"), M["idn"])
+    cp(v("e1", 15, 113, 16), v("bo", 0, 113, 16))
+    tt(M["m1"], M["i2"], M["bo"], A.subtract)
+    ts(M["nb"], M["bo"], -1.0, None, A.mult)
+    ts(v("es"), v("e1"), 16.0, None, A.mult)
+    cp(M["nb0"], M["nb"])
+    fill(v("nb0", 0, 113, 16), 0.0)
+    cp(v("rb"), v("ri"))
+    cp(v("cu"), v("ci"))
+    act(v("sa", 0, S), v("rb"), F.Exp, v("lw"), -5.0 * LN2, 1300.0)
+    for b in range(4):
+        mm([x for k in range(4 * b, 4 * b + 4) for x in acc(ps(4 + b, 128 * (k % 4), 128), [(M["idn"], ek("es", k)), (M["idn"], M["nb0"])])])
+        either(v("ekm", 512 * b, 512), ps(4 + b, 0, 512))
+    ts(v("ki"), v("pi"), 15, None, A.bitwise_and)
+    cp(v("kc"), v("ki"))
+    cp(v("e16"), v("e1"))
+    tt(M["m3"], M["idn"], M["b41"], A.subtract)
+    ts(M["m1s"], M["m1"], 2.0 ** -60, None, A.mult)
+    ts(v("k16"), v("kc"), 16.0, None, A.mult)
+    ts(v("bk"), v("kc"), -LNB, 84.5 - 8.0 * LNB, A.mult, A.add)
+    ts(v("cm"), v("kc"), 0.0, 8192.0, A.is_equal, A.mult)
+    ts(v("cm"), v("cm"), -4096.0, None, A.add)
+    ts(M["cmd"], M["idn"], v("cm"), None, A.mult)
+    fill(v("cs", 0, 8), 2048.0)
+    ts(v("cs", 8, 8), v("rq"), v("k16"), None, A.add)
+    ts(v("c16"), v("ci"), -2048.0, None, A.add)
+    cp(v("hu"), v("hi"))
+    ts(v("f3"), v("fi"), 3, None, A.bitwise_and)
+    cp(v("fb"), v("f3"))
+    ts(v("h16"), v("hi"), -2048.0, None, A.add)
 
-    def counts():
-        V(lambda v: v.tensor_copy(T.fb[:], T.fi[:]), ["fi"], ["fb"])
-        mm([(bank(5, 320, S), T.k8[:], T.fb[:], True, True)], ["k8", "fb"], ["A0"], [5])
-        V(lambda v: v.tensor_copy(T.hu[:], T.hi[:]), ["hi"], ["hu0", "hu1"])
-        V(lambda v: v.tensor_copy(T.a32[:], bank(5, 320, S)), ["A0"], ["a32"], [5])
+    def W(name, t, c):
+        return ch(name, c, 2 * S * t)
 
-    def late_constants():
-        V(lambda v: v.tensor_tensor(T.m2[:], T.mtmp[:, 128:256], T.bo[:], A.subtract), ["mt1", "bo"], ["m2"])
-        V(lambda v: v.tensor_tensor(T.m3[:], T.idn[:], T.mtmp[:, 256:384], A.subtract), ["mt2", "idn"], ["m3"])
-        V(lambda v: v.tensor_copy(T.i16[:], T.idn[:]), ["idn"], ["i16"])
-        V(lambda v: v.tensor_copy(T.ek16[:], T.ek[:]), ekk, ["ek16"])
-        V(lambda v: v.tensor_scalar(T.k16[:], T.kc[:], 16.0, None, A.mult), ["kc"], ["k16"])
-        V(lambda v: v.tensor_scalar(T.bk[:], T.kc[:], -LNB, 84.5, A.mult, A.add), ["kc"], ["bk"])
-        V(lambda v: v.tensor_scalar(T.tc[:], T.kc[:], 0.0, -1e29, A.is_equal, A.mult), ["kc"], ["tc"])
-        for c in range(NC):
-            n, o = WID[c] // 16, LO[c] // 16
-            V(lambda v: v.tensor_scalar(B("cs", c)[:, 0:n], T.rowq[:, 0:n], 0.0, 2048.0, A.mult, A.add), ["rowq"], ["csa%d" % c])
-            V(lambda v: v.tensor_scalar(B("cs", c)[:, n:2 * n], T.rowq[:, o:o + n], T.k16[:], None, A.add), ["rowq", "k16"], ["csb%d" % c])
-        V(lambda v: v.tensor_copy(T.cf[:], T.ci[:]), ["ci"], ["cf0", "cf1"])
-        V(lambda v: v.tensor_copy(T.hf[:], T.hi[:]), ["hi"], ["hf0", "hf1"])
-        V(lambda v: v.tensor_scalar(T.hm16[:], T.hi[:], -2048.0, None, A.add), ["hi"], ["hm160", "hm161"])
+    def cnt_a(name, t, c=None):
+        return v(name, 2 * S * t + S, S) if c is None else ch(name, c, 2 * S * t + S)
 
-    def iw(i):
-        return T.mtmp[:, 384 + 128 * i:512 + 128 * i]
+    def X0(name, t, c=None):
+        return v(name, 2 * S * t, S) if c is None else ch(name, c, 2 * S * t)
 
-    def ek(k):
-        return T.ek[:, 128 * k:128 * k + 128]
+    def ND(name, t, c):
+        return ch(name, c, 2 * S * t + S)
 
-    def ek16(k):
-        return T.ek16[:, 128 * k:128 * k + 128]
+    def big(name, c, first=0, step=1, base=0):
+        return v(name, base + 16 * LO[c] + first, 16 * WID[c] - first, step)
 
-    def pieces(c):
-        return list(range(WID[c] // H0))
+    def quarter(name, c, a, j=0, step=1):
+        return v(name, 16 * LO[c] + 4 * WID[c] * a + j, 4 * WID[c] - j, step)
 
-    def gather(q, which, c, p):
-        name, lst = (("xg", T.cu), ("yg", T.hu))[which]
-        lkey = ("cu%d", "hu%d")[which] % c
-        dst = B(name, c)[:, 16 * H0 * p:16 * H0 * (p + 1)]
-        src = T.xs[:, :].indirect(lst[:, LO[c] + H0 * p:LO[c] + H0 * (p + 1)])
-        key = "%s%d_%d" % (name, c, p)
-        if q == "V":
-            V(lambda v: v.tensor_copy(dst, src), [lkey, "xs"], [key])
-        else:
-            SC(lambda s: s.activation(dst, src, F.Copy), [lkey, "xs"], [key])
+    def dup(b, c, terms):
+        return [x for j in range(4) for x in acc(ps(b, j, 4 * WID[c] - j, 4), terms)]
 
-    def gx(q, c, p):
-        gather(q, 0, c, p)
+    def gather(t, name, lst, c, base=0):
+        n = OPT["piece"]
+        for lo in range(LO[c], LO[c] + WID[c], n):
+            either(v(name, base + 16 * lo, 16 * n), by(v("xs"), v(lst, lo, n)), on="V" if lo // n in OPT[name][t] else "S")
 
-    def gy(q, c, p):
-        gather(q, 1, c, p)
+    def weights(t, c):
+        out = ps(5, S + LO[c], WID[c])
+        mm(acc(out, [(M["idn"], W("sa", t - 1, c)), (M["lv%d" % (2 * t - 1)], ch("sp", c, S * (t - 1))), (M["lv%d" % (2 * t - 2)], ch("rp", c, S * (t - 1)))]))
+        either(W("sa", t, c), out)
 
-    def gk(name, c):
-        return ["%s%d_%d" % (name, c, p) for p in pieces(c)]
+    def counts(t):
+        out = ps(4, S, S)
+        mm(acc(out, [(v("k8"), v("fb"))] + [(M["bo"], v("rp", S * s, S)) for s in range(t)]))
+        either(cnt_a("sa", t), out)
 
-    def thr(t):
-        sw = B("sW", t)
-        V(lambda v: v.tensor_scalar(T.a3[:], T.a32[:], 3, None, A.bitwise_and), ["a32"], ["a3"])
-        V(lambda v: v.tensor_scalar(sw[:, S:2 * S], T.a3[:], 5.5, None, A.add), ["a3"], ["thr%d" % t])
-        send(t, B("rW", t)[:], sw[:], "wth%d" % t, ["w%d0" % t, "w%d1" % t, "thr%d" % t], ["rw%d" % t])
+    def wax(t):
+        send(t, v("ra", 2 * S * t, 2 * S), v("sa", 2 * S * t, 2 * S), "wax%d" % t)
 
-    def x0dup(c):
-        mm([(bank(c, j, 4 * WID[c], 4), T.idn[:], B("xg", c)[:, 0:16 * WID[c]:16], True, True) for j in range(4)],
-           ["idn"] + gk("xg", c), ["x0d%d" % c], [c])
-
-    def wdb(c):
-        return ((2, 0), (1, 256))[c]
-
-    def wdup(t, c):
-        b, o = wdb(c)
-        if t == 0:
-            mm([(bank(b, o + j, 4 * WID[c] - j, 4), T.idn[:], T.sW0[:, sl(c)], True, True) for j in range(4)], ["idn", "w00", "w01"], ["wd%d" % c], [b])
-            return
-        seq = []
-        for j in range(4):
-            out = bank(b, o + j, 4 * WID[c] - j, 4)
-            seq += [(out, T.idn[:], B("sW", t - 1)[:, sl(c)], True, False),
-                    (out, iw(2 * t - 1), B("sP", t - 1)[:, sl(c)], False, False),
-                    (out, iw(2 * t - 2), B("rP", t - 1)[:, sl(c)], False, True)]
-        mm(seq, ["idn", "iw", "w%d%d" % (t - 1, c), "sp%d%d" % (t - 1, c), "rp%d" % (t - 1)], ["wd%d" % c], [b])
-
-    def wcopy(t, c):
-        b, o = wdb(c)
-        SC(lambda s: s.activation(B("sW", t)[:, sl(c)], bank(b, o, 4 * WID[c], 4), F.Copy), ["wd%d" % c], ["w%d%d" % (t, c)], [b])
-
-    def spk_cmp(c, a):
-        V(lambda v: v.tensor_tensor(B("z", c)[:, qr(c, a)], B("xg", c)[:, a:16 * WID[c]:4], bank(c, 0, 4 * WID[c]), A.not_equal),
-          gk("xg", c) + ["x0d%d" % c], ["z%d%d" % (c, a)], [c])
-
-    def dif_b(a):
-        w, c = WID[1], 1
-        o = 4 * w * a
-        seq = [(bank(6, o, 4 * w), T.idn[:], B("xg", c)[:, a:16 * w:4], True, False)]
-        seq += [(bank(6, o + j, 4 * w - j, 4), T.ni[:], B("xg", c)[:, 0:16 * w:16], False, j == 3) for j in range(4)]
-        mm(seq, ["idn", "ni"] + gk("xg", c), ["dif%d" % a], [6 + a // 2])
-
-    def sqr_b():
-        w = WID[1]
-        SC(lambda s: s.activation(T.z1[:, 0:16 * w], bank(6, 0, 16 * w), F.Square), ["dif%d" % a for a in range(4)], ["z1%d" % a for a in range(4)], [6, 7])
-
-    def x0one():
-        w = WID[1]
-        mm([(bank(1, 0, w), T.idn[:], T.xg1[:, 0:16 * w:16], True, True)], ["idn"] + gk("xg", 1), ["x0d1"], [1])
-
-    def spk_wt(c, a):
-        z = B("z", c)[:, qr(c, a)]
-        b, o = wdb(c)
-        V(lambda v: v.tensor_tensor(z, z, bank(b, o, 4 * WID[c]), A.min), ["wd%d" % c], ["z%d%d" % (c, a)], [b])
-
-    def spk_y(c, a):
-        bb = 3 + a % 2
-        mm([(bank(bb, 0, 4 * WID[c]), T.m1[:], B("z", c)[:, qr(c, a)], True, True)], ["m1", "z%d%d" % (c, a)], ["Y%d" % bb], [bb])
-
-    def spk_relu(c, a):
-        bb = 3 + a % 2
-        if c == 1 and a >= OPT["vr"]:
-            V(lambda v: v.tensor_scalar(B("yr", c)[:, qr(c, a)], bank(bb, 0, 4 * WID[c]), 0.0, None, A.max), ["Y%d" % bb], ["yr%d%d" % (c, a)], [bb])
-            return
-        SC(lambda s: s.activation(B("yr", c)[:, qr(c, a)], bank(bb, 0, 4 * WID[c]), F.Relu), ["Y%d" % bb], ["yr%d%d" % (c, a)], [bb])
-
-    def spk_sum(c, a):
-        seq = [(bank(5 + c, 384 * c, WID[c]), T.idn[:], B("yr", c)[:, qj(c, a, j)], a + j == 0, a + j == 6) for j in range(4)]
-        mm(seq, ["idn", "yr%d%d" % (c, a)], ["dsum%d" % c], [5 + c])
-
-    def spk_nd(t, c):
-        sm, w = T["sM%d%d" % (t, c)], WID[c]
-        V(lambda v: v.tensor_scalar(B("nv", c)[:], bank(5 + c, 384 * c, w), 0.0, 1024.0, A.is_le, A.mult), ["dsum%d" % c], ["nv%d" % c], [5 + c])
-        V(lambda v: v.tensor_tensor(sm[:], B("nv", c)[:], (bank(0, 0, 4 * w, 4), bank(1, 0, w) if OPT["sq"] else bank(1, 0, 4 * w, 4))[c], A.add), ["nv%d" % c, "x0d%d" % c], ["sm%d%d" % (t, c)], [c])
-        send(t, T["rM%d%d" % (t, c)][:], sm[:], "msg%d%d" % (t, c), ["sm%d%d" % (t, c)], ["rm%d%d" % (t, c)])
-
-    def mask_f(c, a):
+    def describe(t, c):
         w = WID[c]
-        seq = [(bank(5, 128 - 128 * c, w), ek(a + 4 * j), B("z", c)[:, qj(c, a, j)], a + j == 0, a + j == 6) for j in range(4)]
-        mm(seq, ekk + ["z%d%d" % (c, a)], ["F%d" % c] + ["dsum0"][:c], [5])
+        mm(dup(0, c, [(M["idn"], big("xg", c, 0, 16))]))
+        mm(dup(1, c, [(M["idn"], W("sa", t, c))]))
+        for a in range(4):
+            tt(quarter("z", c, a), big("xg", c, a, 4), ps(0, 0, 4 * w), A.not_equal)
+        for a in range(4):
+            tt(quarter("z", c, a), quarter("z", c, a), ps(1, 0, 4 * w), A.mult)
+            mm([(ps(2 + a % 2, 0, 4 * w), M["m1"], quarter("z", c, a), True, True)])
+            either(quarter("yr", c, a), ps(2 + a % 2, 0, 4 * w), True)
+            mm(acc(ps(4, LO[c], w), [(M["idn"], quarter("yr", c, a, j, 4)) for j in range(1 if a == 0 else 0, 4)], a == 0, a == 3))
+        act(ND("sn", t, c), ps(4, LO[c], w), F.Relu, 1.0, -1.0)
+        lo, n = (2 * S * t, S + w) if c == 0 else (2 * S * t + S + LO[c], w)
+        send(t, v("rn", lo, n), v("sn", lo, n), "nd%d%d" % (t, c))
 
-    def mask_k(c):
+    def tops(c):
+        for a in range(4):
+            terms = [(M["cmd"], ones(c))] if a == 0 else []
+            terms += [(v("ekm", 128 * (a + 4 * j), 128), quarter("z", c, a, j, 4)) for j in range(1 if a == 0 else 0, 4)]
+            mm(acc(ps(5, LO[c], WID[c]), terms, a == 0, a == 3))
+        ts(ch("bc", c), ps(5, LO[c], WID[c]), 2048.0, -2048.0, A.min, A.max)
+
+    def hb(c, lo, n=None):
+        return ps(6 + c % 2, lo, WID[c] if n is None else n)
+
+    def own(t, c, part):
+        n = WID[c] // 16
+        return v("ls", 16 * (NC * t + c) + 8 - (0 if part == 1 else n), 2 * n if part == 2 else n)
+
+    def heard(t, c):
+        return v("rl", 8 * (NC * t + c), WID[c] // 16)
+
+    def star(t, c):
+        return by(big("yg", c, base=BIGW * (t % 2)), own(t, c, 1))
+
+    def resolve(t, c):
+        w, lo, n, nd = WID[c], 2 * LO[c], WID[c] // 16, ND("rn", t, c)
+        mm(dup(c % 2, c, [(M["idn"], X0("rn", t, c)), (M["i1024"], nd)]))
+        for a in range(4):
+            tt(quarter("nq", c, a), big("yg", c, a, 4, BIGW * (t % 2)), ps(c % 2, 0, 4 * w), A.not_equal)
+            terms = [(M["nhalf"], ones(c)), (M["nb"], nd)] if a == 0 else []
+            terms += [(ek("e1", a + 4 * j), quarter("nq", c, a, j, 4)) for j in range(4)]
+            mm(acc(hb(c, 0), terms, a == 0, a == 3))
+        act(ch("wk", c), hb(c, 0), F.Exp, v("bk"), -16.0 * LNB)
+        mm([(hb(c, 128), M["m3"], ch("wk", c), True, True)])
+        ts(hb(c, 256), hb(c, 128), 0.0, None, A.is_gt)
+        ts(v("pr", lo + w, w), hb(c, 128), 0.0, v("kc"), A.is_gt, A.mult)
+        tt(v("pr", lo, w), ch("h16", c), hb(c, 256), A.mult)
+        mm(acc(hb(c, 384, 2 * n), [(M["i16"], v("cs", 8 - n, 2 * n))] + [(ek("e16", j), v("pr", lo + j, 2 * w - j, 16)) for j in range(16)]))
+        cp(own(t, c, 2), hb(c, 384, 2 * n))
+        send(t, heard(t, c), own(t, c, 0), "lst%d%d" % (t, c))
+        ts(ch("bh", c), hb(c, 0), 4096.0, 2048.0, A.mult, A.min)
+
+    def rewrite(t, c):
+        nd, de = ND("rn", t, c), ps(3, S + LO[c], WID[c])
+        mm(acc(de, [(M["idn"], ones(c)), (M["neg"], nd)]))
+        tt(ch("nx", c), X0("rn", t, c), de, A.mult)
+        tt(ch("na", c), star(t, c), nd, A.mult)
+        tt(by(v("xs", 16 * LO[c], 16 * WID[c]), own(t, c, 1)), ch("na", c), ch("nx", c), A.add)
+
+    def judge(t, c):
         w = WID[c]
-        SC(lambda s: s.activation(B("fk", c)[:], bank(5, 128 - 128 * c, w), F.Copy), ["F%d" % c], ["fk%d" % c], [5])
-        mm([(bank(5, 256 + 192 * c, w), T.m2[:], B("fk", c)[:], True, True)], ["m2", "fk%d" % c], ["mp%d" % c], [5])
+        wh, room, yf = ps(2, S + LO[c], w), ps(2 + c % 2, 384, w), ps(c % 2, 0, w)
+        mm([(wh, M["idn"], W("ra", t, c), True, True)])
+        tt(ch("un", c), star(t, c), X0("rn", t, c), A.not_equal)
+        mm(acc(room, [(M["idn"], cnt_a("ra", t, c))] + ([(M["idn"], ch("q", c))] if t else []) + [(M["nb"], ch("un", c))]))
+        act(ch("nf", c), room, F.Relu, 5.5 * 2.0 ** 60, 2.0 ** 60)
+        tt(ch("zf", c), ch("un", c), wh, A.mult)
+        mm([(yf, M["m1s"], ch("zf", c), True, True)])
+        tt(ch("sp", c, S * t), yf, ch("nf", c), A.is_gt)
+        send(t, ch("rp", c, S * t), ch("sp", c, S * t), "phi%d%d" % (t, c))
 
-    def mask_m(c):
-        w = WID[c]
-        V(lambda v: v.tensor_scalar(B("mk", c)[:], bank(5, 256 + 192 * c, w), T.tc[:], None, A.is_gt), ["mp%d" % c, "tc"], ["mk%d" % c], [5])
+    def refill(w, t, c):
+        st, b, tm, lst = (("c16", "bc", "tc", heard(t, c)), ("h16", "bh", "th", own(t, c, 0)))[w]
+        out = ps(5 - w, 384, WID[c]) if c == 0 else ps(6 + w, 400, WID[c])
+        mm(acc(out, [(M["i16"], ch(st, c)), (M["idn"], ch(b, c)), (M["i2048"], ones(c))]))
+        tt(ch(tm, c), by(v("az"), lst), ch(b, c), A.subtract)
+        tt(ch(st, c), ch(tm, c), out, A.min)
+        ts(ch((("cu", "hu") if t < RO - 1 else ("cf", "hf"))[w], c), ch(st, c), 2048.0, None, A.add)
 
-    def mask3(c):
-        SC(lambda s: s.activation(B("km", c)[:], B("mk", c)[:], F.Copy, bias=1.0, scale=-1.0), ["mk%d" % c], ["km%d" % c])
-        V(lambda v: v.tensor_tensor(B("ck", c)[:], T.cf[:, sl(c)], B("km", c)[:], A.mult), ["cf%d" % c, "km%d" % c], ["ck%d" % c])
+    def moves(t):
+        r, rf = ps(2, 0, S), ps(3, 0, S)
+        mm([(r, M["idn"], v("rb"), True, True)])
+        for phi, src, dst in ((v("rp", S * t, S), v("rb"), v("rb1")), (v("sp", S * t, S), v("rb1"), v("rb"))):
+            tt(v("p1"), phi, r, A.mult)
+            mm([(rf, M["bo"], v("p1"), True, True)])
+            tt(v("t1"), rf, src, A.is_gt)
+            mm(acc(r, [(M["idn"], src), (M["n32"], phi), (M["idn"], v("t1"))]))
+            either(dst, r, True)
 
-    def xb(c):
-        return 2 + c
+    def last_moves(c):
+        t, w, lo = RO - 1, WID[c], LO[c]
+        sp, rp, p1, t1, rb, m = ch("sp", c, S * t), ch("rp", c, S * t), ch("p1", c), ch("t1", c), ch("rb", c), ch("rb1", c)
+        r, rf, cap, ahead, dd = ps(0, 256 + lo, w), ps(1, 256 + lo, w), ps(4, lo, w), ps(3, lo, w), ps(4, S + lo, w)
+        mm([(r, M["idn"], rb, True, True)])
+        tt(p1, sp, r, A.mult)
+        mm([(rf, M["bo"], p1, True, True)])
+        tt(t1, rf, rb, A.is_gt)
+        mm(acc(r, [(M["idn"], rb), (M["n32"], sp), (M["idn"], t1)]))
+        either(m, r, True)
+        mm(acc(cap, [(M["bo"], sp), (M["neg"], sp), (M["i32"], ones(c)), (M["n32"], rp)]))
+        tt(p1, rp, r, A.mult)
+        mm(acc(ahead, [(M["neg"], m), (M["n16"], sp), (M["bo"], p1)]))
+        tt(dd, m, cap, A.min)
+        ts(t1, ahead, 0.0, None, A.is_gt)
+        tt(ch("rf", c), t1, dd, A.add)
 
-    def hb(c):
-        return 7 - c
-
-    def hear_in(t, c):
-        rm, w = T["rM%d%d" % (t, c)], WID[c]
-        mm([(bank(xb(c), j, 4 * w - j, 4), T.i16[:], rm[:], True, True) for j in range(4)], ["i16", "rm%d%d" % (t, c)], ["xm%d" % c], [xb(c)])
-
-    def hear_nd(t, c):
-        V(lambda v: v.tensor_scalar(B("nd", c)[:], T["rM%d%d" % (t, c)][:], 512.0, None, A.is_ge), ["rm%d%d" % (t, c)], ["nd%d" % c])
-
-    def hear_px(t, c):
-        rm, w = T["rM%d%d" % (t, c)], WID[c]
-        mm([(bank(c, 0, w), T.i16[:], rm[:], True, False), (bank(c, 0, w), T.ibig[:], B("nd", c)[:], False, True)],
-           ["i16", "ibig", "nd%d" % c, "rm%d%d" % (t, c)], ["pre%d" % c], [c])
-        if t < RO - 1:
-            SC(lambda s: s.activation(B("de", c)[:], B("nd", c)[:], F.Copy, bias=1.0, scale=-1.0), ["nd%d" % c], ["de%d" % c])
-
-    def hear_pw(t, c):
-        w = WID[c]
-        mm([(bank(c, w, w), T.idn[:], B("rW", t)[:, sl(c)], True, True)], ["idn", "rw%d" % t], ["pw%d" % c], [c])
-
-    def hear_nx(t, c):
-        w = WID[c]
-        if t < RO - 1:
-            V(lambda v: v.tensor_tensor(B("nx", c)[:], B("de", c)[:], bank(c, 0, w), A.mult), ["de%d" % c, "pre%d" % c], ["nx%d" % c], [c])
-
-    def hear_cmp(c, a):
-        V(lambda v: v.tensor_tensor(B("yr", c)[:, qr(c, a)], B("yg", c)[:, a:16 * WID[c]:4], bank(xb(c), 0, 4 * WID[c]), A.not_equal),
-          gk("yg", c) + ["xm%d" % c], ["yr%d%d" % (c, a)], [xb(c)])
-
-    def hear_cnt(t, c, a):
-        seq, w = [], WID[c]
-        if a == 1:
-            seq.append((bank(hb(c), 0, w), T.nb[:], B("nd", c)[:], False, False))
-        for j in range(4):
-            seq.append((bank(hb(c), 0, w), ek(a + 4 * j), B("yr", c)[:, qj(c, a, j)], a + j == 0, a + j == 6))
-        mm(seq, ekk + ["yr%d%d" % (c, a)] + (["nb", "nd%d" % c] if a else []), ["miss%d" % c], [hb(c)])
-
-    def hear_b(t, a):
-        hear_cmp(1, a)
-        if a == 0:
-            hear_nd(t, 1)
-        hear_cnt(t, 1, a)
-
-    def pick1(t, c):
-        h, w = hb(c), WID[c]
-        SC(lambda s: s.activation(B("wk", c)[:], bank(h, 0, w), F.Exp, bias=T.bk[:], scale=-16.0 * LNB), ["miss%d" % c, "bk"], ["wk%d" % c], [h])
-        SC(lambda s: s.activation(B("hm", c)[:], bank(h, 0, w), F.Sign), ["miss%d" % c], ["hm%d" % c], [h])
-        mm([(bank(h, 128, w), T.m3[:], B("wk", c)[:], True, True)], ["m3", "wk%d" % c], ["G%d" % c], [h])
-
-    def pick2(t, c):
-        h, w = hb(c), WID[c]
-        pr, n = B("pr", c), WID[c] // 8
-        V(lambda v: v.tensor_scalar(B("ow", c)[:], bank(h, 128, w), 0.0, None, A.is_gt), ["G%d" % c], ["ow%d" % c], [h])
-        V(lambda v: v.tensor_scalar(pr[:, w:2 * w], bank(h, 128, w), 0.0, T.kc[:], A.is_gt, A.mult), ["G%d" % c, "kc"], ["prq%d" % c], [h])
-        V(lambda v: v.tensor_tensor(pr[:, 0:w], B("ow", c)[:], T.hm16[:, sl(c)], A.mult), ["ow%d" % c, "hm16%d" % c], ["prn%d" % c])
-        seq = [(bank(h, 256, n), T.i16[:], B("cs", c)[:], True, False)]
-        for k in range(16):
-            seq.append((bank(h, 256, n), ek16(k), pr[:, k:2 * w:16], False, k == 15))
-        mm(seq, ["i16", "csa%d" % c, "csb%d" % c, "ek16", "prq%d" % c, "prn%d" % c], ["lp%d" % c], [h])
-
-    def pick3(t, c):
-        h, n = hb(c), WID[c] // 16
-        lt = T["L%d%d" % (t, c)]
-        V(lambda v: v.tensor_copy(lt[:], bank(h, 256, 2 * n)), ["lp%d" % c], ["L%d" % c], [h])
-        send(t, T["rL%d%d" % (t, c)][:], lt[:, 0:n], "lst%d%d" % (t, c), ["L%d" % c], ["rl%d%d" % (t, c)])
-
-    def post_h(t, c):
-        hf, n = T.hf[:, sl(c)], WID[c] // 16
-        lt = T["L%d%d" % (t, c)]
-        hd = B("hd", c)
-        V(lambda v: v.tensor_tensor(hd[:], T.az[:, :].indirect(lt[:, 0:n]), hf, A.subtract), ["az", "L%d" % c, "hf%d" % c], ["hd%d" % c])
-        V(lambda v: v.tensor_tensor(hd[:], hd[:], B("hm", c)[:], A.mult), ["hm%d" % c], ["hd%d" % c])
-        V(lambda v: v.tensor_tensor(hf, hf, hd[:], A.add), ["hd%d" % c], ["hf%d" % c])
-        if t < RO - 1:
-            V(lambda v: v.tensor_copy(T.hu[:, sl(c)], hf), ["hf%d" % c], ["hu%d" % c])
-            V(lambda v: v.tensor_scalar(T.hm16[:, sl(c)], hf, -2048.0, None, A.add), ["hf%d" % c], ["hm16%d" % c])
-
-    def post_y(t, c):
-        lt, n = T["L%d%d" % (t, c)], WID[c] // 16
-        SC(lambda s: s.activation(B("ys", c)[:], T.xs[:, :].indirect(lt[:, 0:n]), F.Copy), ["xs", "L%d" % c], ["ys%d" % c])
-
-    def post_na(t, c):
-        lt, n, w = T["L%d%d" % (t, c)], WID[c] // 16, WID[c]
-        V(lambda v: v.tensor_tensor(B("na", c)[:], T.xs[:, :].indirect(lt[:, 0:n]), B("nd", c)[:], A.mult),
-          ["xs", "L%d" % c, "nd%d" % c], ["na%d" % c])
-
-    def post_un(t, c):
-        w = WID[c]
-        V(lambda v: v.tensor_tensor(B("un", c)[:], B("ys", c)[:], bank(c, 0, w), A.not_equal), ["ys%d" % c, "pre%d" % c], ["un%d" % c], [c])
-        V(lambda v: v.tensor_tensor(B("zf", c)[:], B("un", c)[:], bank(c, w, w), A.mult), ["un%d" % c, "pw%d" % c], ["zf%d" % c], [c])
-        u = 4 - c
-        mm([(bank(u, 0, w), T.bo[:], B("un", c)[:], True, True), (bank(u, 128, w), T.m1[:], B("zf", c)[:], True, True)],
-           ["bo", "m1", "un%d" % c, "zf%d" % c], ["UY%d" % c], [u])
-
-    def post_phi(t, c):
-        w, u = WID[c], 4 - c
-        V(lambda v: v.tensor_tensor(B("tt", c)[:], bank(u, 0, w), B("rW", t)[:, S + LO[c]:S + LO[c] + w], A.is_le), ["UY%d" % c, "rw%d" % t], ["tt%d" % c], [u])
-        V(lambda v: v.tensor_tensor(B("sP", t)[:, sl(c)], bank(u, 128, w), B("tt", c)[:], A.is_gt), ["UY%d" % c, "tt%d" % c], ["sp%d%d" % (t, c)], [u])
-
-    def send_phi(t):
-        send(t, B("rP", t)[:], B("sP", t)[:], "phi%d" % t, ["sp%d%d" % (t, c) for c in range(NC)], ["rp%d" % t])
-
-    def scatter(t, c):
-        lt, n = T["L%d%d" % (t, c)], WID[c] // 16
-        V(lambda v: v.tensor_tensor(T.xs[:, :].indirect(lt[:, n:2 * n]), B("na", c)[:], B("nx", c)[:], A.add),
-          ["L%d" % c, "na%d" % c, "nx%d" % c], ["xs"])
-
-    def cupd(t, c):
-        V(lambda v: v.tensor_tensor(B("ct", c)[:], T.az[:, :].indirect(T["rL%d%d" % (t, c)][:]), B("mk", c)[:], A.mult),
-          ["az", "rl%d%d" % (t, c), "mk%d" % c], ["ct%d" % c])
-        V(lambda v: v.tensor_tensor(T.cf[:, sl(c)], B("ct", c)[:], B("ck", c)[:], A.add), ["ct%d" % c, "ck%d" % c], ["cf%d" % c])
-        if t < RO - 1:
-            V(lambda v: v.tensor_copy(T.cu[:, sl(c)], T.cf[:, sl(c)]), ["cf%d" % c], ["cu%d" % c])
-
-    def move1(phi, pk, rb, rk, pb, m):
-        V(lambda v: v.tensor_tensor(pb[:], phi[:], rb[:], A.mult), [rk] + pk, [pb.name])
-        mm([(bank(m, 0, S), T.bo[:], pb[:], True, True)], ["bo", pb.name], ["rf"], [m])
-        mm([(bank(m + 1, 0, S), T.idn[:], rb[:], True, False), (bank(m + 1, 0, S), T.ni[:], pb[:], False, False)],
-           ["idn", "ni", rk, pb.name], ["RR"], [m + 1])
-
-    def move2(rb, rk, tb, m):
-        V(lambda v: v.tensor_tensor(tb[:], bank(m, 0, S), rb[:], A.is_gt), ["rf", rk], [tb.name], [m])
-        mm([(bank(m + 1, 0, S), T.idn[:], tb[:], False, True)], ["idn", tb.name], ["RR"], [m + 1])
-
-    def rup1(t):
-        move1(B("rP", t), ["rp%d" % t], T.rb, "rb", T.p1, 0)
-        mm([(bank(0, 192, S), T.bo[:], B("rP", t)[:], True, True)], ["bo", "rp%d" % t], ["Fo"], [0])
-
-    def rup2(t):
-        move2(T.rb, "rb", T.t1, 0)
-
-    def rup3(t):
-        V(lambda v: v.tensor_copy(T.rb2[:], bank(1, 0, S)), ["RR"], ["rb2"], [1])
-        move1(B("sP", t), ["sp%d%d" % (t, c) for c in range(NC)], T.rb2, "rb2", T.p1, 2)
-
-    def rup4(t):
-        move2(T.rb2, "rb2", T.t1, 2)
-
-    def last_orders1():
-        sp = B("sP", RO - 1)
-        sk = ["sp%d%d" % (RO - 1, c) for c in range(NC)]
-        V(lambda v: v.tensor_tensor(T.p1[:], sp[:], T.rb[:], A.mult), ["rb"] + sk, ["p1"])
-        mm([(bank(2, 0, S), T.bo[:], T.p1[:], True, True)], ["bo", "p1"], ["rf"], [2])
-        V(lambda v: v.tensor_tensor(T.t1[:], bank(2, 0, S), T.rb[:], A.is_gt), ["rf", "rb"], ["t1"], [2])
-        m = [(T.idn[:], T.rb[:]), (T.ni[:], T.p1[:]), (T.idn[:], T.t1[:])]
-        seq = []
-        for out, terms in ((bank(7, 0, S), m + [(T.mtmp[:, 128:256], sp[:])]), (bank(6, 0, S), m),
-                           (bank(6, 192, S), m + [(T.nb[:], sp[:]), (T.idn[:], sp[:])])):
-            seq += [(out, l, r, i == 0, i == len(terms) - 1) for i, (l, r) in enumerate(terms)]
-        mm(seq, ["idn", "ni", "nb", "mt1", "rb", "p1", "t1"] + sk, ["MK"], [6, 7])
-        SC(lambda s: s.activation(T.rb2[:], bank(7, 0, S), F.Copy), ["MK"], ["rb2"], [7])
-
-    def last_orders2():
-        rp = B("rP", RO - 1)
-        rk = ["rp%d" % (RO - 1)]
-        V(lambda v: v.tensor_tensor(T.p1[:], rp[:], bank(6, 0, S), A.mult), ["MK"] + rk, ["p1"], [6])
-        mm([(bank(5, 0, S), T.bo[:], T.p1[:], True, True)], ["bo", "p1"], ["m1f"], [5])
-        V(lambda v: v.tensor_tensor(T.t1[:], rp[:], bank(6, 192, S), A.mult), ["MK"] + rk, ["t1"], [6])
-        V(lambda v: v.tensor_tensor(bank(0, 0, S), bank(6, 0, S), T.t1[:], A.subtract), ["MK", "t1"], ["dd"], [6, 0])
-        V(lambda v: v.tensor_tensor(T.p1[:], bank(5, 0, S), T.rb2[:], A.is_gt), ["m1f", "rb2"], ["p1"], [5])
-        V(lambda v: v.tensor_tensor(T.rout[:, 0:S], T.p1[:], bank(0, 0, S), A.add), ["p1", "dd"], ["rout"], [0])
-        dma("Y", T.ypref[:], T.rout[:, 0:S], "o2", ["rout"], [])
-        mm([(bank(4, 192, S), T.bo[:], rp[:], True, True)], ["bo"] + rk, ["Fo"], [4])
-        V(lambda v: v.tensor_tensor(T.rout[:, S:2 * S], bank(4, 192, S), T.a32[:], A.add), ["Fo", "a32"], ["aout"], [4])
-        dma("S", T.yfail[:], T.rout[0:128:16, S:2 * S], "o3", ["aout"], [])
-
-    def rup5(t):
-        SC(lambda s: s.activation(T.rb[:], bank(3, 0, S), F.Copy), ["RR"], ["rb"], [3])
-
-    def aup(t):
-        V(lambda v: v.tensor_tensor(T.a32[:], bank(0, 192, S), T.a32[:], A.add), ["Fo"], ["a32"], [0])
-
-    cb = OPT["cb"]
-    if OPT["sq"]:
-        cb = 0
     for t in range(RO):
+        for c in range(NC):
+            gather(t, "xg", "cu", c)
+            gather(t, "yg", "hu", c, BIGW * (t % 2))
+            if t > 0:
+                weights(t, c)
+        cp(X0("sn", t), v("xg", 0, BIGW, 16))
         if t == 0:
-            gx("S", 0, 0)
-            gx("V", 0, 1)
-            x0dup(0)
-            orders()
-            gx("S", 1, 0)
-            wdup(t, 0)
-            for a in range(4):
-                spk_cmp(0, a)
-            x0dup(1)
-            wdup(t, 1)
-            counts()
-            thr(t)
-        else:
-            x0dup(0)
-            cupd(t - 1, 1)
-            gx("S", 1, 0)
-            for a in range(4):
-                spk_cmp(0, a)
-            wdup(t, 0)
-            wcopy(t, 0)
-            x0dup(1)
-            wdup(t, 1)
-            for a in range(cb):
-                spk_cmp(1, a)
-        for a in range(4):
-            spk_wt(0, a)
-            spk_y(0, a)
-            spk_relu(0, a)
-            if a > 0:
-                spk_sum(0, a - 1)
-        for a in range(4):
-            if t == 0 or a >= cb:
-                spk_cmp(1, a)
-            spk_wt(1, a)
-            spk_y(1, a)
-            if a < OPT["vr"]:
-                spk_relu(1, a)
-            if a == 0:
-                spk_sum(0, 3)
-            elif a <= OPT["vr"]:
-                spk_sum(1, a - 1)
-            if a == OPT["nda"]:
-                spk_nd(t, 0)
-        for a in range(OPT["vr"], 4):
-            spk_relu(1, a)
-            spk_sum(1, a)
-        if OPT["vr"] == 4:
-            spk_sum(1, 3)
-        spk_nd(t, 1)
-        if t == 0:
-            late_constants()
-        else:
-            wcopy(t, 1)
-            rup1(t - 1)
-        for a in range(4):
-            mask_f(0, a)
-        gy("V", 0, 0)
-        gy("S", 0, 1)
+            counts(t)
+        for c in range(NC):
+            describe(t, c)
         if t > 0:
-            rup2(t - 1)
-            aup(t - 1)
-            thr(t)
-            post_h(t - 1, 1)
-        for a in range(4):
-            mask_f(1, a)
-        gy("S", 1, 0)
-        hear_in(t, 0)
-        for a in range(4):
-            hear_cmp(0, a)
-            if a == 0:
-                hear_nd(t, 0)
-            hear_cnt(t, 0, a)
-            if a == 1:
-                hear_in(t, 1)
-        mask_k(0)
-        pick1(t, 0)
-        hear_b(t, 0)
-        hear_b(t, 1)
-        pick2(t, 0)
-        mask_m(0)
-        hear_b(t, 2)
-        hear_b(t, 3)
-        pick1(t, 1)
+            counts(t)
+        wax(t)
+        for c in range(NC):
+            tops(c)
         if t > 0:
-            rup3(t - 1)
-        mask_k(1)
-        hear_px(t, 0)
-        pick3(t, 0)
-        post_y(t, 0)
-        hear_nx(t, 0)
-        if t < RO - 1:
-            post_na(t, 0)
-        mask3(0)
-        pick2(t, 1)
-        if t > 0:
-            rup4(t - 1)
-        post_h(t, 0)
-        hear_px(t, 1)
-        hear_pw(t, 0)
-        hear_pw(t, 1)
-        pick3(t, 1)
-        post_y(t, 1)
-        if t > 0:
-            rup5(t - 1)
-        if t < RO - 1:
-            post_na(t, 1)
-        post_un(t, 0)
-        post_un(t, 1)
-        post_phi(t, 0)
-        post_phi(t, 1)
-        send_phi(t)
-        hear_nx(t, 1)
-        if t < RO - 1:
-            scatter(t, 0)
-            scatter(t, 1)
-        mask_m(1)
-        cupd(t, 0)
-        mask3(1)
-        if t < RO - 1:
-            gx("V", 0, 0)
-            gx("S", 0, 1)
-        else:
-            post_h(t, 1)
-            dma("Y", T.ycand[:], T.hf[:], "o1", ["hf0", "hf1"], [])
-            last_orders1()
-    cupd(RO - 1, 1)
-    dma("Y", T.yctx[:], T.cf[:], "o0", ["cf0", "cf1"], [])
-    last_orders2()
+            ts(v("q"), cnt_a("ra", t), 3.5, -4.0, A.is_ge, A.mult)
+            moves(t - 1)
+        for c in range(NC):
+            resolve(t, c)
+        for c in range(NC):
+            if t < RO - 1:
+                rewrite(t, c)
+            judge(t, c)
+        for c in range(NC):
+            refill(0, t, c)
+            refill(1, t, c)
+    for c in range(NC):
+        last_moves(c)
+    mm(acc(ps(2, 0, S, rows=8), [(v("bo", 0, 113, 16), v("rp", S * s, S)) for s in range(RO)]))
+    tt(v("fo"), ps(2, 0, S, rows=8), v("fi"), A.add)
+    store("Y", T.ycand, "hf", "o1")
+    store("Y", T.yctx, "cf", "o0")
+    store("Y", T.ypref, "rf", "o2")
+    store("S", T.yfail, "fo", "o3")
+
+    for i, q in plan(calls):
+        issue(q, calls[i])
     for s in ("o0", "o1", "o2", "o3"):
         g.sync.wait_ge(T.sem[s], 16)
     for q in ("V", "S", "P", "G"):
-        K["need"]("G", (QS[q], K["cnt"][q]))
+        need("G", (QS[q], cnt[q]))
     g.wait_ge(T.sem["loc"], nloc[0])

@@ -4,19 +4,22 @@ from concourse.mybir import AluOpType as A, ActivationFunctionType as F
 
 RO = 3
 S = 192
-WID = [128, 64]
-LO = [0, 128]
-NC = len(WID)
 BIGW = 16 * S
-OPT = {"passes": 4, "xg": [[0, 1], [0], [0]], "yg": [[0], [0], [0]], "piece": 32, "cyc": 0.95, "pe": 0.55, "hop": 110, "flight": 1900, "look": 200, "spare": 400, "fix": 40, "gat": 1.56}
+ALL = (0, S)
+TWO = [(0, 128), (128, 64)]
+THREE = [(0, 64), (64, 64), (128, 64)]
+OPT = {"passes": 4, "steps": 60000, "xg": [[0], [], []], "yg": [[4, 5, 6, 7]] * 3, "piece": (32, 16), "cyc": 0.85, "pe": 0.45, "hop": 160, "flight": 1300, "fix": 50,
+       "gat": 1.3, "lx": 4800, "mp": 0, "mt": 0, "kc": 1, "kh": 1, "hd": 1, "hr": 1,
+       "des": THREE, "res": TWO, "jud": TWO, "rew": [ALL], "tol": [ALL], "kcr": TWO, "las": [ALL],
+       "cre": [((0, 64), (5, 384)), ((64, 128), (4, 384))], "hre": [(ALL, (7, 256))]}
 
 SCRATCH = {"ps": ("psum", [128, 4096], "float32"), "xs": ("sbuf", [128, 4096], "bfloat16"), "az": ("sbuf", [128, 4096], "int32"),
            "fi": ("sbuf", [8, S], "int32"), "f3": ("sbuf", [8, S], "int32"), "fb": ("sbuf", [8, S], "bfloat16"), "fo": ("sbuf", [8, S], "float32"),
            "k8a": ("sbuf", [8, 128], "bfloat16"), "k8": ("sbuf", [8, 128], "bfloat16")}
 for _d, _l in (("int32", (("ci", S), ("hi", S), ("ri", S), ("pi", 1), ("ki", 1))),
-               ("uint16", (("cu", S), ("hu", S), ("ls", 16 * RO * NC), ("rl", 8 * RO * NC))),
+               ("uint16", (("cu", S), ("hu", S), ("ln", 16 * RO), ("lk", 16 * RO), ("rl", 16 * RO))),
                ("float16", (("c16", S), ("h16", S), ("tc", S), ("th", S), ("pr", 2 * S), ("i16", 128), ("e16", 144), ("cs", 16))),
-               ("float32", (("cf", S), ("hf", S), ("rf", S), ("kc", 1), ("k16", 1), ("bk", 1), ("cm", 1), ("lw", 1), ("rq", 8))),
+               ("float32", (("cf", S), ("hf", S), ("rf", S), ("kc", 1), ("k16", 1), ("bk", 1), ("cm", 1), ("lw", 1), ("rq", 12))),
                ("bfloat16", (("xg", BIGW), ("yg", 2 * BIGW), ("z", BIGW), ("yr", BIGW), ("nq", BIGW), ("ekm", 2048), ("e1", 144), ("es", 144),
                              ("sa", 2 * S * RO), ("ra", 2 * S * RO), ("sn", 2 * S * RO), ("rn", 2 * S * RO), ("sp", S * RO), ("rp", S * RO),
                              ("ones", S), ("bo0", 128), ("bo", 128), ("idn", 128), ("m1", 128), ("m1s", 128), ("m3", 128), ("nb", 128), ("nb0", 128),
@@ -27,8 +30,9 @@ for _d, _l in (("int32", (("ci", S), ("hi", S), ("ri", S), ("pi", 1), ("ki", 1))
         SCRATCH[_n] = ("sbuf", [128, _w], _d)
 SEMAPHORES = ["sv", "ss", "st", "sg", "lctx", "lcand", "lpref", "lfail", "lx", "las", "loc", "o0", "o1", "o2", "o3"]
 for _t in range(RO):
-    SEMAPHORES += ["wax%d" % _t] + ["%s%d%d" % (_n, _t, _c) for _n in ("nd", "lst", "phi") for _c in range(NC)]
+    SEMAPHORES += ["wax%d" % _t, "tar%d" % _t] + ["%s%d%d" % (_n, _t, _c) for _n in ("nd", "lst", "phi") for _c in range(6)]
 
+ORDER = []
 QS = {"V": "sv", "S": "ss", "P": "st", "G": "sg"}
 LNB = 0.96 * math.log(2.0)
 LN2 = math.log(2.0)
@@ -52,6 +56,70 @@ def note(wrote, read, r, w, x):
         read.setdefault(n, []).append((lo, hi, x))
 
 
+def refine(calls, pre, post, order):
+    hop, n = OPT["hop"], len(calls)
+    q, ns, lat, bk = [[c[k] for c in calls] for k in ("q", "ns", "lat", "banks")]
+    gap = [[(j, lat[j] + (hop if q[j] != "P" or q[i] != "P" else 0.0)) for j in pre[i]] for i in range(n)]
+
+    def longest(order):
+        free, held, done, why, end, last = {}, [{} for _ in range(8)], [0.0] * n, [None] * n, 0.0, None
+        for i in order:
+            s, w = free.get(q[i], (0.0, None))
+            for j, d in gap[i]:
+                if done[j] + d > s:
+                    s, w = done[j] + d, j
+            for b in bk[i]:
+                for q2, j in held[b].items():
+                    if q2 != q[i] and done[j] + hop > s:
+                        s, w = done[j] + hop, j
+            done[i], why[i] = s + ns[i], w
+            free[q[i]] = (done[i], i)
+            for b in bk[i]:
+                held[b][q[i]] = i
+            if done[i] + lat[i] > end:
+                end, last = done[i] + lat[i], i
+        return end, why, last
+
+    now = longest(order)
+    best, pairs, steps = (now[0], order), None, OPT["steps"]
+    for step, (u0, u1, u2, u3, u4) in enumerate(np.random.default_rng(0).random((steps, 5)).tolist()):
+        if pairs is None:
+            pairs, i = [], now[2]
+            while now[1][i] is not None:
+                if now[1][i] not in pre[i] and q[i] != "Y":
+                    pairs.append((now[1][i], i))
+                i = now[1][i]
+            place = {x: k for k, x in enumerate(order)}
+        a, b = pairs[int(u0 * len(pairs))]
+        lo, hi = place[a], place[b]
+        if u1 < 0.15:
+            lo = max(0, lo - 1 - int(12 * u2))
+        elif u1 < 0.3:
+            hi = min(n - 1, hi + 1 + int(12 * u2))
+        part = order[lo:hi + 1]
+        if u3 < 0.5:
+            move = {b}
+            for x in reversed(part):
+                if any(y in move for y in post[x]):
+                    move.add(x)
+            new = [x for x in part if x in move] + [x for x in part if x not in move]
+        else:
+            move = {a}
+            for x in part:
+                if any(y in move for y in pre[x]):
+                    move.add(x)
+            new = [x for x in part if x not in move] + [x for x in part if x in move]
+        if a in move and b in move:
+            continue
+        tried = order[:lo] + new + order[hi + 1:]
+        got = longest(tried)
+        if got[0] <= now[0] - math.log(u4 + 1e-12) * hop * OPT.get("heat", 0.4) * (1 - step / steps):
+            order, now, pairs = tried, got, None
+            if got[0] < best[0]:
+                best = (got[0], tried)
+    return best[1]
+
+
 def plan(calls):
     hop, n = OPT["hop"], len(calls)
     wrote, read, group, loose = {}, {}, {}, {}
@@ -71,30 +139,24 @@ def plan(calls):
         pre.append(sorted(p))
         for j in pre[i]:
             post[j].append(i)
-        c["banks"] = banks(c["r"] + c["w"])
 
-    def lay(rank, before, after, back, fixed):
+    def lay(rank, before, after, back):
         busy, held, at, left = {}, {}, {}, [len(p) for p in before]
         ready = [i for i in range(n) if not left[i]]
         while ready:
             i = min(ready, key=lambda j: (rank[j], j))
             ready.remove(i)
-            c, best = calls[i], None
-            s0 = max([at[j][1] + (hop if calls[j]["first"] != "P" or c["first"] != "P" else 0.0) + calls[i if back else j]["lat"] for j in before[i]],
-                     default=c["lat"] if back else 0.0)
-            for q in ([fixed[i]] if fixed else c["on"]):
-                d, s = c["on"][q][0], s0
-                taken = sorted(busy.get(q, []) + [(a - hop, b + hop) for k in c["banks"] for a, b, q2 in held.get(k, []) if q2 != q])
-                for a, b in taken:
-                    if b > s and a < s + d:
-                        s = b
-                key = s + d + (OPT["spare"] if q != c["first"] else 0.0)
-                if best is None or key < best[0]:
-                    best = (key, s, s + d, q)
-            at[i] = best[1:]
-            busy.setdefault(best[3], []).append(best[1:3])
+            c = calls[i]
+            q, d = c["q"], c["ns"]
+            s = max([at[j][1] + (hop if calls[j]["q"] != "P" or q != "P" else 0.0) + calls[i if back else j]["lat"] for j in before[i]],
+                    default=c["lat"] if back else 0.0)
+            for a, b in sorted(busy.get(q, []) + [(a - hop, b + hop) for k in c["banks"] for a, b, q2 in held.get(k, []) if q2 != q]):
+                if b > s and a < s + d:
+                    s = b
+            at[i] = (s, s + d, q)
+            busy.setdefault(q, []).append((s, s + d))
             for k in c["banks"]:
-                held.setdefault(k, []).append(best[1:])
+                held.setdefault(k, []).append(at[i])
             for j in after[i]:
                 left[j] -= 1
                 if not left[j]:
@@ -103,19 +165,18 @@ def plan(calls):
 
     way = [0.0] * n
     for i in range(n - 1, -1, -1):
-        way[i] = min(x[0] for x in calls[i]["on"].values()) + calls[i]["lat"] + max([hop + way[j] for j in post[i]], default=0.0)
+        way[i] = calls[i]["ns"] + calls[i]["lat"] + max([hop + way[j] for j in post[i]], default=0.0)
     pin = {i: i - 1e9 for i, c in enumerate(calls) if c["sem"] and c["w"]}
     rank, best = [pin.get(i, -x) for i, x in enumerate(way)], None
     for _ in range(OPT["passes"]):
-        at = lay(rank, pre, post, False, None)
+        at = lay(rank, pre, post, False)
         end = max(at[i][1] + calls[i]["lat"] for i in range(n))
         if best is None or end < best[0]:
             best = (end, at)
-        bk = lay([-(at[i][1] + calls[i]["lat"]) for i in range(n)], post, pre, True, [at[i][2] for i in range(n)])
+        bk = lay([-(at[i][1] + calls[i]["lat"]) for i in range(n)], post, pre, True)
         rank = [pin.get(i, -bk[i][1]) for i in range(n)]
     at = best[1]
-    OPT["end"] = best[0]
-    return [(i, at[i][2]) for i in sorted(range(n), key=lambda i: (at[i][0], i))]
+    return refine(calls, pre, post, sorted(range(n), key=lambda i: (at[i][0], i)))
 
 
 def tracker(g, T):
@@ -134,8 +195,8 @@ def tracker(g, T):
             if seen[q].get(k, 0) < v:
                 seen[q][k] = v
 
-    def issue(q, c):
-        r, w = c["r"], ([] if c["lands"] else c["w"])
+    def issue(c):
+        q, r, w = c["q"], c["r"], ([] if c["lands"] else c["w"])
         toks = meet(wrote, r) + meet(read, w) + meet(wrote, [x for x in w if x not in c["goes_on"]])
         toks += [tok for b in c["banks"] for q2, tok in bank.get(b, {}).items() if q2 != q]
         top = {}
@@ -143,7 +204,7 @@ def tracker(g, T):
             top[s] = max(top.get(s, 0), n)
         for s in sorted(top, key=lambda s: s == QS.get(q)):
             need(q, (s, top[s]))
-        ins = c["on"][q][1](qq[q])
+        ins = c["run"](qq[q])
         if c["lands"]:
             return
         if c["sem"]:
@@ -180,20 +241,18 @@ def rank_program(g, core, T, topo):
     def ps(b, lo, n, step=1, rows=128):
         return v("ps", 512 * b + lo, n, step, rows)
 
-    def ch(name, c, base=0):
-        return v(name, base + LO[c], WID[c])
-
     def by(win, lst):
         return dict(win, ap=win["ap"].indirect(lst["ap"]), n=16 * lst["n"], by=lst["at"])
 
     def ap(x):
         return x["ap"] if isinstance(x, dict) else x
 
-    def call(on, out, ins, lat=0.0, sem=None, landing=False, starts=(), open_=(), goes_on=()):
+    def call(q, ns, run, out, ins, lat=0.0, sem=None, landing=False, starts=(), open_=(), goes_on=()):
         ins = [i for i in ins if isinstance(i, dict)]
-        calls.append({"on": on, "first": list(on)[0], "w": [x for o in out for x in o["at"]], "lat": lat, "sem": sem, "lands": landing,
+        calls.append({"q": q, "ns": ns, "run": run, "w": [x for o in out for x in o["at"]], "lat": lat, "sem": sem, "lands": landing,
                       "r": [x for i in ins for x in i["at"] + i["by"]] + [x for o in out for x in o["by"]],
                       "starts": starts, "open": dict(open_), "goes_on": goes_on})
+        calls[-1]["banks"] = banks(calls[-1]["r"] + calls[-1]["w"])
 
     def ns(out, a, per):
         if out["by"]:
@@ -206,46 +265,41 @@ def rank_program(g, core, T, topo):
         return 0.5 if out["two"] and a["two"] else 1.0
 
     def tt(out, a, b, o):
-        call({"V": (ns(out, a, 1 if a["ps"] or b["ps"] else 2), lambda e: e.tensor_tensor(out["ap"], a["ap"], b["ap"], o))}, [out], [a, b])
+        call("V", ns(out, a, 1 if a["ps"] or b["ps"] else 2), lambda e: e.tensor_tensor(out["ap"], a["ap"], b["ap"], o), [out], [a, b])
 
     def ts(out, a, s1, s2, *o):
-        call({"V": (ns(out, a, half(out, a)), lambda e: e.tensor_scalar(out["ap"], a["ap"], ap(s1), ap(s2), *o))}, [out], [a, s1, s2])
+        call("V", ns(out, a, half(out, a)), lambda e: e.tensor_scalar(out["ap"], a["ap"], ap(s1), ap(s2), *o), [out], [a, s1, s2])
 
     def cp(out, a):
-        call({"V": (ns(out, a, half(out, a)), lambda e: e.tensor_copy(out["ap"], a["ap"]))}, [out], [a])
+        call("V", ns(out, a, half(out, a)), lambda e: e.tensor_copy(out["ap"], a["ap"]), [out], [a])
 
     def fill(out, x):
-        call({"V": (ns(out, out, half(out, out)), lambda e: e.memset(out["ap"], x))}, [out], [])
+        call("V", ns(out, out, half(out, out)), lambda e: e.memset(out["ap"], x), [out], [])
 
     def act(out, a, f, bias=0.0, scale=1.0, more=0.0):
-        call({"S": (more + ns(out, a, 1), lambda e: e.activation(out["ap"], a["ap"], f, bias=ap(bias), scale=ap(scale)))}, [out], [a, bias, scale])
-
-    def either(out, a, relu=False, on="S"):
-        how = {"S": (ns(out, a, 1), lambda e: e.activation(out["ap"], a["ap"], F.Relu if relu else F.Copy)),
-               "V": (ns(out, a, 1), lambda e: e.tensor_scalar(out["ap"], a["ap"], 0.0, None, A.max) if relu else e.tensor_copy(out["ap"], a["ap"]))}
-        call({q: how[q] for q in on}, [out], [a])
+        call("S", more + ns(out, a, 1), lambda e: e.activation(out["ap"], a["ap"], f, bias=ap(bias), scale=ap(scale)), [out], [a, bias, scale])
 
     def sel(out, a, *rest):
-        call({"G": (170 + 2 * OPT["cyc"] * out["n"], lambda e: e.affine_select(out["ap"], a["ap"], *rest))}, [out], [a])
+        call("G", 170 + 2 * OPT["cyc"] * out["n"], lambda e: e.affine_select(out["ap"], a["ap"], *rest), [out], [a])
 
     def iota(out, pattern, mult, **kw):
-        call({"G": (150.0, lambda e: e.iota(out["ap"], pattern, 0, mult, **kw))}, [out], [])
+        call("G", 150.0, lambda e: e.iota(out["ap"], pattern, 0, mult, **kw), [out], [])
 
     def mm(seq):
         def run(e):
             return [e.matmul(o["ap"], l["ap"], r["ap"], start, stop) for o, l, r, start, stop in seq][-1]
         started = [x for s in seq if s[3] for x in s[0]["at"]]
-        call({"P": (sum(max(64, s[2]["n"]) for s in seq) * OPT["pe"], run)}, [s[0] for s in seq], [x for s in seq for x in s[1:3]], starts=banks(started),
+        call("P", sum(max(64, s[2]["n"]) for s in seq) * OPT["pe"], run, [s[0] for s in seq], [x for s in seq for x in s[1:3]], starts=banks(started),
              open_=[(b, not s[4]) for s in seq for b in banks(s[0]["at"])], goes_on=[x for s in seq for x in s[0]["at"] if x not in started])
 
     def acc(out, terms, start=True, stop=True):
         return [(out, l, r, start and i == 0, stop and i == len(terms) - 1) for i, (l, r) in enumerate(terms)]
 
     def load(q, name, src, sem, lat, after=()):
-        call({q: (60.0, lambda e: e.dma_start(T[name][:], src[:]))}, [v(name)], list(after), lat, sem)
+        call(q, 60.0, lambda e: e.dma_start(T[name][:], src[:]), [v(name)], list(after), lat, sem)
 
     def store(q, dst, name, sem):
-        call({q: (60.0, lambda e: e.dma_start(dst[:], T[name][:]))}, [], [v(name)], 2000.0, sem)
+        call(q, 60.0, lambda e: e.dma_start(dst[:], T[name][:]), [], [v(name)], 2000.0, sem)
 
     def send(t, out, in_, sem):
         peer = T.cores[rank ^ (1 << t)]
@@ -253,8 +307,8 @@ def rank_program(g, core, T, topo):
         ne = len(topo.engines(core, peer))
         lands(out["at"], (sem, ne))
         nloc[0] += ne
-        call({"G": (300.0, lambda e: e.remote_dma(out_ap=out["ap"], in_ap=in_["ap"], remote_sem=T.sem[sem], local_sem=T.sem["loc"], pid=pid, routing_id=rid,
-                                                   dma_engine_mask=topo.mask(core, peer)))}, [out], [in_], OPT["flight"] - 300.0, landing=True)
+        call("G", 300.0, lambda e: e.remote_dma(out_ap=out["ap"], in_ap=in_["ap"], remote_sem=T.sem[sem], local_sem=T.sem["loc"], pid=pid, routing_id=rid,
+                                                dma_engine_mask=topo.mask(core, peer)), [out], [in_], OPT["flight"] - 300.0 + 2.5 * in_["n"], landing=True)
 
     M = {n: v("sc", 128 * i, 128) for i, (n, _, _) in enumerate(SCALED)}
     for n in ("idn", "bo", "m1", "m1s", "m3", "nb", "nb0", "cmd", "i16"):
@@ -263,14 +317,11 @@ def rank_program(g, core, T, topo):
     def ek(name, k):
         return v(name, 15 - k, 128)
 
-    def ones(c):
-        return v("ones", 0, WID[c])
-
     load("Y", "ci", T.ctx, "lctx", 2000.0)
     load("S", "ri", T.pref, "lpref", 2500.0)
-    load("Y", "xs", T.x, "lx", 5900.0)
-    load("Y", "hi", T.cand, "lcand", 6400.0)
-    load("Y", "fi", T.fail0, "lfail", 6500.0)
+    load("S", "fi", T.fail0, "lfail", 2600.0)
+    load("Y", "xs", T.x, "lx", OPT["lx"])
+    load("Y", "hi", T.cand, "lcand", OPT["lx"] + 500)
     load("Y", "az", T.assoc, "las", 8000.0, [v("xs")])
 
     fill(v("ones"), 1.0)
@@ -281,7 +332,7 @@ def rank_program(g, core, T, topo):
     sel(v("bo0"), o128, [[-16, 8], [0, 16]], A.is_ge, 0.0, 0, 1)
     sel(v("bo"), v("bo0"), [[16, 8], [0, 16]], A.is_ge, 0.0, 15, -1)
     iota(v("pi"), [[1, 1]], 1)
-    iota(v("rq"), [[256, 8]], 0, allow_small_or_imprecise_dtypes=True)
+    iota(v("rq"), [[256, 12]], 0, allow_small_or_imprecise_dtypes=True)
     sel(v("k8a"), v("ones", 0, 128, rows=8), [[1, 128]], A.is_ge, 0.0, 0, -16)
     sel(v("k8"), v("k8a"), [[-1, 128]], A.is_ge, 0.0, 15, 16)
     for n, src, f in SCALED:
@@ -298,7 +349,7 @@ def rank_program(g, core, T, topo):
     act(v("sa", 0, S), v("rb"), F.Exp, v("lw"), -5.0 * LN2, 1300.0)
     for b in range(4):
         mm([x for k in range(4 * b, 4 * b + 4) for x in acc(ps(4 + b, 128 * (k % 4), 128), [(M["idn"], ek("es", k)), (M["idn"], M["nb0"])])])
-        either(v("ekm", 512 * b, 512), ps(4 + b, 0, 512))
+        act(v("ekm", 512 * b, 512), ps(4 + b, 0, 512), F.Copy)
     ts(v("ki"), v("pi"), 15, None, A.bitwise_and)
     cp(v("kc"), v("ki"))
     cp(v("e16"), v("e1"))
@@ -309,190 +360,230 @@ def rank_program(g, core, T, topo):
     ts(v("cm"), v("kc"), 0.0, 8192.0, A.is_equal, A.mult)
     ts(v("cm"), v("cm"), -4096.0, None, A.add)
     ts(M["cmd"], M["idn"], v("cm"), None, A.mult)
-    fill(v("cs", 0, 8), 2048.0)
-    ts(v("cs", 8, 8), v("rq"), v("k16"), None, A.add)
+    ts(v("cs", 0, 12), v("rq"), v("k16"), None, A.add)
     ts(v("c16"), v("ci"), -2048.0, None, A.add)
     cp(v("hu"), v("hi"))
     ts(v("f3"), v("fi"), 3, None, A.bitwise_and)
     cp(v("fb"), v("f3"))
     ts(v("h16"), v("hi"), -2048.0, None, A.add)
 
-    def W(name, t, c):
-        return ch(name, c, 2 * S * t)
+    def at(name, r, base=0):
+        return v(name, base + r[0], r[1])
 
-    def cnt_a(name, t, c=None):
-        return v(name, 2 * S * t + S, S) if c is None else ch(name, c, 2 * S * t + S)
+    def pat(b, base, r):
+        return ps(b, base + r[0], r[1])
 
-    def X0(name, t, c=None):
-        return v(name, 2 * S * t, S) if c is None else ch(name, c, 2 * S * t)
+    def W(name, t, r):
+        return at(name, r, 2 * S * t)
 
-    def ND(name, t, c):
-        return ch(name, c, 2 * S * t + S)
+    def AM(name, t, r):
+        return at(name, r, 2 * S * t + S)
 
-    def big(name, c, first=0, step=1, base=0):
-        return v(name, base + 16 * LO[c] + first, 16 * WID[c] - first, step)
+    X0, ND = W, AM
 
-    def quarter(name, c, a, j=0, step=1):
-        return v(name, 16 * LO[c] + 4 * WID[c] * a + j, 4 * WID[c] - j, step)
+    def one(r):
+        return v("ones", 0, r[1])
 
-    def dup(b, c, terms):
-        return [x for j in range(4) for x in acc(ps(b, j, 4 * WID[c] - j, 4), terms)]
+    def big(name, r, first=0, step=1, base=0):
+        return v(name, base + 16 * r[0] + first, 16 * r[1] - first, step)
 
-    def gather(t, name, lst, c, base=0):
-        n = OPT["piece"]
-        for lo in range(LO[c], LO[c] + WID[c], n):
-            either(v(name, base + 16 * lo, 16 * n), by(v("xs"), v(lst, lo, n)), on="V" if lo // n in OPT[name][t] else "S")
+    def parts(kind, r):
+        R = 8 if OPT[kind] and r[1] <= 64 else 4
+        return 16 // R, R
 
-    def weights(t, c):
-        out = ps(5, S + LO[c], WID[c])
-        mm(acc(out, [(M["idn"], W("sa", t - 1, c)), (M["lv%d" % (2 * t - 1)], ch("sp", c, S * (t - 1))), (M["lv%d" % (2 * t - 2)], ch("rp", c, S * (t - 1)))]))
-        either(W("sa", t, c), out)
+    def part(name, r, a, R, j=0, step=1):
+        return v(name, 16 * r[0] + R * r[1] * a + j, R * r[1] - j, step)
+
+    def dup(b, r, R, src):
+        return [(ps(b, j, R * r[1] - j, R), M["idn"], src, True, True) for j in range(R)]
+
+    def lst(name, t, r):
+        return v(name, 16 * t + r[0] // 16, r[1] // 16)
+
+    def gather(t, name, by_, base=0):
+        n = OPT["piece"][name == "yg"]
+        for lo in range(0, S, n):
+            out, src = v(name, base + 16 * lo, 16 * n), by(v("xs"), v(by_, lo, n))
+            if lo // n in OPT[name][t]:
+                cp(out, src)
+            else:
+                act(out, src, F.Copy)
+
+    def weights(t, r):
+        out = pat(5, S, r)
+        mm(acc(out, [(M["idn"], W("sa", t - 1, r)), (M["lv%d" % (2 * t - 1)], at("sp", r, S * (t - 1))), (M["lv%d" % (2 * t - 2)], at("rp", r, S * (t - 1)))]))
+        act(W("sa", t, r), out, F.Copy)
 
     def counts(t):
         out = ps(4, S, S)
         mm(acc(out, [(v("k8"), v("fb"))] + [(M["bo"], v("rp", S * s, S)) for s in range(t)]))
-        either(cnt_a("sa", t), out)
-
-    def wax(t):
+        act(AM("sa", t, ALL), out, F.Copy)
         send(t, v("ra", 2 * S * t, 2 * S), v("sa", 2 * S * t, 2 * S), "wax%d" % t)
 
-    def describe(t, c):
-        w = WID[c]
-        mm(dup(0, c, [(M["idn"], big("xg", c, 0, 16))]))
-        mm(dup(1, c, [(M["idn"], W("sa", t, c))]))
-        for a in range(4):
-            tt(quarter("z", c, a), big("xg", c, a, 4), ps(0, 0, 4 * w), A.not_equal)
-        for a in range(4):
-            tt(quarter("z", c, a), quarter("z", c, a), ps(1, 0, 4 * w), A.mult)
-            mm([(ps(2 + a % 2, 0, 4 * w), M["m1"], quarter("z", c, a), True, True)])
-            either(quarter("yr", c, a), ps(2 + a % 2, 0, 4 * w), True)
-            mm(acc(ps(4, LO[c], w), [(M["idn"], quarter("yr", c, a, j, 4)) for j in range(1 if a == 0 else 0, 4)], a == 0, a == 3))
-        act(ND("sn", t, c), ps(4, LO[c], w), F.Relu, 1.0, -1.0)
-        lo, n = (2 * S * t, S + w) if c == 0 else (2 * S * t + S + LO[c], w)
-        send(t, v("rn", lo, n), v("sn", lo, n), "nd%d%d" % (t, c))
+    def describe(t, c, r):
+        w = r[1]
+        P, R = parts("hd", r)
+        mm(dup(0, r, R, big("xg", r, 0, 16)))
+        mm(dup(1, r, R, W("sa", t, r)))
+        for a in range(P):
+            tt(part("z", r, a, R), big("xg", r, a, P), ps(0, 0, R * w), A.not_equal)
+        for a in range(P):
+            tt(part("z", r, a, R), part("z", r, a, R), ps(1, 0, R * w), A.mult)
+            mm([(ps(2 + a % 2, 0, R * w), M["m1"], part("z", r, a, R), True, True)])
+            act(part("yr", r, a, R), ps(2 + a % 2, 0, R * w), F.Relu)
+            mm(acc(pat(4, 0, r), [(M["idn"], part("yr", r, a, R, j, R)) for j in range(1 if a == 0 else 0, R)], a == 0, a == P - 1))
 
-    def tops(c):
-        for a in range(4):
-            terms = [(M["cmd"], ones(c))] if a == 0 else []
-            terms += [(v("ekm", 128 * (a + 4 * j), 128), quarter("z", c, a, j, 4)) for j in range(1 if a == 0 else 0, 4)]
-            mm(acc(ps(5, LO[c], WID[c]), terms, a == 0, a == 3))
-        ts(ch("bc", c), ps(5, LO[c], WID[c]), 2048.0, -2048.0, A.min, A.max)
+    def tell(t, r):
+        act(ND("sn", t, r), pat(4, 0, r), F.Relu, 1.0, -1.0)
+        send(t, ND("rn", t, r), ND("sn", t, r), "nd%d%d" % (t, r[0] // 32))
 
-    def hb(c, lo, n=None):
-        return ps(6 + c % 2, lo, WID[c] if n is None else n)
+    def tops(r):
+        P, R = parts("hd", r)
+        for a in range(P):
+            terms = [(M["cmd"], one(r))] if a == 0 else []
+            terms += [(v("ekm", 128 * (a + P * j), 128), part("z", r, a, R, j, R)) for j in range(1 if a == 0 else 0, R)]
+            mm(acc(pat(5, 0, r), terms, a == 0, a == P - 1))
 
-    def own(t, c, part):
-        n = WID[c] // 16
-        return v("ls", 16 * (NC * t + c) + 8 - (0 if part == 1 else n), 2 * n if part == 2 else n)
+    def keep(name, src, r, how):
+        if OPT["k" + name[1]]:
+            act(src, src, F.Sign)
+            act(at(name, r), src, F.Copy, 0.0, 2048.0)
+        else:
+            ts(at(name, r), src, *how)
 
-    def heard(t, c):
-        return v("rl", 8 * (NC * t + c), WID[c] // 16)
+    def star(t, r):
+        return by(v("yg", BIGW * (t % 2), BIGW), lst("lk", t, r))
 
-    def star(t, c):
-        return by(big("yg", c, base=BIGW * (t % 2)), own(t, c, 1))
+    def resolve(t, c, r):
+        w, lo, n, nd = r[1], 2 * r[0], r[1] // 16, ND("rn", t, r)
+        base = (3 * OPT["res"][0][1] + 16) * (c // 2)
+        miss, gap, ow, lp = [ps(6 + c % 2, base + w * i, w if i < 3 else 2 * n) for i in range(4)]
+        P, R = parts("hr", r)
+        xm = [ps(c % 2, j, R * w - j, R) for j in range(R)]
+        mm([(xm[j], M["idn"], X0("rn", t, r), j == 0, False) for j in range(R)])
+        mm([(xm[j], M["i1024"], nd, False, j == R - 1) for j in range(R)])
+        for a in range(P):
+            tt(part("nq", r, a, R), big("yg", r, a, P, BIGW * (t % 2)), ps(c % 2, 0, R * w), A.not_equal)
+            terms = [(M["nhalf"], one(r)), (M["nb"], nd)] if a == 0 else []
+            terms += [(ek("e1", a + P * j), part("nq", r, a, R, j, R)) for j in range(R)]
+            mm(acc(miss, terms, a == 0, a == P - 1))
+        act(at("wk", r), miss, F.Exp, v("bk"), -16.0 * LNB)
+        mm([(gap, M["m3"], at("wk", r), True, True)])
+        ts(ow, gap, 0.0, None, A.is_gt)
+        ts(v("pr", lo + w, w), gap, 0.0, v("kc"), A.is_gt, A.mult)
+        tt(v("pr", lo, w), at("h16", r), ow, A.mult)
+        lpn, lpk = ps(6 + c % 2, base + 3 * w, n), ps(6 + c % 2, base + 3 * w + n, n)
+        mm(acc(lp, [(ek("e16", j), v("pr", lo + j, 2 * w - j, 16)) for j in range(16)], True, False) + [(lpk, M["i16"], lst("cs", 0, r), False, True)])
+        ts(lst("ln", t, r), lpn, 2048.0, None, A.add)
+        send(t, lst("rl", t, r), lst("ln", t, r), "lst%d%d" % (t, r[0] // 32))
+        cp(lst("lk", t, r), lpk)
+        keep("bh", miss, r, (4096.0, 2048.0, A.mult, A.min))
 
-    def resolve(t, c):
-        w, lo, n, nd = WID[c], 2 * LO[c], WID[c] // 16, ND("rn", t, c)
-        mm(dup(c % 2, c, [(M["idn"], X0("rn", t, c)), (M["i1024"], nd)]))
-        for a in range(4):
-            tt(quarter("nq", c, a), big("yg", c, a, 4, BIGW * (t % 2)), ps(c % 2, 0, 4 * w), A.not_equal)
-            terms = [(M["nhalf"], ones(c)), (M["nb"], nd)] if a == 0 else []
-            terms += [(ek("e1", a + 4 * j), quarter("nq", c, a, j, 4)) for j in range(4)]
-            mm(acc(hb(c, 0), terms, a == 0, a == 3))
-        act(ch("wk", c), hb(c, 0), F.Exp, v("bk"), -16.0 * LNB)
-        mm([(hb(c, 128), M["m3"], ch("wk", c), True, True)])
-        ts(hb(c, 256), hb(c, 128), 0.0, None, A.is_gt)
-        ts(v("pr", lo + w, w), hb(c, 128), 0.0, v("kc"), A.is_gt, A.mult)
-        tt(v("pr", lo, w), ch("h16", c), hb(c, 256), A.mult)
-        mm(acc(hb(c, 384, 2 * n), [(M["i16"], v("cs", 8 - n, 2 * n))] + [(ek("e16", j), v("pr", lo + j, 2 * w - j, 16)) for j in range(16)]))
-        cp(own(t, c, 2), hb(c, 384, 2 * n))
-        send(t, heard(t, c), own(t, c, 0), "lst%d%d" % (t, c))
-        ts(ch("bh", c), hb(c, 0), 4096.0, 2048.0, A.mult, A.min)
+    def told(t, r):
+        de = pat(3, S, r)
+        mm(acc(de, [(M["idn"], one(r)), (M["neg"], ND("rn", t, r))]))
+        tt(at("nx", r), X0("rn", t, r), de, A.mult)
 
-    def rewrite(t, c):
-        nd, de = ND("rn", t, c), ps(3, S + LO[c], WID[c])
-        mm(acc(de, [(M["idn"], ones(c)), (M["neg"], nd)]))
-        tt(ch("nx", c), X0("rn", t, c), de, A.mult)
-        tt(ch("na", c), star(t, c), nd, A.mult)
-        tt(by(v("xs", 16 * LO[c], 16 * WID[c]), own(t, c, 1)), ch("na", c), ch("nx", c), A.add)
+    def rewrite(t, r):
+        tt(at("na", r), star(t, r), ND("rn", t, r), A.mult)
+        tt(by(v("xs", 0, BIGW), lst("lk", t, r)), at("na", r), at("nx", r), A.add)
 
-    def judge(t, c):
-        w = WID[c]
-        wh, room, yf = ps(2, S + LO[c], w), ps(2 + c % 2, 384, w), ps(c % 2, 0, w)
-        mm([(wh, M["idn"], W("ra", t, c), True, True)])
-        tt(ch("un", c), star(t, c), X0("rn", t, c), A.not_equal)
-        mm(acc(room, [(M["idn"], cnt_a("ra", t, c))] + ([(M["idn"], ch("q", c))] if t else []) + [(M["nb"], ch("un", c))]))
-        act(ch("nf", c), room, F.Relu, 5.5 * 2.0 ** 60, 2.0 ** 60)
-        tt(ch("zf", c), ch("un", c), wh, A.mult)
-        mm([(yf, M["m1s"], ch("zf", c), True, True)])
-        tt(ch("sp", c, S * t), yf, ch("nf", c), A.is_gt)
-        send(t, ch("rp", c, S * t), ch("sp", c, S * t), "phi%d%d" % (t, c))
+    def judge(t, c, r):
+        wh, room, yf = pat(2, S, r), ps(2 + c % 2, 384, r[1]), ps(c % 2, 0, r[1])
+        mm([(wh, M["idn"], W("ra", t, r), True, True)])
+        tt(at("un", r), star(t, r), X0("rn", t, r), A.not_equal)
+        mm(acc(room, [(M["idn"], AM("ra", t, r))] + ([(M["i2"], at("q", r))] if t else []) + [(M["nb"], at("un", r))]))
+        act(at("nf", r), room, F.Relu, (3.5 if t else 5.5) * 2.0 ** 60, 2.0 ** 60)
+        tt(at("zf", r), at("un", r), wh, A.mult)
+        mm([(yf, M["m1s"], at("zf", r), True, True)])
+        tt(at("sp", r, S * t), yf, at("nf", r), A.is_gt)
+        send(t, at("rp", r, S * t), at("sp", r, S * t), "phi%d%d" % (t, r[0] // 32))
 
-    def refill(w, t, c):
-        st, b, tm, lst = (("c16", "bc", "tc", heard(t, c)), ("h16", "bh", "th", own(t, c, 0)))[w]
-        out = ps(5 - w, 384, WID[c]) if c == 0 else ps(6 + w, 400, WID[c])
-        mm(acc(out, [(M["i16"], ch(st, c)), (M["idn"], ch(b, c)), (M["i2048"], ones(c))]))
-        tt(ch(tm, c), by(v("az"), lst), ch(b, c), A.subtract)
-        tt(ch(st, c), ch(tm, c), out, A.min)
-        ts(ch((("cu", "hu") if t < RO - 1 else ("cf", "hf"))[w], c), ch(st, c), 2048.0, None, A.add)
+    def refill(w, t, r, where):
+        st, b, tm, ls = (("c16", "bc", "tc", "rl"), ("h16", "bh", "th", "ln"))[w]
+        out = ps(where[0], where[1], r[1])
+        mm(acc(out, [(M["i16"], at(st, r)), (M["idn"], at(b, r)), (M["i2048"], one(r))]))
+        tt(at(tm, r), by(v("az"), lst(ls, t, r)), at(b, r), A.subtract)
+        tt(at(st, r), at(tm, r), out, A.min)
+        ts(at((("cu", "hu") if t < RO - 1 else ("cf", "hf"))[w], r), at(st, r), 2048.0, None, A.add)
 
     def moves(t):
         r, rf = ps(2, 0, S), ps(3, 0, S)
-        mm([(r, M["idn"], v("rb"), True, True)])
+        if not OPT["mp"]:
+            mm([(r, M["idn"], v("rb"), True, True)])
         for phi, src, dst in ((v("rp", S * t, S), v("rb"), v("rb1")), (v("sp", S * t, S), v("rb1"), v("rb"))):
-            tt(v("p1"), phi, r, A.mult)
-            mm([(rf, M["bo"], v("p1"), True, True)])
-            tt(v("t1"), rf, src, A.is_gt)
-            mm(acc(r, [(M["idn"], src), (M["n32"], phi), (M["idn"], v("t1"))]))
-            either(dst, r, True)
+            if OPT["mp"]:
+                mm(acc(r, [(M["neg"], src), (M["n16"], phi)]))
+                act(v("p1"), r, F.Relu, -16.0, -1.0)
+            else:
+                tt(v("p1"), phi, r, A.mult)
+            if OPT["mt"]:
+                mm(acc(rf, [(M["idn"], src), (M["nb"], v("p1"))]))
+                act(v("t1"), rf, F.Sign, 0.5)
+                mm(acc(r, [(M["idn"], src), (M["n32"], phi), (M["nhalf"], v("t1"))]))
+                act(dst, r, F.Relu, 0.5)
+            else:
+                mm([(rf, M["bo"], v("p1"), True, True)])
+                tt(v("t1"), rf, src, A.is_gt)
+                mm(acc(r, [(M["idn"], src), (M["n32"], phi), (M["idn"], v("t1"))]))
+                act(dst, r, F.Relu)
 
-    def last_moves(c):
-        t, w, lo = RO - 1, WID[c], LO[c]
-        sp, rp, p1, t1, rb, m = ch("sp", c, S * t), ch("rp", c, S * t), ch("p1", c), ch("t1", c), ch("rb", c), ch("rb1", c)
-        r, rf, cap, ahead, dd = ps(0, 256 + lo, w), ps(1, 256 + lo, w), ps(4, lo, w), ps(3, lo, w), ps(4, S + lo, w)
+    def last_moves(x):
+        t = RO - 1
+        sp, rp, p1, t1, rb, m = at("sp", x, S * t), at("rp", x, S * t), at("p1", x), at("t1", x), at("rb", x), at("rb1", x)
+        r, rf, cap, ahead, dd = pat(0, 256, x), pat(3, 0, x), pat(4, 0, x), pat(3, S, x), pat(4, S, x)
         mm([(r, M["idn"], rb, True, True)])
         tt(p1, sp, r, A.mult)
         mm([(rf, M["bo"], p1, True, True)])
         tt(t1, rf, rb, A.is_gt)
         mm(acc(r, [(M["idn"], rb), (M["n32"], sp), (M["idn"], t1)]))
-        either(m, r, True)
-        mm(acc(cap, [(M["bo"], sp), (M["neg"], sp), (M["i32"], ones(c)), (M["n32"], rp)]))
+        act(m, r, F.Relu)
+        mm(acc(cap, [(M["bo"], sp), (M["neg"], sp), (M["i32"], one(x)), (M["n32"], rp)]))
         tt(p1, rp, r, A.mult)
         mm(acc(ahead, [(M["neg"], m), (M["n16"], sp), (M["bo"], p1)]))
         tt(dd, m, cap, A.min)
         ts(t1, ahead, 0.0, None, A.is_gt)
-        tt(ch("rf", c), t1, dd, A.add)
+        tt(at("rf", x), t1, dd, A.add)
 
     for t in range(RO):
-        for c in range(NC):
-            gather(t, "xg", "cu", c)
-            gather(t, "yg", "hu", c, BIGW * (t % 2))
-            if t > 0:
-                weights(t, c)
-        cp(X0("sn", t), v("xg", 0, BIGW, 16))
+        gather(t, "xg", "cu")
+        gather(t, "yg", "hu", BIGW * (t % 2))
+        if t > 0:
+            for r in OPT["jud"]:
+                weights(t, r)
+        cp(X0("sn", t, ALL), v("xg", 0, BIGW, 16))
+        send(t, X0("rn", t, ALL), X0("sn", t, ALL), "tar%d" % t)
         if t == 0:
             counts(t)
-        for c in range(NC):
-            describe(t, c)
+        for c, r in enumerate(OPT["des"]):
+            describe(t, c, r)
+            for x in OPT["res"]:
+                if x[0] + x[1] == r[0] + r[1]:
+                    tell(t, x)
         if t > 0:
             counts(t)
-        wax(t)
-        for c in range(NC):
-            tops(c)
+        for r in OPT["des"]:
+            tops(r)
+        for r in OPT["kcr"]:
+            keep("bc", pat(5, 0, r), r, (2048.0, -2048.0, A.min, A.max))
         if t > 0:
-            ts(v("q"), cnt_a("ra", t), 3.5, -4.0, A.is_ge, A.mult)
+            act(v("q"), AM("ra", t, ALL), F.Sign, 3.5, -1.0)
             moves(t - 1)
-        for c in range(NC):
-            resolve(t, c)
-        for c in range(NC):
-            if t < RO - 1:
-                rewrite(t, c)
-            judge(t, c)
-        for c in range(NC):
-            refill(0, t, c)
-            refill(1, t, c)
-    for c in range(NC):
-        last_moves(c)
+        for c, r in enumerate(OPT["res"]):
+            resolve(t, c, r)
+        if t < RO - 1:
+            for r in OPT["tol"]:
+                told(t, r)
+            for r in OPT["rew"]:
+                rewrite(t, r)
+        for c, r in enumerate(OPT["jud"]):
+            judge(t, c, r)
+        for r, where in OPT["cre"]:
+            refill(0, t, r, where)
+        for r, where in OPT["hre"]:
+            refill(1, t, r, where)
+    for r in OPT["las"]:
+        last_moves(r)
     mm(acc(ps(2, 0, S, rows=8), [(v("bo", 0, 113, 16), v("rp", S * s, S)) for s in range(RO)]))
     tt(v("fo"), ps(2, 0, S, rows=8), v("fi"), A.add)
     store("Y", T.ycand, "hf", "o1")
@@ -500,8 +591,10 @@ def rank_program(g, core, T, topo):
     store("Y", T.ypref, "rf", "o2")
     store("S", T.yfail, "fo", "o3")
 
-    for i, q in plan(calls):
-        issue(q, calls[i])
+    if not ORDER:
+        ORDER.extend(plan(calls))
+    for i in ORDER:
+        issue(calls[i])
     for s in ("o0", "o1", "o2", "o3"):
         g.sync.wait_ge(T.sem[s], 16)
     for q in ("V", "S", "P", "G"):

@@ -8,27 +8,27 @@ BIGW = 16 * S
 ALL = (0, S)
 TWO = [(0, 128), (128, 64)]
 THREE = [(0, 64), (64, 64), (128, 64)]
-OPT = {"passes": 4, "steps": 60000, "xg": [[0], [], []], "yg": [[4, 5, 6, 7]] * 3, "piece": (32, 16), "cyc": 0.85, "pe": 0.45, "hop": 160, "flight": 1300, "fix": 50,
-       "gat": 1.3, "lx": 4800, "mp": 0, "mt": 0, "kc": 1, "kh": 1, "hd": 1, "hr": 1,
-       "des": THREE, "res": TWO, "jud": TWO, "rew": [ALL], "tol": [ALL], "kcr": TWO, "las": [ALL],
+OPT = {"passes": 4, "steps": 50000, "cases": [(0.8, 1.1, 0.95, 0.0, 0.75, 500.0, 15.0, 0.03), (1.2, 0.85, 1.15, 50.0, 1.1, 700.0, 60.0, 0.07)], "xg": [[0], [], []], "yg": [[2, 3]] * 3, "piece": (32, 32), "cyc": 0.85, "pe": 0.5, "hop": 145, "flight": 1400, "fix": 45, "sfix": 40,
+       "gat": 1.3, "lx": 4200, "mp": 0, "mt": 0, "hd": 1, "hr": 0,
+       "des": THREE, "res": TWO, "jud": TWO, "rew": [ALL], "tol": [ALL], "kcr": TWO, "las": TWO, "azp": 4,
        "cre": [((0, 64), (5, 384)), ((64, 128), (4, 384))], "hre": [(ALL, (7, 256))]}
 
 SCRATCH = {"ps": ("psum", [128, 4096], "float32"), "xs": ("sbuf", [128, 4096], "bfloat16"), "az": ("sbuf", [128, 4096], "int32"),
-           "fi": ("sbuf", [8, S], "int32"), "f3": ("sbuf", [8, S], "int32"), "fb": ("sbuf", [8, S], "bfloat16"), "fo": ("sbuf", [8, S], "float32"),
+           "fi": ("sbuf", [8, S], "int32"), "f3": ("sbuf", [8, S], "int32"), "fb": ("sbuf", [8, S], "bfloat16"), "fa": ("sbuf", [8, S], "bfloat16"), "fo": ("sbuf", [8, S], "float32"),
            "k8a": ("sbuf", [8, 128], "bfloat16"), "k8": ("sbuf", [8, 128], "bfloat16")}
 for _d, _l in (("int32", (("ci", S), ("hi", S), ("ri", S), ("pi", 1), ("ki", 1))),
                ("uint16", (("cu", S), ("hu", S), ("ln", 16 * RO), ("lk", 16 * RO), ("rl", 16 * RO))),
                ("float16", (("c16", S), ("h16", S), ("tc", S), ("th", S), ("pr", 2 * S), ("i16", 128), ("e16", 144), ("cs", 16))),
-               ("float32", (("cf", S), ("hf", S), ("rf", S), ("kc", 1), ("k16", 1), ("bk", 1), ("cm", 1), ("lw", 1), ("rq", 12))),
+               ("float32", (("cf", S), ("hf", S), ("rf", S), ("kc", 1), ("k16", 1), ("bk", 1), ("cm", 1), ("lv", 4), ("rq", 12))),
                ("bfloat16", (("xg", BIGW), ("yg", 2 * BIGW), ("z", BIGW), ("yr", BIGW), ("nq", BIGW), ("ekm", 2048), ("e1", 144), ("es", 144),
                              ("sa", 2 * S * RO), ("ra", 2 * S * RO), ("sn", 2 * S * RO), ("rn", 2 * S * RO), ("sp", S * RO), ("rp", S * RO),
                              ("ones", S), ("bo0", 128), ("bo", 128), ("idn", 128), ("m1", 128), ("m1s", 128), ("m3", 128), ("nb", 128), ("nb0", 128),
-                             ("cmd", 128), ("sc", 128 * 14),
+                             ("cmd", 128), ("sc", 128 * 16),
                              ("wk", S), ("bh", S), ("bc", S), ("na", S), ("nx", S), ("un", S), ("zf", S), ("nf", S), ("q", S),
                              ("rb", S), ("rb1", S), ("p1", S), ("t1", S)))):
     for _n, _w in _l:
         SCRATCH[_n] = ("sbuf", [128, _w], _d)
-SEMAPHORES = ["sv", "ss", "st", "sg", "lctx", "lcand", "lpref", "lfail", "lx", "las", "loc", "o0", "o1", "o2", "o3"]
+SEMAPHORES = ["sv", "ss", "st", "sg", "lctx", "lcand", "lpref", "lfail", "lx", "loc", "o0", "o1", "o2", "o3"] + ["las%d" % _j for _j in range(8)]
 for _t in range(RO):
     SEMAPHORES += ["wax%d" % _t, "tar%d" % _t] + ["%s%d%d" % (_n, _t, _c) for _n in ("nd", "lst", "phi") for _c in range(6)]
 
@@ -36,8 +36,8 @@ ORDER = []
 QS = {"V": "sv", "S": "ss", "P": "st", "G": "sg"}
 LNB = 0.96 * math.log(2.0)
 LN2 = math.log(2.0)
-SCALED = [("i2", "idn", 2.0), ("neg", "idn", -1.0), ("i1024", "idn", 1024.0), ("i2048", "idn", 2048.0), ("nhalf", "idn", -0.5), ("n32", "idn", -32.0),
-          ("n16", "idn", -16.0), ("i32", "idn", 32.0), ("i60", "idn", 2.0 ** 60)] + [("lv%d" % _i, "i60", 2.0 ** (35 + 5 * _i)) for _i in range(4)] + [("b41", "bo", 0.41)]
+SCALED = [("i2", "idn", 2.0), ("neg", "idn", -1.0), ("i1024", "idn", 1024.0), ("i2048", "idn", 2048.0), ("i6144", "idn", 6144.0), ("nhalf", "idn", -0.5), ("n32", "idn", -32.0),
+          ("n16", "idn", -16.0), ("i32", "idn", 32.0), ] + [("lv%d" % _i, "idn", _i) for _i in range(4)] + [("b41", "bo", 0.41)]
 
 
 def banks(pieces):
@@ -58,37 +58,60 @@ def note(wrote, read, r, w, x):
 
 def refine(calls, pre, post, order):
     hop, n = OPT["hop"], len(calls)
-    q, ns, lat, bk = [[c[k] for c in calls] for k in ("q", "ns", "lat", "banks")]
-    gap = [[(j, lat[j] + (hop if q[j] != "P" or q[i] != "P" else 0.0)) for j in pre[i]] for i in range(n)]
+    q, bk = [[c[k] for c in calls] for k in ("q", "banks")]
 
-    def longest(order):
-        free, held, done, why, end, last = {}, [{} for _ in range(8)], [0.0] * n, [None] * n, 0.0, None
-        for i in order:
-            s, w = free.get(q[i], (0.0, None))
+    stores = [i for i, c in enumerate(calls) if c["sem"] and not c["w"]]
+
+    def costs(kh, kp, kg, ks, kl, start, row, byte):
+        ns = [c["ns"] * (kp if c["q"] == "P" else kg if c["far"] else 1.0) + (ks if c["q"] == "S" else 0.0) for c in calls]
+        lat = [start if c["lands"] else kl * c["lat"] for c in calls]
+        wire = [16 * (row + byte * c["lands"]) if c["lands"] else 0.0 for c in calls]
+        return [[(j, hop * kh if q[j] != "P" or q[i] != "P" else 0.0) for j in pre[i]] for i in range(n)], ns, lat, wire, hop * kh
+
+    def timed(order, lo, old, gap, ns, lat, wire, hop):
+        free, held, link = {}, [{} for _ in range(8)], None
+        ends, done, why = old[1][:], old[2][:], old[3][:]
+        for i in order[max(0, lo - 90):lo]:
+            free[q[i]] = i
+            link = i if wire[i] else link
+            for b in bk[i]:
+                held[b][q[i]] = i
+        for i in order[lo:]:
+            w = free.get(q[i])
+            s = 0.0 if w is None else ends[w]
             for j, d in gap[i]:
                 if done[j] + d > s:
                     s, w = done[j] + d, j
             for b in bk[i]:
                 for q2, j in held[b].items():
-                    if q2 != q[i] and done[j] + hop > s:
-                        s, w = done[j] + hop, j
-            done[i], why[i] = s + ns[i], w
-            free[q[i]] = (done[i], i)
-            for b in bk[i]:
+                    if q2 != q[i] and ends[j] + hop > s:
+                        s, w = ends[j] + hop, j
                 held[b][q[i]] = i
-            if done[i] + lat[i] > end:
-                end, last = done[i] + lat[i], i
-        return end, why, last
+            ends[i] = s = s + ns[i]
+            s += lat[i]
+            if wire[i]:
+                if link is not None and done[link] > s:
+                    s, w = done[link], link
+                s, link = s + wire[i], i
+            done[i], why[i], free[q[i]] = s, w, i
+        return max((done[i], i) for i in stores), ends, done, why
 
-    now = longest(order)
+    cases = [costs(*k) for k in OPT["cases"]]
+
+    def longest(order, lo, old):
+        got = [timed(order, lo, o, *m) for o, m in zip(old, cases)]
+        return sum(x[0][0] for x in got) / len(got), got
+
+    now = longest(order, 0, [(None, [0.0] * n, [0.0] * n, [None] * n)] * len(cases))
     best, pairs, steps = (now[0], order), None, OPT["steps"]
     for step, (u0, u1, u2, u3, u4) in enumerate(np.random.default_rng(0).random((steps, 5)).tolist()):
         if pairs is None:
-            pairs, i = [], now[2]
-            while now[1][i] is not None:
-                if now[1][i] not in pre[i] and q[i] != "Y":
-                    pairs.append((now[1][i], i))
-                i = now[1][i]
+            pairs = []
+            for (_, i), _, _, why in now[1]:
+                while why[i] is not None:
+                    if why[i] not in pre[i] and q[i] != "Y":
+                        pairs.append((why[i], i))
+                    i = why[i]
             place = {x: k for k, x in enumerate(order)}
         a, b = pairs[int(u0 * len(pairs))]
         lo, hi = place[a], place[b]
@@ -112,7 +135,7 @@ def refine(calls, pre, post, order):
         if a in move and b in move:
             continue
         tried = order[:lo] + new + order[hi + 1:]
-        got = longest(tried)
+        got = longest(tried, lo, now[1])
         if got[0] <= now[0] - math.log(u4 + 1e-12) * hop * OPT.get("heat", 0.4) * (1 - step / steps):
             order, now, pairs = tried, got, None
             if got[0] < best[0]:
@@ -252,6 +275,7 @@ def rank_program(g, core, T, topo):
         calls.append({"q": q, "ns": ns, "run": run, "w": [x for o in out for x in o["at"]], "lat": lat, "sem": sem, "lands": landing,
                       "r": [x for i in ins for x in i["at"] + i["by"]] + [x for o in out for x in o["by"]],
                       "starts": starts, "open": dict(open_), "goes_on": goes_on})
+        calls[-1]["far"] = any(i["by"] for i in ins + out)
         calls[-1]["banks"] = banks(calls[-1]["r"] + calls[-1]["w"])
 
     def ns(out, a, per):
@@ -276,8 +300,8 @@ def rank_program(g, core, T, topo):
     def fill(out, x):
         call("V", ns(out, out, half(out, out)), lambda e: e.memset(out["ap"], x), [out], [])
 
-    def act(out, a, f, bias=0.0, scale=1.0, more=0.0):
-        call("S", more + ns(out, a, 1), lambda e: e.activation(out["ap"], a["ap"], f, bias=ap(bias), scale=ap(scale)), [out], [a, bias, scale])
+    def act(out, a, f, bias=0.0, scale=1.0, more=0.0, after=None):
+        call("S", more + OPT["sfix"] + ns(out, a, 1), lambda e: e.activation(out["ap"], a["ap"], f, bias=ap(bias), scale=ap(scale)), [out], [a, bias, scale, after])
 
     def sel(out, a, *rest):
         call("G", 170 + 2 * OPT["cyc"] * out["n"], lambda e: e.affine_select(out["ap"], a["ap"], *rest), [out], [a])
@@ -295,8 +319,9 @@ def rank_program(g, core, T, topo):
     def acc(out, terms, start=True, stop=True):
         return [(out, l, r, start and i == 0, stop and i == len(terms) - 1) for i, (l, r) in enumerate(terms)]
 
-    def load(q, name, src, sem, lat, after=()):
-        call(q, 60.0, lambda e: e.dma_start(T[name][:], src[:]), [v(name)], list(after), lat, sem)
+    def load(q, name, src, sem, lat, after=(), lo=0, n=None):
+        n = T[name].shape[1] if n is None else n
+        call(q, 60.0, lambda e: e.dma_start(T[name][:, lo:lo + n], src[:, lo:lo + n]), [v(name, lo, n)], list(after), lat, sem)
 
     def store(q, dst, name, sem):
         call(q, 60.0, lambda e: e.dma_start(dst[:], T[name][:]), [], [v(name)], 2000.0, sem)
@@ -308,7 +333,7 @@ def rank_program(g, core, T, topo):
         lands(out["at"], (sem, ne))
         nloc[0] += ne
         call("G", 300.0, lambda e: e.remote_dma(out_ap=out["ap"], in_ap=in_["ap"], remote_sem=T.sem[sem], local_sem=T.sem["loc"], pid=pid, routing_id=rid,
-                                                dma_engine_mask=topo.mask(core, peer)), [out], [in_], OPT["flight"] - 300.0 + 2.5 * in_["n"], landing=True)
+                                                dma_engine_mask=topo.mask(core, peer)), [out], [in_], OPT["flight"] - 300.0 + 2.5 * in_["n"], landing=2 * in_["n"])
 
     M = {n: v("sc", 128 * i, 128) for i, (n, _, _) in enumerate(SCALED)}
     for n in ("idn", "bo", "m1", "m1s", "m3", "nb", "nb0", "cmd", "i16"):
@@ -322,11 +347,12 @@ def rank_program(g, core, T, topo):
     load("S", "fi", T.fail0, "lfail", 2600.0)
     load("Y", "xs", T.x, "lx", OPT["lx"])
     load("Y", "hi", T.cand, "lcand", OPT["lx"] + 500)
-    load("Y", "az", T.assoc, "las", 8000.0, [v("xs")])
+    wide = 4096 // OPT["azp"]
+    for j in range(OPT["azp"]):
+        load("Y", "az", T.assoc, "las%d" % j, 1200.0 + 14000.0 / OPT["azp"], [v("xs") if j < 2 else v("az", wide * (j - 2), wide)], wide * j, wide)
 
     fill(v("ones"), 1.0)
     fill(v("e1"), 0.0)
-    fill(v("lw"), 90.0 * LN2)
     o128 = v("ones", 0, 128)
     sel(v("idn"), o128, [[-1, 128]], A.is_equal, 0.0, 0, 1)
     sel(v("bo0"), o128, [[-16, 8], [0, 16]], A.is_ge, 0.0, 0, 1)
@@ -335,8 +361,9 @@ def rank_program(g, core, T, topo):
     iota(v("rq"), [[256, 12]], 0, allow_small_or_imprecise_dtypes=True)
     sel(v("k8a"), v("ones", 0, 128, rows=8), [[1, 128]], A.is_ge, 0.0, 0, -16)
     sel(v("k8"), v("k8a"), [[-1, 128]], A.is_ge, 0.0, 15, 16)
+    act(v("lv"), v("rq", 0, 4), F.Exp, 95.0 * LN2, 5.0 * LN2 / 256, 1300.0)
     for n, src, f in SCALED:
-        ts(M[n], M[src], float(f), None, A.mult)
+        ts(M[n], M[src], v("lv", f, 1) if n[:2] == "lv" else float(f), None, A.mult)
     cp(v("i16"), M["idn"])
     cp(v("e1", 15, 113, 16), v("bo", 0, 113, 16))
     tt(M["m1"], M["i2"], M["bo"], A.subtract)
@@ -346,7 +373,7 @@ def rank_program(g, core, T, topo):
     fill(v("nb0", 0, 113, 16), 0.0)
     cp(v("rb"), v("ri"))
     cp(v("cu"), v("ci"))
-    act(v("sa", 0, S), v("rb"), F.Exp, v("lw"), -5.0 * LN2, 1300.0)
+    act(v("sa", 0, S), v("rb"), F.Exp, 90.0 * LN2, -5.0 * LN2, after=v("lv"))
     for b in range(4):
         mm([x for k in range(4 * b, 4 * b + 4) for x in acc(ps(4 + b, 128 * (k % 4), 128), [(M["idn"], ek("es", k)), (M["idn"], M["nb0"])])])
         act(v("ekm", 512 * b, 512), ps(4 + b, 0, 512), F.Copy)
@@ -356,15 +383,15 @@ def rank_program(g, core, T, topo):
     tt(M["m3"], M["idn"], M["b41"], A.subtract)
     ts(M["m1s"], M["m1"], 2.0 ** -60, None, A.mult)
     ts(v("k16"), v("kc"), 16.0, None, A.mult)
-    ts(v("bk"), v("kc"), -LNB, 84.5 - 8.0 * LNB, A.mult, A.add)
+    ts(v("bk"), v("kc"), -LNB, 84.5, A.mult, A.add)
     ts(v("cm"), v("kc"), 0.0, 8192.0, A.is_equal, A.mult)
     ts(v("cm"), v("cm"), -4096.0, None, A.add)
-    ts(M["cmd"], M["idn"], v("cm"), None, A.mult)
     ts(v("cs", 0, 12), v("rq"), v("k16"), None, A.add)
     ts(v("c16"), v("ci"), -2048.0, None, A.add)
     cp(v("hu"), v("hi"))
     ts(v("f3"), v("fi"), 3, None, A.bitwise_and)
     cp(v("fb"), v("f3"))
+    cp(v("fa"), v("fi"))
     ts(v("h16"), v("hi"), -2048.0, None, A.add)
 
     def at(name, r, base=0):
@@ -440,19 +467,15 @@ def rank_program(g, core, T, topo):
     def tops(r):
         P, R = parts("hd", r)
         for a in range(P):
-            terms = [(M["cmd"], one(r))] if a == 0 else []
-            terms += [(v("ekm", 128 * (a + P * j), 128), part("z", r, a, R, j, R)) for j in range(1 if a == 0 else 0, R)]
+            terms = [(v("ekm", 128 * (a + P * j), 128), part("z", r, a, R, j, R)) for j in range(1 if a == 0 else 0, R)]
             mm(acc(pat(5, 0, r), terms, a == 0, a == P - 1))
 
-    def keep(name, src, r, how):
-        if OPT["k" + name[1]]:
-            act(src, src, F.Sign)
-            act(at(name, r), src, F.Copy, 0.0, 2048.0)
-        else:
-            ts(at(name, r), src, *how)
+    def keep(t, name, src, r, bias):
+        act(src, src, F.Sign, bias)
+        act(at(name, r), src, F.Copy, 0.0 if t < RO - 1 else -2048.0, 2048.0)
 
     def star(t, r):
-        return by(v("yg", BIGW * (t % 2), BIGW), lst("lk", t, r))
+        return by(v("yg", BIGW * (t % 2), BIGW), lst("lk", t, r)) if t < RO - 1 else by(v("xs"), lst("ln", t, r))
 
     def resolve(t, c, r):
         w, lo, n, nd = r[1], 2 * r[0], r[1] // 16, ND("rn", t, r)
@@ -464,20 +487,25 @@ def rank_program(g, core, T, topo):
         mm([(xm[j], M["i1024"], nd, False, j == R - 1) for j in range(R)])
         for a in range(P):
             tt(part("nq", r, a, R), big("yg", r, a, P, BIGW * (t % 2)), ps(c % 2, 0, R * w), A.not_equal)
-            terms = [(M["nhalf"], one(r)), (M["nb"], nd)] if a == 0 else []
+            terms = [(M["nb"], nd)] if a == 0 else []
             terms += [(ek("e1", a + P * j), part("nq", r, a, R, j, R)) for j in range(R)]
             mm(acc(miss, terms, a == 0, a == P - 1))
         act(at("wk", r), miss, F.Exp, v("bk"), -16.0 * LNB)
         mm([(gap, M["m3"], at("wk", r), True, True)])
         ts(ow, gap, 0.0, None, A.is_gt)
-        ts(v("pr", lo + w, w), gap, 0.0, v("kc"), A.is_gt, A.mult)
+        if t < RO - 1:
+            ts(v("pr", lo + w, w), gap, 0.0, v("kc"), A.is_gt, A.mult)
         tt(v("pr", lo, w), at("h16", r), ow, A.mult)
         lpn, lpk = ps(6 + c % 2, base + 3 * w, n), ps(6 + c % 2, base + 3 * w + n, n)
-        mm(acc(lp, [(ek("e16", j), v("pr", lo + j, 2 * w - j, 16)) for j in range(16)], True, False) + [(lpk, M["i16"], lst("cs", 0, r), False, True)])
+        if t < RO - 1:
+            mm(acc(lp, [(ek("e16", j), v("pr", lo + j, 2 * w - j, 16)) for j in range(16)], True, False) + [(lpk, M["i16"], lst("cs", 0, r), False, True)])
+        else:
+            mm(acc(lpn, [(ek("e16", j), v("pr", lo + j, w - j, 16)) for j in range(16)]))
         ts(lst("ln", t, r), lpn, 2048.0, None, A.add)
         send(t, lst("rl", t, r), lst("ln", t, r), "lst%d%d" % (t, r[0] // 32))
-        cp(lst("lk", t, r), lpk)
-        keep("bh", miss, r, (4096.0, 2048.0, A.mult, A.min))
+        if t < RO - 1:
+            cp(lst("lk", t, r), lpk)
+        keep(t, "bh", miss, r, -0.5)
 
     def told(t, r):
         de = pat(3, S, r)
@@ -502,10 +530,13 @@ def rank_program(g, core, T, topo):
     def refill(w, t, r, where):
         st, b, tm, ls = (("c16", "bc", "tc", "rl"), ("h16", "bh", "th", "ln"))[w]
         out = ps(where[0], where[1], r[1])
-        mm(acc(out, [(M["i16"], at(st, r)), (M["idn"], at(b, r)), (M["i2048"], one(r))]))
+        mm(acc(out, [(M["i16"], at(st, r)), (M["idn"], at(b, r)), (M["i2048" if t < RO - 1 else "i6144"], one(r))]))
+        if t == RO - 1:
+            st = tm = ("cf", "hf")[w]
         tt(at(tm, r), by(v("az"), lst(ls, t, r)), at(b, r), A.subtract)
         tt(at(st, r), at(tm, r), out, A.min)
-        ts(at((("cu", "hu") if t < RO - 1 else ("cf", "hf"))[w], r), at(st, r), 2048.0, None, A.add)
+        if t < RO - 1:
+            ts(at(("cu", "hu")[w], r), at(st, r), 2048.0, None, A.add)
 
     def moves(t):
         r, rf = ps(2, 0, S), ps(3, 0, S)
@@ -539,11 +570,13 @@ def rank_program(g, core, T, topo):
         mm(acc(r, [(M["idn"], rb), (M["n32"], sp), (M["idn"], t1)]))
         act(m, r, F.Relu)
         mm(acc(cap, [(M["bo"], sp), (M["neg"], sp), (M["i32"], one(x)), (M["n32"], rp)]))
-        tt(p1, rp, r, A.mult)
-        mm(acc(ahead, [(M["neg"], m), (M["n16"], sp), (M["bo"], p1)]))
+        r0, p2, t2 = pat(1, 256, x), at("na", x), at("nx", x)
+        mm(acc(r0, [(M["idn"], rb), (M["n32"], sp)]))
+        tt(p2, rp, r0, A.mult)
+        mm(acc(ahead, [(M["neg"], rb), (M["n16"], sp), (M["bo"], p2)]))
         tt(dd, m, cap, A.min)
-        ts(t1, ahead, 0.0, None, A.is_gt)
-        tt(at("rf", x), t1, dd, A.add)
+        ts(t2, ahead, 0.0, None, A.is_gt)
+        tt(at("rf", x), t2, dd, A.add)
 
     for t in range(RO):
         gather(t, "xg", "cu")
@@ -551,7 +584,7 @@ def rank_program(g, core, T, topo):
         if t > 0:
             for r in OPT["jud"]:
                 weights(t, r)
-        cp(X0("sn", t, ALL), v("xg", 0, BIGW, 16))
+        sel(X0("sn", t, ALL), v("xg", 0, BIGW, 16), [[0, S]], A.is_ge, 0.0, 0, 0)
         send(t, X0("rn", t, ALL), X0("sn", t, ALL), "tar%d" % t)
         if t == 0:
             counts(t)
@@ -565,7 +598,7 @@ def rank_program(g, core, T, topo):
         for r in OPT["des"]:
             tops(r)
         for r in OPT["kcr"]:
-            keep("bc", pat(5, 0, r), r, (2048.0, -2048.0, A.min, A.max))
+            keep(t, "bc", pat(5, 0, r), r, v("cm"))
         if t > 0:
             act(v("q"), AM("ra", t, ALL), F.Sign, 3.5, -1.0)
             moves(t - 1)
@@ -584,8 +617,8 @@ def rank_program(g, core, T, topo):
             refill(1, t, r, where)
     for r in OPT["las"]:
         last_moves(r)
-    mm(acc(ps(2, 0, S, rows=8), [(v("bo", 0, 113, 16), v("rp", S * s, S)) for s in range(RO)]))
-    tt(v("fo"), ps(2, 0, S, rows=8), v("fi"), A.add)
+    mm(acc(ps(2, 0, S, rows=8), [(v("idn", 0, 8, rows=8), v("fa"))] + [(v("bo", 0, 113, 16), v("rp", S * s, S)) for s in range(RO)]))
+    act(v("fo"), ps(2, 0, S, rows=8), F.Copy)
     store("Y", T.ycand, "hf", "o1")
     store("Y", T.yctx, "cf", "o0")
     store("Y", T.ypref, "rf", "o2")

import math
import numpy as np
from concourse.mybir import AluOpType as A, ActivationFunctionType as F

RO = 3
S = 192
BIGW = 16 * S
ALL = (0, S)
TWO = [(0, 128), (128, 64)]
THREE = [(0, 64), (64, 64), (128, 64)]
OPT = {"passes": 4, "steps": 50000, "cases": [(0.8, 1.1, 0.95, 0.0, 0.75, 500.0, 15.0, 0.03), (1.2, 0.85, 1.15, 50.0, 1.1, 700.0, 60.0, 0.07)], "xg": [[0], [], []], "yg": [[2, 3]] * 3, "piece": (32, 32), "cyc": 0.85, "pe": 0.5, "hop": 145, "flight": 1400, "fix": 45, "sfix": 40,
       "gat": 1.3, "lx": 4200, "mp": 0, "mt": 0, "hd": 1, "hr": 0,
       "des": THREE, "res": TWO, "jud": TWO, "rew": [ALL], "tol": [ALL], "kcr": TWO, "las": TWO, "azp": 4,
       "cre": [((0, 64), (5, 384)), ((64, 128), (4, 384))], "hre": [(ALL, (7, 256))]}

SCRATCH = {"ps": ("psum", [128, 4096], "float32"), "xs": ("sbuf", [128, 4096], "bfloat16"), "az": ("sbuf", [128, 4096], "int32"),
           "fi": ("sbuf", [8, S], "int32"), "f3": ("sbuf", [8, S], "int32"), "fb": ("sbuf", [8, S], "bfloat16"), "fa": ("sbuf", [8, S], "bfloat16"), "fo": ("sbuf", [8, S], "float32"),
           "k8a": ("sbuf", [8, 128], "bfloat16"), "k8": ("sbuf", [8, 128], "bfloat16")}
for _d, _l in (("int32", (("ci", S), ("hi", S), ("ri", S), ("pi", 1), ("ki", 1))),
               ("uint16", (("cu", S), ("hu", S), ("ln", 16 * RO), ("lk", 16 * RO), ("rl", 16 * RO))),
               ("float16", (("c16", S), ("h16", S), ("tc", S), ("th", S), ("pr", 2 * S), ("i16", 128), ("e16", 144), ("cs", 16))),
               ("float32", (("cf", S), ("hf", S), ("rf", S), ("kc", 1), ("k16", 1), ("bk", 1), ("cm", 1), ("lv", 4), ("rq", 12))),
               ("bfloat16", (("xg", BIGW), ("yg", 2 * BIGW), ("z", BIGW), ("yr", BIGW), ("nq", BIGW), ("ekm", 2048), ("e1", 144), ("es", 144),
                             ("sa", 2 * S * RO), ("ra", 2 * S * RO), ("sn", 2 * S * RO), ("rn", 2 * S * RO), ("sp", S * RO), ("rp", S * RO),
                             ("ones", S), ("bo0", 128), ("bo", 128), ("idn", 128), ("m1", 128), ("m1s", 128), ("m3", 128), ("nb", 128), ("nb0", 128),
                             ("cmd", 128), ("sc", 128 * 16),
                             ("wk", S), ("bh", S), ("bc", S), ("na", S), ("nx", S), ("un", S), ("zf", S), ("nf", S), ("q", S),
                             ("rb", S), ("rb1", S), ("p1", S), ("t1", S)))):
    for _n, _w in _l:
        SCRATCH[_n] = ("sbuf", [128, _w], _d)
SEMAPHORES = ["sv", "ss", "st", "sg", "lctx", "lcand", "lpref", "lfail", "lx", "loc", "o0", "o1", "o2", "o3"] + ["las%d" % _j for _j in range(8)]
for _t in range(RO):
    SEMAPHORES += ["wax%d" % _t, "tar%d" % _t] + ["%s%d%d" % (_n, _t, _c) for _n in ("nd", "lst", "phi") for _c in range(6)]

ORDER = []
QS = {"V": "sv", "S": "ss", "P": "st", "G": "sg"}
LNB = 0.96 * math.log(2.0)
LN2 = math.log(2.0)
SCALED = [("i2", "idn", 2.0), ("neg", "idn", -1.0), ("i1024", "idn", 1024.0), ("i2048", "idn", 2048.0), ("i6144", "idn", 6144.0), ("nhalf", "idn", -0.5), ("n32", "idn", -32.0),
          ("n16", "idn", -16.0), ("i32", "idn", 32.0), ] + [("lv%d" % _i, "idn", _i) for _i in range(4)] + [("b41", "bo", 0.41)]


def banks(pieces):
    return sorted({b for n, lo, hi in pieces if n == "ps" for b in range(lo // 512, (hi - 1) // 512 + 1)})


def meet(table, pieces):
    return [x for n, lo, hi in pieces for l, h, x in table.get(n, []) if l < hi and lo < h]


def note(wrote, read, r, w, x):
    for n, lo, hi in w:
        wrote[n] = [y for y in wrote.get(n, []) if not (lo <= y[0] and y[1] <= hi)] + [(lo, hi, x)]
        read[n] = [y for y in read.get(n, []) if not (lo <= y[0] and y[1] <= hi)]
    for n, lo, hi in r:
        read.setdefault(n, []).append((lo, hi, x))


def refine(calls, pre, post, order):
    hop, n = OPT["hop"], len(calls)
    q, bk = [[c[k] for c in calls] for k in ("q", "banks")]

    stores = [i for i, c in enumerate(calls) if c["sem"] and not c["w"]]

    def costs(kh, kp, kg, ks, kl, start, row, byte):
        ns = [c["ns"] * (kp if c["q"] == "P" else kg if c["far"] else 1.0) + (ks if c["q"] == "S" else 0.0) for c in calls]
        lat = [start if c["lands"] else kl * c["lat"] for c in calls]
        wire = [16 * (row + byte * c["lands"]) if c["lands"] else 0.0 for c in calls]
        return [[(j, hop * kh if q[j] != "P" or q[i] != "P" else 0.0) for j in pre[i]] for i in range(n)], ns, lat, wire, hop * kh

    def timed(order, lo, old, gap, ns, lat, wire, hop):
        free, held, link = {}, [{} for _ in range(8)], None
        ends, done, why = old[1][:], old[2][:], old[3][:]
        for i in order[max(0, lo - 90):lo]:
            free[q[i]] = i
            link = i if wire[i] else link
            for b in bk[i]:
                held[b][q[i]] = i
        for i in order[lo:]:
            w = free.get(q[i])
            s = 0.0 if w is None else ends[w]
            for j, d in gap[i]:
                if done[j] + d > s:
                    s, w = done[j] + d, j
            for b in bk[i]:
                for q2, j in held[b].items():
                    if q2 != q[i] and ends[j] + hop > s:
                        s, w = ends[j] + hop, j
                held[b][q[i]] = i
            ends[i] = s = s + ns[i]
            s += lat[i]
            if wire[i]:
                if link is not None and done[link] > s:
                    s, w = done[link], link
                s, link = s + wire[i], i
            done[i], why[i], free[q[i]] = s, w, i
        return max((done[i], i) for i in stores), ends, done, why

    cases = [costs(*k) for k in OPT["cases"]]

    def longest(order, lo, old):
        got = [timed(order, lo, o, *m) for o, m in zip(old, cases)]
        return sum(x[0][0] for x in got) / len(got), got

    now = longest(order, 0, [(None, [0.0] * n, [0.0] * n, [None] * n)] * len(cases))
    best, pairs, steps = (now[0], order), None, OPT["steps"]
    for step, (u0, u1, u2, u3, u4) in enumerate(np.random.default_rng(0).random((steps, 5)).tolist()):
        if pairs is None:
            pairs = []
            for (_, i), _, _, why in now[1]:
                while why[i] is not None:
                    if why[i] not in pre[i] and q[i] != "Y":
                        pairs.append((why[i], i))
                    i = why[i]
            place = {x: k for k, x in enumerate(order)}
        a, b = pairs[int(u0 * len(pairs))]
        lo, hi = place[a], place[b]
        if u1 < 0.15:
            lo = max(0, lo - 1 - int(12 * u2))
        elif u1 < 0.3:
            hi = min(n - 1, hi + 1 + int(12 * u2))
        part = order[lo:hi + 1]
        if u3 < 0.5:
            move = {b}
            for x in reversed(part):
                if any(y in move for y in post[x]):
                    move.add(x)
            new = [x for x in part if x in move] + [x for x in part if x not in move]
        else:
            move = {a}
            for x in part:
                if any(y in move for y in pre[x]):
                    move.add(x)
            new = [x for x in part if x not in move] + [x for x in part if x in move]
        if a in move and b in move:
            continue
        tried = order[:lo] + new + order[hi + 1:]
        got = longest(tried, lo, now[1])
        if got[0] <= now[0] - math.log(u4 + 1e-12) * hop * OPT.get("heat", 0.4) * (1 - step / steps):
            order, now, pairs = tried, got, None
            if got[0] < best[0]:
                best = (got[0], tried)
    return best[1]


def plan(calls):
    hop, n = OPT["hop"], len(calls)
    wrote, read, group, loose = {}, {}, {}, {}
    pre, post = [], [[] for _ in calls]
    for i, c in enumerate(calls):
        p = set(meet(wrote, c["r"]) + meet(wrote, c["w"]) + meet(read, c["w"]))
        note(wrote, read, c["r"], c["w"], i)
        for b in c["starts"]:
            p.update(group.get(b, []))
            if c["open"][b]:
                p.update(loose.pop(b, []))
            loose.setdefault(b, []).append(i)
        for b in c["open"]:
            if c["open"][b] or b not in c["starts"]:
                group[b] = [i]
        p.discard(i)
        pre.append(sorted(p))
        for j in pre[i]:
            post[j].append(i)

    def lay(rank, before, after, back):
        busy, held, at, left = {}, {}, {}, [len(p) for p in before]
        ready = [i for i in range(n) if not left[i]]
        while ready:
            i = min(ready, key=lambda j: (rank[j], j))
            ready.remove(i)
            c = calls[i]
            q, d = c["q"], c["ns"]
            s = max([at[j][1] + (hop if calls[j]["q"] != "P" or q != "P" else 0.0) + calls[i if back else j]["lat"] for j in before[i]],
                    default=c["lat"] if back else 0.0)
            for a, b in sorted(busy.get(q, []) + [(a - hop, b + hop) for k in c["banks"] for a, b, q2 in held.get(k, []) if q2 != q]):
                if b > s and a < s + d:
                    s = b
            at[i] = (s, s + d, q)
            busy.setdefault(q, []).append((s, s + d))
            for k in c["banks"]:
                held.setdefault(k, []).append(at[i])
            for j in after[i]:
                left[j] -= 1
                if not left[j]:
                    ready.append(j)
        return at

    way = [0.0] * n
    for i in range(n - 1, -1, -1):
        way[i] = calls[i]["ns"] + calls[i]["lat"] + max([hop + way[j] for j in post[i]], default=0.0)
    pin = {i: i - 1e9 for i, c in enumerate(calls) if c["sem"] and c["w"]}
    rank, best = [pin.get(i, -x) for i, x in enumerate(way)], None
    for _ in range(OPT["passes"]):
        at = lay(rank, pre, post, False)
        end = max(at[i][1] + calls[i]["lat"] for i in range(n))
        if best is None or end < best[0]:
            best = (end, at)
        bk = lay([-(at[i][1] + calls[i]["lat"]) for i in range(n)], post, pre, True)
        rank = [pin.get(i, -bk[i][1]) for i in range(n)]
    at = best[1]
    return refine(calls, pre, post, sorted(range(n), key=lambda i: (at[i][0], i)))


def tracker(g, T):
    qq = {"V": g.vector, "S": g.scalar, "P": g.tensor, "G": g, "Y": g.sync}
    seen = {q: {} for q in qq}
    know = {}
    cnt = {q: 0 for q in QS}
    wrote, read, bank = {}, {}, {}

    def need(q, tok):
        s, n = tok
        if seen[q].get(s, 0) >= n:
            return
        qq[q].wait_ge(T.sem[s], n)
        for k, v in list(know.get(tok, {}).items()) + [(s, n)]:
            if seen[q].get(k, 0) < v:
                seen[q][k] = v

    def issue(c):
        q, r, w = c["q"], c["r"], ([] if c["lands"] else c["w"])
        toks = meet(wrote, r) + meet(read, w) + meet(wrote, [x for x in w if x not in c["goes_on"]])
        toks += [tok for b in c["banks"] for q2, tok in bank.get(b, {}).items() if q2 != q]
        top = {}
        for s, n in toks:
            top[s] = max(top.get(s, 0), n)
        for s in sorted(top, key=lambda s: s == QS.get(q)):
            need(q, (s, top[s]))
        ins = c["run"](qq[q])
        if c["lands"]:
            return
        if c["sem"]:
            tok = (c["sem"], 16)
            ins.then_inc(T.sem[c["sem"]], 16)
        else:
            cnt[q] += 1
            tok = (QS[q], cnt[q])
            ins.then_inc(T.sem[QS[q]], 1)
        know[tok] = dict(seen[q])
        note(wrote, read, r, w, tok)
        for b in c["banks"]:
            bank.setdefault(b, {})[q] = tok

    def lands(pieces, tok):
        note(wrote, read, [], pieces, tok)

    return issue, lands, need, cnt


def rank_program(g, core, T, topo):
    rank = T.rank_of(core)
    if rank is None:
        return
    issue, lands, need, cnt = tracker(g, T)
    calls = []
    nloc = [0]

    def v(name, lo=0, n=None, step=1, rows=128):
        n = T[name].shape[1] - lo if n is None else n
        return {"ap": T[name][0:min(rows, T[name].shape[0]), lo:lo + n:step], "at": [(name, lo, lo + n)], "n": (n + step - 1) // step, "by": [],
                "two": SCRATCH[name][2] in ("bfloat16", "float16", "uint16"), "ps": name == "ps"}

    def ps(b, lo, n, step=1, rows=128):
        return v("ps", 512 * b + lo, n, step, rows)

    def by(win, lst):
        return dict(win, ap=win["ap"].indirect(lst["ap"]), n=16 * lst["n"], by=lst["at"])

    def ap(x):
        return x["ap"] if isinstance(x, dict) else x

    def call(q, ns, run, out, ins, lat=0.0, sem=None, landing=False, starts=(), open_=(), goes_on=()):
        ins = [i for i in ins if isinstance(i, dict)]
        calls.append({"q": q, "ns": ns, "run": run, "w": [x for o in out for x in o["at"]], "lat": lat, "sem": sem, "lands": landing,
                      "r": [x for i in ins for x in i["at"] + i["by"]] + [x for o in out for x in o["by"]],
                      "starts": starts, "open": dict(open_), "goes_on": goes_on})
        calls[-1]["far"] = any(i["by"] for i in ins + out)
        calls[-1]["banks"] = banks(calls[-1]["r"] + calls[-1]["w"])

    def ns(out, a, per):
        if out["by"]:
            per = 3.8
        elif a["by"]:
            per = OPT["gat"]
        return OPT["fix"] + max(64, per * a["n"]) * OPT["cyc"]

    def half(out, a):
        return 0.5 if out["two"] and a["two"] else 1.0

    def tt(out, a, b, o):
        call("V", ns(out, a, 1 if a["ps"] or b["ps"] else 2), lambda e: e.tensor_tensor(out["ap"], a["ap"], b["ap"], o), [out], [a, b])

    def ts(out, a, s1, s2, *o):
        call("V", ns(out, a, half(out, a)), lambda e: e.tensor_scalar(out["ap"], a["ap"], ap(s1), ap(s2), *o), [out], [a, s1, s2])

    def cp(out, a):
        call("V", ns(out, a, half(out, a)), lambda e: e.tensor_copy(out["ap"], a["ap"]), [out], [a])

    def fill(out, x):
        call("V", ns(out, out, half(out, out)), lambda e: e.memset(out["ap"], x), [out], [])

    def act(out, a, f, bias=0.0, scale=1.0, more=0.0, after=None):
        call("S", more + OPT["sfix"] + ns(out, a, 1), lambda e: e.activation(out["ap"], a["ap"], f, bias=ap(bias), scale=ap(scale)), [out], [a, bias, scale, after])

    def sel(out, a, *rest):
        call("G", 170 + 2 * OPT["cyc"] * out["n"], lambda e: e.affine_select(out["ap"], a["ap"], *rest), [out], [a])

    def iota(out, pattern, mult, **kw):
        call("G", 150.0, lambda e: e.iota(out["ap"], pattern, 0, mult, **kw), [out], [])

    def mm(seq):
        def run(e):
            return [e.matmul(o["ap"], l["ap"], r["ap"], start, stop) for o, l, r, start, stop in seq][-1]
        started = [x for s in seq if s[3] for x in s[0]["at"]]
        call("P", sum(max(64, s[2]["n"]) for s in seq) * OPT["pe"], run, [s[0] for s in seq], [x for s in seq for x in s[1:3]], starts=banks(started),
             open_=[(b, not s[4]) for s in seq for b in banks(s[0]["at"])], goes_on=[x for s in seq for x in s[0]["at"] if x not in started])

    def acc(out, terms, start=True, stop=True):
        return [(out, l, r, start and i == 0, stop and i == len(terms) - 1) for i, (l, r) in enumerate(terms)]

    def load(q, name, src, sem, lat, after=(), lo=0, n=None):
        n = T[name].shape[1] if n is None else n
        call(q, 60.0, lambda e: e.dma_start(T[name][:, lo:lo + n], src[:, lo:lo + n]), [v(name, lo, n)], list(after), lat, sem)

    def store(q, dst, name, sem):
        call(q, 60.0, lambda e: e.dma_start(dst[:], T[name][:]), [], [v(name)], 2000.0, sem)

    def send(t, out, in_, sem):
        peer = T.cores[rank ^ (1 << t)]
        rid, pid = topo.addr(peer)[:2]
        ne = len(topo.engines(core, peer))
        lands(out["at"], (sem, ne))
        nloc[0] += ne
        call("G", 300.0, lambda e: e.remote_dma(out_ap=out["ap"], in_ap=in_["ap"], remote_sem=T.sem[sem], local_sem=T.sem["loc"], pid=pid, routing_id=rid,
                                                dma_engine_mask=topo.mask(core, peer)), [out], [in_], OPT["flight"] - 300.0 + 2.5 * in_["n"], landing=2 * in_["n"])

    M = {n: v("sc", 128 * i, 128) for i, (n, _, _) in enumerate(SCALED)}
    for n in ("idn", "bo", "m1", "m1s", "m3", "nb", "nb0", "cmd", "i16"):
        M[n] = v(n)

    def ek(name, k):
        return v(name, 15 - k, 128)

    load("Y", "ci", T.ctx, "lctx", 2000.0)
    load("S", "ri", T.pref, "lpref", 2500.0)
    load("S", "fi", T.fail0, "lfail", 2600.0)
    load("Y", "xs", T.x, "lx", OPT["lx"])
    load("Y", "hi", T.cand, "lcand", OPT["lx"] + 500)
    wide = 4096 // OPT["azp"]
    for j in range(OPT["azp"]):
        load("Y", "az", T.assoc, "las%d" % j, 1200.0 + 14000.0 / OPT["azp"], [v("xs") if j < 2 else v("az", wide * (j - 2), wide)], wide * j, wide)

    fill(v("ones"), 1.0)
    fill(v("e1"), 0.0)
    o128 = v("ones", 0, 128)
    sel(v("idn"), o128, [[-1, 128]], A.is_equal, 0.0, 0, 1)
    sel(v("bo0"), o128, [[-16, 8], [0, 16]], A.is_ge, 0.0, 0, 1)
    sel(v("bo"), v("bo0"), [[16, 8], [0, 16]], A.is_ge, 0.0, 15, -1)
    iota(v("pi"), [[1, 1]], 1)
    iota(v("rq"), [[256, 12]], 0, allow_small_or_imprecise_dtypes=True)
    sel(v("k8a"), v("ones", 0, 128, rows=8), [[1, 128]], A.is_ge, 0.0, 0, -16)
    sel(v("k8"), v("k8a"), [[-1, 128]], A.is_ge, 0.0, 15, 16)
    act(v("lv"), v("rq", 0, 4), F.Exp, 95.0 * LN2, 5.0 * LN2 / 256, 1300.0)
    for n, src, f in SCALED:
        ts(M[n], M[src], v("lv", f, 1) if n[:2] == "lv" else float(f), None, A.mult)
    cp(v("i16"), M["idn"])
    cp(v("e1", 15, 113, 16), v("bo", 0, 113, 16))
    tt(M["m1"], M["i2"], M["bo"], A.subtract)
    ts(M["nb"], M["bo"], -1.0, None, A.mult)
    ts(v("es"), v("e1"), 16.0, None, A.mult)
    cp(M["nb0"], M["nb"])
    fill(v("nb0", 0, 113, 16), 0.0)
    cp(v("rb"), v("ri"))
    cp(v("cu"), v("ci"))
    act(v("sa", 0, S), v("rb"), F.Exp, 90.0 * LN2, -5.0 * LN2, after=v("lv"))
    for b in range(4):
        mm([x for k in range(4 * b, 4 * b + 4) for x in acc(ps(4 + b, 128 * (k % 4), 128), [(M["idn"], ek("es", k)), (M["idn"], M["nb0"])])])
        act(v("ekm", 512 * b, 512), ps(4 + b, 0, 512), F.Copy)
    ts(v("ki"), v("pi"), 15, None, A.bitwise_and)
    cp(v("kc"), v("ki"))
    cp(v("e16"), v("e1"))
    tt(M["m3"], M["idn"], M["b41"], A.subtract)
    ts(M["m1s"], M["m1"], 2.0 ** -60, None, A.mult)
    ts(v("k16"), v("kc"), 16.0, None, A.mult)
    ts(v("bk"), v("kc"), -LNB, 84.5, A.mult, A.add)
    ts(v("cm"), v("kc"), 0.0, 8192.0, A.is_equal, A.mult)
    ts(v("cm"), v("cm"), -4096.0, None, A.add)
    ts(v("cs", 0, 12), v("rq"), v("k16"), None, A.add)
    ts(v("c16"), v("ci"), -2048.0, None, A.add)
    cp(v("hu"), v("hi"))
    ts(v("f3"), v("fi"), 3, None, A.bitwise_and)
    cp(v("fb"), v("f3"))
    cp(v("fa"), v("fi"))
    ts(v("h16"), v("hi"), -2048.0, None, A.add)

    def at(name, r, base=0):
        return v(name, base + r[0], r[1])

    def pat(b, base, r):
        return ps(b, base + r[0], r[1])

    def W(name, t, r):
        return at(name, r, 2 * S * t)

    def AM(name, t, r):
        return at(name, r, 2 * S * t + S)

    X0, ND = W, AM

    def one(r):
        return v("ones", 0, r[1])

    def big(name, r, first=0, step=1, base=0):
        return v(name, base + 16 * r[0] + first, 16 * r[1] - first, step)

    def parts(kind, r):
        R = 8 if OPT[kind] and r[1] <= 64 else 4
        return 16 // R, R

    def part(name, r, a, R, j=0, step=1):
        return v(name, 16 * r[0] + R * r[1] * a + j, R * r[1] - j, step)

    def dup(b, r, R, src):
        return [(ps(b, j, R * r[1] - j, R), M["idn"], src, True, True) for j in range(R)]

    def lst(name, t, r):
        return v(name, 16 * t + r[0] // 16, r[1] // 16)

    def gather(t, name, by_, base=0):
        n = OPT["piece"][name == "yg"]
        for lo in range(0, S, n):
            out, src = v(name, base + 16 * lo, 16 * n), by(v("xs"), v(by_, lo, n))
            if lo // n in OPT[name][t]:
                cp(out, src)
            else:
                act(out, src, F.Copy)

    def weights(t, r):
        out = pat(5, S, r)
        mm(acc(out, [(M["idn"], W("sa", t - 1, r)), (M["lv%d" % (2 * t - 1)], at("sp", r, S * (t - 1))), (M["lv%d" % (2 * t - 2)], at("rp", r, S * (t - 1)))]))
        act(W("sa", t, r), out, F.Copy)

    def counts(t):
        out = ps(4, S, S)
        mm(acc(out, [(v("k8"), v("fb"))] + [(M["bo"], v("rp", S * s, S)) for s in range(t)]))
        act(AM("sa", t, ALL), out, F.Copy)
        send(t, v("ra", 2 * S * t, 2 * S), v("sa", 2 * S * t, 2 * S), "wax%d" % t)

    def describe(t, c, r):
        w = r[1]
        P, R = parts("hd", r)
        mm(dup(0, r, R, big("xg", r, 0, 16)))
        mm(dup(1, r, R, W("sa", t, r)))
        for a in range(P):
            tt(part("z", r, a, R), big("xg", r, a, P), ps(0, 0, R * w), A.not_equal)
        for a in range(P):
            tt(part("z", r, a, R), part("z", r, a, R), ps(1, 0, R * w), A.mult)
            mm([(ps(2 + a % 2, 0, R * w), M["m1"], part("z", r, a, R), True, True)])
            act(part("yr", r, a, R), ps(2 + a % 2, 0, R * w), F.Relu)
            mm(acc(pat(4, 0, r), [(M["idn"], part("yr", r, a, R, j, R)) for j in range(1 if a == 0 else 0, R)], a == 0, a == P - 1))

    def tell(t, r):
        act(ND("sn", t, r), pat(4, 0, r), F.Relu, 1.0, -1.0)
        send(t, ND("rn", t, r), ND("sn", t, r), "nd%d%d" % (t, r[0] // 32))

    def tops(r):
        P, R = parts("hd", r)
        for a in range(P):
            terms = [(v("ekm", 128 * (a + P * j), 128), part("z", r, a, R, j, R)) for j in range(1 if a == 0 else 0, R)]
            mm(acc(pat(5, 0, r), terms, a == 0, a == P - 1))

    def keep(t, name, src, r, bias):
        act(src, src, F.Sign, bias)
        act(at(name, r), src, F.Copy, 0.0 if t < RO - 1 else -2048.0, 2048.0)

    def star(t, r):
        return by(v("yg", BIGW * (t % 2), BIGW), lst("lk", t, r)) if t < RO - 1 else by(v("xs"), lst("ln", t, r))

    def resolve(t, c, r):
        w, lo, n, nd = r[1], 2 * r[0], r[1] // 16, ND("rn", t, r)
        base = (3 * OPT["res"][0][1] + 16) * (c // 2)
        miss, gap, ow, lp = [ps(6 + c % 2, base + w * i, w if i < 3 else 2 * n) for i in range(4)]
        P, R = parts("hr", r)
        xm = [ps(c % 2, j, R * w - j, R) for j in range(R)]
        mm([(xm[j], M["idn"], X0("rn", t, r), j == 0, False) for j in range(R)])
        mm([(xm[j], M["i1024"], nd, False, j == R - 1) for j in range(R)])
        for a in range(P):
            tt(part("nq", r, a, R), big("yg", r, a, P, BIGW * (t % 2)), ps(c % 2, 0, R * w), A.not_equal)
            terms = [(M["nb"], nd)] if a == 0 else []
            terms += [(ek("e1", a + P * j), part("nq", r, a, R, j, R)) for j in range(R)]
            mm(acc(miss, terms, a == 0, a == P - 1))
        act(at("wk", r), miss, F.Exp, v("bk"), -16.0 * LNB)
        mm([(gap, M["m3"], at("wk", r), True, True)])
        ts(ow, gap, 0.0, None, A.is_gt)
        if t < RO - 1:
            ts(v("pr", lo + w, w), gap, 0.0, v("kc"), A.is_gt, A.mult)
        tt(v("pr", lo, w), at("h16", r), ow, A.mult)
        lpn, lpk = ps(6 + c % 2, base + 3 * w, n), ps(6 + c % 2, base + 3 * w + n, n)
        if t < RO - 1:
            mm(acc(lp, [(ek("e16", j), v("pr", lo + j, 2 * w - j, 16)) for j in range(16)], True, False) + [(lpk, M["i16"], lst("cs", 0, r), False, True)])
        else:
            mm(acc(lpn, [(ek("e16", j), v("pr", lo + j, w - j, 16)) for j in range(16)]))
        ts(lst("ln", t, r), lpn, 2048.0, None, A.add)
        send(t, lst("rl", t, r), lst("ln", t, r), "lst%d%d" % (t, r[0] // 32))
        if t < RO - 1:
            cp(lst("lk", t, r), lpk)
        keep(t, "bh", miss, r, -0.5)

    def told(t, r):
        de = pat(3, S, r)
        mm(acc(de, [(M["idn"], one(r)), (M["neg"], ND("rn", t, r))]))
        tt(at("nx", r), X0("rn", t, r), de, A.mult)

    def rewrite(t, r):
        tt(at("na", r), star(t, r), ND("rn", t, r), A.mult)
        tt(by(v("xs", 0, BIGW), lst("lk", t, r)), at("na", r), at("nx", r), A.add)

    def judge(t, c, r):
        wh, room, yf = pat(2, S, r), ps(2 + c % 2, 384, r[1]), ps(c % 2, 0, r[1])
        mm([(wh, M["idn"], W("ra", t, r), True, True)])
        tt(at("un", r), star(t, r), X0("rn", t, r), A.not_equal)
        mm(acc(room, [(M["idn"], AM("ra", t, r))] + ([(M["i2"], at("q", r))] if t else []) + [(M["nb"], at("un", r))]))
        act(at("nf", r), room, F.Relu, (3.5 if t else 5.5) * 2.0 ** 60, 2.0 ** 60)
        tt(at("zf", r), at("un", r), wh, A.mult)
        mm([(yf, M["m1s"], at("zf", r), True, True)])
        tt(at("sp", r, S * t), yf, at("nf", r), A.is_gt)
        send(t, at("rp", r, S * t), at("sp", r, S * t), "phi%d%d" % (t, r[0] // 32))

    def refill(w, t, r, where):
        st, b, tm, ls = (("c16", "bc", "tc", "rl"), ("h16", "bh", "th", "ln"))[w]
        out = ps(where[0], where[1], r[1])
        mm(acc(out, [(M["i16"], at(st, r)), (M["idn"], at(b, r)), (M["i2048" if t < RO - 1 else "i6144"], one(r))]))
        if t == RO - 1:
            st = tm = ("cf", "hf")[w]
        tt(at(tm, r), by(v("az"), lst(ls, t, r)), at(b, r), A.subtract)
        tt(at(st, r), at(tm, r), out, A.min)
        if t < RO - 1:
            ts(at(("cu", "hu")[w], r), at(st, r), 2048.0, None, A.add)

    def moves(t):
        r, rf = ps(2, 0, S), ps(3, 0, S)
        if not OPT["mp"]:
            mm([(r, M["idn"], v("rb"), True, True)])
        for phi, src, dst in ((v("rp", S * t, S), v("rb"), v("rb1")), (v("sp", S * t, S), v("rb1"), v("rb"))):
            if OPT["mp"]:
                mm(acc(r, [(M["neg"], src), (M["n16"], phi)]))
                act(v("p1"), r, F.Relu, -16.0, -1.0)
            else:
                tt(v("p1"), phi, r, A.mult)
            if OPT["mt"]:
                mm(acc(rf, [(M["idn"], src), (M["nb"], v("p1"))]))
                act(v("t1"), rf, F.Sign, 0.5)
                mm(acc(r, [(M["idn"], src), (M["n32"], phi), (M["nhalf"], v("t1"))]))
                act(dst, r, F.Relu, 0.5)
            else:
                mm([(rf, M["bo"], v("p1"), True, True)])
                tt(v("t1"), rf, src, A.is_gt)
                mm(acc(r, [(M["idn"], src), (M["n32"], phi), (M["idn"], v("t1"))]))
                act(dst, r, F.Relu)

    def last_moves(x):
        t = RO - 1
        sp, rp, p1, t1, rb, m = at("sp", x, S * t), at("rp", x, S * t), at("p1", x), at("t1", x), at("rb", x), at("rb1", x)
        r, rf, cap, ahead, dd = pat(0, 256, x), pat(3, 0, x), pat(4, 0, x), pat(3, S, x), pat(4, S, x)
        mm([(r, M["idn"], rb, True, True)])
        tt(p1, sp, r, A.mult)
        mm([(rf, M["bo"], p1, True, True)])
        tt(t1, rf, rb, A.is_gt)
        mm(acc(r, [(M["idn"], rb), (M["n32"], sp), (M["idn"], t1)]))
        act(m, r, F.Relu)
        mm(acc(cap, [(M["bo"], sp), (M["neg"], sp), (M["i32"], one(x)), (M["n32"], rp)]))
        r0, p2, t2 = pat(1, 256, x), at("na", x), at("nx", x)
        mm(acc(r0, [(M["idn"], rb), (M["n32"], sp)]))
        tt(p2, rp, r0, A.mult)
        mm(acc(ahead, [(M["neg"], rb), (M["n16"], sp), (M["bo"], p2)]))
        tt(dd, m, cap, A.min)
        ts(t2, ahead, 0.0, None, A.is_gt)
        tt(at("rf", x), t2, dd, A.add)

    for t in range(RO):
        gather(t, "xg", "cu")
        gather(t, "yg", "hu", BIGW * (t % 2))
        if t > 0:
            for r in OPT["jud"]:
                weights(t, r)
        sel(X0("sn", t, ALL), v("xg", 0, BIGW, 16), [[0, S]], A.is_ge, 0.0, 0, 0)
        send(t, X0("rn", t, ALL), X0("sn", t, ALL), "tar%d" % t)
        if t == 0:
            counts(t)
        for c, r in enumerate(OPT["des"]):
            describe(t, c, r)
            for x in OPT["res"]:
                if x[0] + x[1] == r[0] + r[1]:
                    tell(t, x)
        if t > 0:
            counts(t)
        for r in OPT["des"]:
            tops(r)
        for r in OPT["kcr"]:
            keep(t, "bc", pat(5, 0, r), r, v("cm"))
        if t > 0:
            act(v("q"), AM("ra", t, ALL), F.Sign, 3.5, -1.0)
            moves(t - 1)
        for c, r in enumerate(OPT["res"]):
            resolve(t, c, r)
        if t < RO - 1:
            for r in OPT["tol"]:
                told(t, r)
            for r in OPT["rew"]:
                rewrite(t, r)
        for c, r in enumerate(OPT["jud"]):
            judge(t, c, r)
        for r, where in OPT["cre"]:
            refill(0, t, r, where)
        for r, where in OPT["hre"]:
            refill(1, t, r, where)
    for r in OPT["las"]:
        last_moves(r)
    mm(acc(ps(2, 0, S, rows=8), [(v("idn", 0, 8, rows=8), v("fa"))] + [(v("bo", 0, 113, 16), v("rp", S * s, S)) for s in range(RO)]))
    act(v("fo"), ps(2, 0, S, rows=8), F.Copy)
    store("Y", T.ycand, "hf", "o1")
    store("Y", T.yctx, "cf", "o0")
    store("Y", T.ypref, "rf", "o2")
    store("S", T.yfail, "fo", "o3")

    if not ORDER:
        ORDER.extend(plan(calls))
    for i in ORDER:
        issue(calls[i])
    for s in ("o0", "o1", "o2", "o3"):
        g.sync.wait_ge(T.sem[s], 16)
    for q in ("V", "S", "P", "G"):
        need("G", (QS[q], cnt[q]))
    g.wait_ge(T.sem["loc"], nloc[0])
